import numpy as np
import ml_dtypes


def mxq(x, axis, fmt="e4m3"):
    dtype, down = {"e4m3": (ml_dtypes.float8_e4m3fn, 7), "e5m2": (ml_dtypes.float8_e5m2, 14)}[fmt]
    v = np.moveaxis(np.asarray(x, np.float32).astype(ml_dtypes.bfloat16).astype(np.float64), axis, -1)
    blocks = v.reshape(v.shape[:-1] + (-1, 32))
    amax = np.abs(blocks).max(-1, keepdims=True)
    byte = np.maximum(np.where(amax > 0, np.frexp(amax)[1] - 1 + 127, 0) - down, 1)
    scale = np.exp2(byte - 127.0)
    codes = (blocks / scale).astype(np.float32).astype(dtype).astype(np.float64)
    return np.moveaxis((codes * scale).reshape(v.shape), -1, axis)


WIDE = False


def mx_kscale(k):
    if not WIDE:
        return np.ones(k)
    levels = np.array([10, -10, 5, -5, 0])
    if k % 512:
        return np.exp2(np.random.permutation(np.resize(levels, k // 32))).repeat(32)
    a = np.empty((k // 512, 16))
    for p in range(k // 512):
        a[p, :8] = np.random.permutation(np.resize(levels, 8))
        for g in range(8):
            far = levels[np.abs(levels - a[p, g]) >= 10]
            a[p, g + 8] = far[np.random.randint(len(far))]
    return np.exp2(a.ravel()).repeat(32)


BF16 = ml_dtypes.bfloat16


def bf(x):
    return np.asarray(x, np.float32).astype(BF16)


def f64(x):
    return np.asarray(x).astype(np.float64)


E2M1 = np.array([0.0, 0.5, 1.0, 1.5, 2.0, 3.0, 4.0, 6.0, -0.0, -0.5, -1.0, -1.5, -2.0, -3.0, -4.0, -6.0])


def pack_weight(w, fmt):
    k, n = w.shape
    w = f64(bf(w)).reshape(k // 32, 32, n)
    amax = np.abs(w).max(1)
    if fmt == "e4m3":
        byte = np.frexp(amax)[1] - 1 + 127 - 7
    else:
        mant, ex = np.frexp(amax / 6.0)
        byte = np.where(mant > 0.5, ex, ex - 1) + 127
    byte = np.clip(np.where(amax > 0, byte, 1), 1, 254)
    scaled = (w * np.exp2(127.0 - byte)[:, None, :]).reshape(k, n).astype(np.float32)
    by_word = np.ascontiguousarray(scaled.reshape(k // 512, 128, 4, n).transpose(0, 1, 3, 2))
    if fmt == "e4m3":
        words = by_word.astype(ml_dtypes.float8_e4m3fn).view(np.uint8)
    else:
        c = by_word.astype(ml_dtypes.float4_e2m1fn).view(np.uint8) & 0xF
        words = c[..., 0::2] | (c[..., 1::2] << 4)
    return np.ascontiguousarray(words), np.ascontiguousarray(byte.astype(np.uint8).reshape(k // 512, 16, n))


def unpack_weight(words, scales, fmt):
    g, p, n, _ = words.shape
    if fmt == "e4m3":
        vals = np.ascontiguousarray(words).view(ml_dtypes.float8_e4m3fn).astype(np.float64)
    else:
        nib = np.empty((g, p, n, 4), np.uint8)
        nib[..., 0::2] = words & 0xF
        nib[..., 1::2] = words >> 4
        vals = E2M1[nib]
    vals = vals * np.repeat(np.exp2(scales.astype(np.float64) - 127.0), 8, axis=1)[..., None]
    return vals.transpose(0, 1, 3, 2).reshape(g * 512, n)
def pack4(w):
    words, scales = pack_weight(w, "e2m1")
    return words.reshape(words.shape[0], 128, -1), scales


def unpack4(words, scales):
    return unpack_weight(words.reshape(words.shape[0], 128, -1, 2), scales, "e2m1")


B, KO, KR, F, J = 1024, 512, 2048, 1024, 1024

OUTLIER = 4.0
SPREAD = 0.45


def draw0():
    u, s, t = mx_kscale(KO), mx_kscale(KR), mx_kscale(F)
    base = SPREAD * np.random.standard_normal((KR, F)) / np.sqrt(KR)
    proj = np.random.standard_normal((F, J)) / np.sqrt(F)
    base_words, base_scales = pack4(base / s[:, None])
    proj_words, proj_scales = pack4(proj / t[:, None])
    online = 0.1 + np.random.exponential(size=(B, J))
    return {"x_out": bf(OUTLIER * np.random.standard_normal((B, KO)) * u),
            "w_out": bf(SPREAD / OUTLIER * np.random.standard_normal((KO, F)) / np.sqrt(KO) / u[:, None]),
            "x_rest": bf(np.random.standard_normal((B, KR)) * s),
            "base_words": base_words,
            "base_scales": base_scales,
            "spacing": bf((1 + 0.1 * np.random.standard_normal(F)) * t),
            "proj_words": proj_words,
            "proj_scales": proj_scales,
            "online": bf(online / online.sum(axis=1, keepdims=True))}


def core(x_out, w_out, x_rest, base_words, base_scales, spacing, proj_words, proj_scales, online):
    z = ((mxq(f64(x_out), 1, "e4m3") @ mxq(f64(w_out), 0, "e4m3"))
         + (mxq(f64(x_rest), 1, "e4m3") @ unpack4(base_words, base_scales)))
    mass = np.exp(z) * f64(spacing)
    target = mxq(mass, 1, "e4m3") @ unpack4(proj_words, proj_scales)
    loss = -np.mean(target * np.log(f64(online)), axis=1)
    return target, loss


def e4m3fn_bytes(y):
    return np.clip(np.asarray(y, np.float64), -448.0, 448.0).astype(np.float32).astype(ml_dtypes.float8_e4m3fn).view(np.uint8)


def e4m3fn_values(b):
    return np.asarray(b, np.uint8).view(ml_dtypes.float8_e4m3fn).astype(np.float64)


def setup_inputs():
    d = draw0()
    x0 = np.asarray(d['x_rest']).astype(np.float64)
    s = (np.max(np.abs(x0), axis=(0,), keepdims=True) / 448.0).astype(np.float32)
    out = {}
    for k, v in d.items():
        if k == 'x_rest':
            out['x_rest_bytes'] = e4m3fn_bytes(x0 / s.astype(np.float64))
            out['x_rest_scale'] = s
        else:
            out[k] = v
    return out


def reference(x_out, w_out, x_rest_bytes, x_rest_scale, base_words, base_scales, spacing, proj_words, proj_scales, online):
    return core(x_out, w_out, e4m3fn_values(x_rest_bytes) * x_rest_scale.astype(np.float64), base_words, base_scales, spacing, proj_words, proj_scales, online)

@@ -1,0 +1,527 @@
+from contextlib import ExitStack
+
+import concourse.mybir as mybir
+from concourse.masks import make_identity
+
+B, KO, KR, F, J = 1024, 512, 2048, 1024, 1024
+FLOPS = 2 * B * F * (KO + KR) + 2 * B * J * F
+
+F32 = mybir.dt.float32
+BF16 = mybir.dt.bfloat16
+I32 = mybir.dt.int32
+U32 = mybir.dt.uint32
+U8 = mybir.dt.uint8
+FP8 = mybir.dt.float8_e4m3fn
+FP8X4 = mybir.dt.float8_e4m3fn_x4
+FP4X4 = mybir.dt.float4_e2m1fn_x4
+ACT = mybir.ActivationFunctionType
+ALU = mybir.AluOpType
+
+P = 128
+NT = B // P
+HALF = 512
+GR = KR // 512
+GM = F // 512
+
+
+def tile_c51_shifted_log_loss_s3_kernel(
+    tc, x_out, w_out, x_rest_bytes, x_rest_scale, base_words, base_scales, spacing, proj_words, proj_scales, online, target, loss
+):
+    nc = tc.nc
+    with ExitStack() as ctx:
+        keep = ctx.enter_context(tc.tile_pool(name="keep", bufs=1))
+        work = ctx.enter_context(tc.tile_pool(name="work", bufs=3))
+        psum = ctx.enter_context(tc.psum_pool(name="psum", bufs=4))
+
+        def kept(shape, dtype, name):
+            return keep.tile(shape, dtype, name=name, tag=name, align_bytes=64)
+
+        xr = [kept([P, KR], U8, "xr%d" % i) for i in range(NT)]
+        sc = kept([P, GR, 2, 2], F32, "sc")
+        base = kept([P, GR, 2 * F], U8, "base")
+        scb = kept([P, KR], F32, "scb")
+        bsc = kept([P, GR, F], U8, "bsc")
+        proj = kept([P, GM, 2 * J], U8, "proj")
+        psc = kept([P, GM, J], U8, "psc")
+        wraw = kept([P, 4, F], BF16, "wraw")
+        wgrp = [kept([P, HALF, 4], BF16, "wgrp%d" % h) for h in range(2)]
+        wcod = [kept([P, HALF], U32, "wcod%d" % h) for h in range(2)]
+        wscl = [kept([P, HALF], U8, "wscl%d" % h) for h in range(2)]
+        xo = [kept([P, 2, KO], BF16, "xo%d" % i) for i in range(NT // 2)]
+        onl = [kept([P, 2, J], BF16, "onl%d" % i) for i in range(NT // 2)]
+        logs = kept([P, NT, J], F32, "logs")
+        spc = kept([P, F], BF16, "spc")
+        ident = kept([P, P], F32, "ident")
+        acc = [kept([P, NT], F32, "acc%d" % h) for h in range(2)]
+        lpad = kept([P, P], F32, "lpad")
+        lrow = kept([32, P], F32, "lrow")
+        one = kept([P, 1], F32, "one")
+        junk1 = kept([P, 1], F32, "junk1")
+        xcod = [kept([P, GR, P], U32, "xcod%d" % i) for i in range(NT)]
+        xscl = [kept([P, GR, P], U8, "xscl%d" % i) for i in range(NT)]
+        ocod = [kept([P, 2, P], U32, "ocod%d" % i) for i in range(NT // 2)]
+        oscl = [kept([P, 2, P], U8, "oscl%d" % i) for i in range(NT // 2)]
+
+        with tc.manual_schedule():
+            nc.vector.memset(one[:], 1.0)
+            nc.vector.memset(bsc[:].rearrange("p g n -> p (g n)").bitcast(I32), 0)
+            nc.vector.memset(psc[:].rearrange("p g n -> p (g n)").bitcast(I32), 0)
+            nc.vector.memset(lpad[:], 0.0)
+            nc.scalar.activation(out=junk1[:], in_=one[:], func=ACT.Ln)
+            make_identity(nc, ident[:])
+
+            def load_x(i):
+                if i == 0:
+                    nc.sync.dma_start(out=xr[i][:, 0:1024], in_=x_rest_bytes[0:P, 0:1024])
+                    nc.sync.dma_start(out=xr[i][:, 1024:2048], in_=x_rest_bytes[0:P, 1024:2048])
+                    return
+                nc.sync.dma_start(out=xr[i][:], in_=x_rest_bytes[P * i : P * (i + 1), :])
+
+            def load_onl(a):
+                nc.sync.dma_start(out=onl[a][:], in_=online[2 * P * a : 2 * P * (a + 1), :].rearrange("(i r) j -> r i j", r=P))
+
+            def load_xo(a):
+                nc.sync.dma_start(out=xo[a][:], in_=x_out[2 * P * a : 2 * P * (a + 1), :].rearrange("(i r) k -> r i k", r=P))
+
+            load_x(0)
+            load_x(1)
+            load_xo(0)
+            nc.sync.dma_start(out=sc[:].rearrange("p g u e -> p g (u e)"), in_=x_rest_scale.rearrange("o (g p t) -> p (o g) t", p=P, t=4))
+            nc.sync.dma_start(out=wraw[:], in_=w_out.rearrange("(p j) n -> p j n", j=4))
+            load_x(2)
+            load_onl(0)
+            load_xo(1)
+            nc.sync.dma_start(out=base[:], in_=base_words.rearrange("g p n -> p g n"))
+            for q in range(4):
+                nc.sync.dma_start(
+                    out=bsc[32 * q : 32 * q + 4].bitcast(I32),
+                    in_=base_scales[:, 4 * q : 4 * q + 4, :].rearrange("g r n -> r g n").bitcast(I32),
+                )
+            load_onl(1)
+            load_x(3)
+            load_onl(2)
+            nc.sync.dma_start(out=scb[:], in_=x_rest_scale.rearrange("o k -> (o k)").partition_broadcast(P))
+            load_x(4)
+            load_x(7)
+            load_xo(2)
+            load_x(6)
+            load_xo(3)
+            load_onl(3)
+            load_x(5)
+            nc.sync.dma_start(out=spc[:], in_=spacing.partition_broadcast(P))
+            nc.sync.dma_start(out=proj[:], in_=proj_words.rearrange("g p n -> p g n"))
+            for q in range(4):
+                nc.sync.dma_start(
+                    out=psc[32 * q : 32 * q + 4].bitcast(I32),
+                    in_=proj_scales[:, 4 * q : 4 * q + 4, :].rearrange("g r n -> r g n").bitcast(I32),
+                )
+
+            wide = {}
+            xt = {}
+            grp = {}
+            z = {}
+            ex = {}
+            mass = {}
+            mt = {}
+            mgrp = {}
+            mcod = {}
+            mscl = {}
+            tg = {}
+            tout = {}
+
+            def cast(i):
+                if i in (3, 4, 5, 6, 7,):
+                    t = work.tile([P, KR], BF16, name="wide", tag="wide", bufs=4)
+                    wide[i] = t
+                    nc.vector.tensor_tensor(out=t[:], in0=xr[i][:].bitcast(FP8), in1=scb[:], op=ALU.mult)
+                    return
+                t = work.tile([P, KR], BF16, name="wide", tag="wide", bufs=4)
+                wide[i] = t
+                if i == 0:
+                    for c in (0, 1024):
+                        nc.scalar.copy(out=t[:, c : c + 512], in_=xr[i][:, c : c + 512].bitcast(FP8))
+                        nc.vector.tensor_copy(out=t[:, c + 512 : c + 1024], in_=xr[i][:, c + 512 : c + 1024].bitcast(FP8))
+                elif i == 1:
+                    nc.scalar.copy(out=t[:, 0:1024], in_=xr[i][:, 0:1024].bitcast(FP8))
+                    nc.vector.tensor_copy(out=t[:, 1024:2048], in_=xr[i][:, 1024:2048].bitcast(FP8))
+                else:
+                    nc.scalar.copy(out=t[:], in_=xr[i][:].bitcast(FP8))
+
+            def xtrans(i, b):
+                t = psum.tile([P, 2, 2, P], F32, name="xt", tag="xt", bufs=4)
+                xt[i, b] = t
+                words = wide[i][:].bitcast(F32)
+                for gg in range(2):
+                    g = 2 * b + gg
+                    for u in range(2):
+                        nc.tensor.transpose(t[:, u, gg, :], words[:, 256 * g + u : 256 * (g + 1) : 2], ident[:])
+
+            def prod(i, b):
+                if i not in grp:
+                    grp[i] = work.tile([P, GR, P, 2, 2], BF16, name="grp", tag="grp", bufs=4, align_bytes=64)
+                if i in (3, 4, 5, 6, 7,):
+                    nc.scalar.copy(
+                        out=grp[i][:, 2 * b : 2 * b + 2].rearrange("p g r u e -> p (g r u e)").bitcast(F32).rearrange("p (g r u) -> p g r u", g=2, u=2),
+                        in_=xt[i, b][:].rearrange("p u g r -> p g r u"),
+                    )
+                    return
+                t = xt[i, b][:].rearrange("p u g r -> p (u g r)").bitcast(BF16).rearrange("p (u g r e) -> p g r u e", u=2, g=2, e=2)
+                s = sc[:, 2 * b : 2 * b + 2].unsqueeze(2).to_broadcast([P, 2, P, 2, 2])
+                nc.vector.tensor_tensor(out=grp[i][:, 2 * b : 2 * b + 2], in0=t, in1=s, op=ALU.mult)
+
+            def xquant(i):
+                nc.vector.quantize_mx(
+                    out=xcod[i][:].rearrange("p g r -> p (g r)").bitcast(FP8X4),
+                    scales=xscl[i][:].rearrange("p g r -> p (g r)"),
+                    in_=grp[i][:].rearrange("p g r u e -> p (g r u e)"),
+                )
+
+            def otrans(a):
+                t = psum.tile([P, 2, 2, P], F32, name="xt", tag="xt", bufs=4)
+                xt["o", a] = t
+                for i in range(2):
+                    words = xo[a][:, i, :].bitcast(F32)
+                    for u in range(2):
+                        nc.tensor.transpose(t[:, u, i, :], words[:, u::2], ident[:])
+
+            def oexit(a):
+                grp["o", a] = work.tile([P, 2 * P * 4], BF16, name="ogrp", tag="ogrp", bufs=2, align_bytes=64)
+                nc.scalar.copy(
+                    out=grp["o", a][:].bitcast(F32).rearrange("p (i r u) -> p i r u", i=2, u=2),
+                    in_=xt["o", a][:].rearrange("p u i r -> p i r u"),
+                )
+
+            def oquant(a):
+                nc.vector.quantize_mx(
+                    out=ocod[a][:].rearrange("p i r -> p (i r)").bitcast(FP8X4),
+                    scales=oscl[a][:].rearrange("p i r -> p (i r)"),
+                    in_=grp["o", a][:],
+                )
+
+            def wgroup(h):
+                for c in range(0, HALF, P):
+                    nc.gpsimd.tensor_scalar(
+                        out=wgrp[h][:, c : c + P],
+                        in0=wraw[:, :, HALF * h + c : HALF * h + c + P].rearrange("p j n -> p n j"),
+                        scalar1=1.0,
+                        scalar2=0.0,
+                        op0=ALU.mult,
+                        op1=ALU.add,
+                    )
+
+            def wquant(h):
+                nc.vector.quantize_mx(out=wcod[h][:].bitcast(FP8X4), scales=wscl[h][:], in_=wgrp[h][:].rearrange("p n j -> p (n j)"))
+
+            def zrest(i, h):
+                t = psum.tile([P, HALF], F32, name="mm", tag="mm", bufs=4)
+                z[i, h] = t
+                for g in range(GR):
+                    nc.tensor.matmul_mx(
+                        out=t[:],
+                        lhsT=xcod[i][:, g, :].bitcast(FP8X4),
+                        lhsT_scale=xscl[i][:, g, :],
+                        rhs=base[:, g, 2 * HALF * h : 2 * HALF * (h + 1)].bitcast(FP4X4),
+                        rhs_scale=bsc[:, g, HALF * h : HALF * (h + 1)],
+                        start=(g == 0),
+                        stop=False,
+                    )
+
+            def zout(i, h):
+                a, j = i // 2, i % 2
+                nc.tensor.matmul_mx(
+                    out=z[i, h][:],
+                    lhsT=ocod[a][:, j, :].bitcast(FP8X4),
+                    lhsT_scale=oscl[a][:, j, :],
+                    rhs=wcod[h][:].bitcast(FP8X4),
+                    rhs_scale=wscl[h][:],
+                    start=False,
+                    stop=True,
+                )
+
+            def exp(i, h):
+                if i not in ex:
+                    ex[i] = work.tile([P, F], F32, name="ex", tag="ex", bufs=3)
+                nc.scalar.activation(out=ex[i][:, HALF * h : HALF * (h + 1)], in_=z[i, h][:], func=ACT.Exp)
+
+            def mul(i, h):
+                if i not in mass:
+                    mass[i] = work.tile([P, GM, 2, P, 2], BF16, name="mass", tag="mass", bufs=3)
+                eng = nc.vector
+                cols = slice(HALF * h, HALF * (h + 1))
+                eng.tensor_tensor(
+                    out=mass[i][:, h],
+                    in0=ex[i][:, cols].rearrange("b (p u e) -> b u p e", u=2, e=2),
+                    in1=spc[:, cols].rearrange("b (p u e) -> b u p e", u=2, e=2),
+                    op=ALU.mult,
+                )
+
+            def mtrans(i):
+                t = psum.tile([P, 2, 2, P], F32, name="xt", tag="xt", bufs=4)
+                mt[i] = t
+                for g in range(GM):
+                    for u in range(2):
+                        nc.tensor.transpose(t[:, u, g, :], mass[i][:, g, u].rearrange("b p e -> b (p e)").bitcast(F32), ident[:])
+
+            def mexit(i):
+                mgrp[i] = work.tile([P, GM * P * 4], BF16, name="mgrp", tag="mgrp", bufs=2, align_bytes=64)
+                nc.scalar.copy(
+                    out=mgrp[i][:].bitcast(F32).rearrange("p (g b u) -> p g b u", g=GM, u=2),
+                    in_=mt[i][:].rearrange("p u g b -> p g b u"),
+                )
+
+            def mquant(i):
+                mcod[i] = work.tile([P, GM, P], U32, name="mcod", tag="mcod", bufs=3, align_bytes=64)
+                mscl[i] = work.tile([P, GM, P], U8, name="mscl", tag="mscl", bufs=3, align_bytes=64)
+                nc.vector.quantize_mx(
+                    out=mcod[i][:].rearrange("p g b -> p (g b)").bitcast(FP8X4),
+                    scales=mscl[i][:].rearrange("p g b -> p (g b)"),
+                    in_=mgrp[i][:],
+                )
+
+            def tmat(i, h):
+                t = psum.tile([P, HALF], F32, name="mm", tag="mm", bufs=4)
+                tg[i, h] = t
+                for g in range(GM):
+                    nc.tensor.matmul_mx(
+                        out=t[:],
+                        lhsT=mcod[i][:, g, :].bitcast(FP8X4),
+                        lhsT_scale=mscl[i][:, g, :],
+                        rhs=proj[:, g, 2 * HALF * h : 2 * HALF * (h + 1)].bitcast(FP4X4),
+                        rhs_scale=psc[:, g, HALF * h : HALF * (h + 1)],
+                        start=(g == 0),
+                        stop=(g == GM - 1),
+                    )
+
+            def tcopy(i, h):
+                half = work.tile([P, HALF], F32, name="tout", tag="tout", bufs=8)
+                nc.scalar.copy(out=half[:], in_=tg[i, h][:])
+                nc.sync.dma_start(out=target[P * i : P * (i + 1), HALF * h : HALF * (h + 1)], in_=half[:])
+
+            def lossp(i, h):
+                prods = work.tile([P, HALF], F32, name="prods", tag="prods", bufs=2)
+                nc.vector.scalar_tensor_tensor(
+                    out=prods[:],
+                    in0=tg[i, h][:],
+                    scalar=-1.0 / J,
+                    in1=logs[:, i, HALF * h : HALF * (h + 1)],
+                    op0=ALU.mult,
+                    op1=ALU.mult,
+                    accum_out=acc[h][:, i : i + 1],
+                )
+
+            def ln(i):
+                nc.scalar.activation(out=logs[:, i, :], in_=onl[i // 2][:, i % 2, :], func=ACT.Ln)
+
+            cast(0)
+            wgroup(0)
+            xtrans(0, 0)
+            cast(1)
+            xtrans(0, 1)
+            prod(0, 0)
+            otrans(0)
+            oexit(0)
+            xtrans(1, 0)
+            xtrans(1, 1)
+            prod(0, 1)
+            oquant(0)
+            prod(1, 0)
+            cast(2)
+            ln(0)
+            xquant(0)
+            prod(1, 1)
+            xtrans(2, 0)
+            wquant(0)
+            xtrans(2, 1)
+            otrans(1)
+            xquant(1)
+            prod(2, 0)
+            ln(1)
+            zrest(0, 0)
+            oexit(1)
+            wgroup(1)
+            prod(2, 1)
+            zrest(0, 1)
+            wquant(1)
+            xquant(2)
+            zout(0, 0)
+            ln(2)
+            zrest(1, 0)
+            zout(0, 1)
+            zout(1, 0)
+            zrest(1, 1)
+            zout(1, 1)
+            otrans(2)
+            ln(3)
+            cast(3)
+            ln(4)
+            ln(5)
+            xtrans(3, 0)
+            exp(0, 0)
+            xtrans(3, 1)
+            oquant(1)
+            zrest(2, 0)
+            exp(0, 1)
+            oexit(2)
+            exp(1, 0)
+            exp(1, 1)
+            zout(2, 0)
+            zrest(2, 1)
+            cast(4)
+            cast(5)
+            zout(2, 1)
+            prod(3, 0)
+            xtrans(4, 0)
+            xtrans(4, 1)
+            xtrans(5, 0)
+            exp(2, 0)
+            mul(0, 0)
+            prod(3, 1)
+            xtrans(5, 1)
+            exp(2, 1)
+            xquant(3)
+            prod(4, 0)
+            otrans(3)
+            zrest(3, 0)
+            mul(0, 1)
+            prod(4, 1)
+            oquant(2)
+            ln(6)
+            prod(5, 0)
+            zout(3, 0)
+            mul(1, 0)
+            mul(1, 1)
+            prod(5, 1)
+            mul(2, 0)
+            xquant(4)
+            oexit(3)
+            zrest(3, 1)
+            cast(6)
+            mul(2, 1)
+            zrest(4, 0)
+            ln(7)
+            zrest(4, 1)
+            zout(3, 1)
+            xquant(5)
+            zout(4, 0)
+            mtrans(0)
+            cast(7)
+            xtrans(6, 0)
+            mtrans(1)
+            exp(3, 0)
+            xtrans(6, 1)
+            mexit(0)
+            mquant(0)
+            mul(3, 0)
+            exp(3, 1)
+            prod(6, 0)
+            mul(3, 1)
+            zrest(5, 0)
+            exp(4, 0)
+            mexit(1)
+            mul(4, 0)
+            zout(4, 1)
+            mquant(1)
+            zout(5, 0)
+            tmat(0, 0)
+            prod(6, 1)
+            xtrans(7, 0)
+            exp(4, 1)
+            exp(5, 0)
+            mtrans(2)
+            xquant(6)
+            lossp(0, 0)
+            prod(7, 0)
+            xtrans(7, 1)
+            mexit(2)
+            tcopy(0, 0)
+            mtrans(3)
+            tmat(0, 1)
+            tmat(1, 0)
+            lossp(0, 1)
+            mul(4, 1)
+            zrest(5, 1)
+            oquant(3)
+            mquant(2)
+            prod(7, 1)
+            lossp(1, 0)
+            tcopy(0, 1)
+            tcopy(1, 0)
+            zout(5, 1)
+            xquant(7)
+            zrest(6, 0)
+            tmat(1, 1)
+            zout(6, 0)
+            mul(5, 0)
+            exp(5, 1)
+            exp(6, 0)
+            mul(5, 1)
+            lossp(1, 1)
+            tmat(2, 0)
+            mexit(3)
+            zrest(6, 1)
+            zout(6, 1)
+            mtrans(4)
+            tcopy(1, 1)
+            exp(6, 1)
+            mexit(4)
+            mquant(3)
+            lossp(2, 0)
+            mtrans(5)
+            tmat(2, 1)
+            tcopy(2, 0)
+            mexit(5)
+            zrest(7, 0)
+            tmat(3, 0)
+            mul(6, 0)
+            lossp(2, 1)
+            mquant(4)
+            mul(6, 1)
+            tmat(3, 1)
+            tcopy(2, 1)
+            lossp(3, 0)
+            zout(7, 0)
+            exp(7, 0)
+            zrest(7, 1)
+            tcopy(3, 0)
+            mquant(5)
+            lossp(3, 1)
+            tmat(4, 0)
+            zout(7, 1)
+            mul(7, 0)
+            lossp(4, 0)
+            tmat(4, 1)
+            tcopy(3, 1)
+            exp(7, 1)
+            lossp(4, 1)
+            mtrans(6)
+            mul(7, 1)
+            mexit(6)
+            tmat(5, 0)
+            mquant(6)
+            tmat(5, 1)
+            tcopy(4, 0)
+            lossp(5, 0)
+            tcopy(4, 1)
+            mtrans(7)
+            mexit(7)
+            tcopy(5, 0)
+            lossp(5, 1)
+            tmat(6, 0)
+            tmat(6, 1)
+            tcopy(5, 1)
+            mquant(7)
+            lossp(6, 0)
+            tmat(7, 0)
+            tcopy(6, 0)
+            tmat(7, 1)
+            lossp(6, 1)
+            tcopy(6, 1)
+            lossp(7, 0)
+            tcopy(7, 0)
+            lossp(7, 1)
+            tcopy(7, 1)
+            nc.vector.tensor_tensor(out=lpad[:, 0:NT], in0=acc[0][:], in1=acc[1][:], op=ALU.add)
+            lt = psum.tile([P, 2, 2, P], F32, name="xt", tag="xt", bufs=4)
+            nc.tensor.transpose(lt[:, 0, 0, :], lpad[:], ident[:])
+            nc.scalar.copy(out=lrow[:], in_=lt[0:32, 0, 0, :])
+            nc.sync.dma_start(out=loss.rearrange("(i b) -> i b", b=P), in_=lrow[0:NT, :])

@@ -22,6 +22,9 @@ NT = B // P
 HALF = 512
 GR = KR // 512
 GM = F // 512
+EARLY = 0
+LAG = 5
+HELD = 2
 
 
 def tile_c51_shifted_log_loss_s3_kernel(
@@ -37,491 +40,402 @@ def tile_c51_shifted_log_loss_s3_kernel(
             return keep.tile(shape, dtype, name=name, tag=name, align_bytes=64)
 
         xr = [kept([P, KR], U8, "xr%d" % i) for i in range(NT)]
-        sc = kept([P, GR, 2, 2], F32, "sc")
-        base = kept([P, GR, 2 * F], U8, "base")
-        scb = kept([P, KR], F32, "scb")
+        sc = kept([P, GR, 4], F32, "sc")
+        scb = [kept([P, HALF], F32, "scb%d" % g) for g in range(GR)]
+        base = [kept([P, GR, F], U8, "base%d" % h) for h in range(2)]
         bsc = kept([P, GR, F], U8, "bsc")
         proj = kept([P, GM, 2 * J], U8, "proj")
         psc = kept([P, GM, J], U8, "psc")
-        wraw = kept([P, 4, F], BF16, "wraw")
+        wraw = [kept([P, 4, HALF], BF16, "wraw%d" % h) for h in range(2)]
         wgrp = [kept([P, HALF, 4], BF16, "wgrp%d" % h) for h in range(2)]
         wcod = [kept([P, HALF], U32, "wcod%d" % h) for h in range(2)]
         wscl = [kept([P, HALF], U8, "wscl%d" % h) for h in range(2)]
-        xo = [kept([P, 2, KO], BF16, "xo%d" % i) for i in range(NT // 2)]
-        onl = [kept([P, 2, J], BF16, "onl%d" % i) for i in range(NT // 2)]
-        logs = kept([P, NT, J], F32, "logs")
+        xo = [kept([P, 2, KO], BF16, "xo%d" % a) for a in range(NT // 2)]
+        onl = [kept([P, J], BF16, "onl%d" % i) for i in range(NT)]
+        logs = [kept([P, J], F32, "logs%d" % i) for i in range(NT)]
         spc = kept([P, F], BF16, "spc")
         ident = kept([P, P], F32, "ident")
-        acc = [kept([P, NT], F32, "acc%d" % h) for h in range(2)]
-        lpad = kept([P, P], F32, "lpad")
-        lrow = kept([32, P], F32, "lrow")
+        rowloss = kept([P, NT], F32, "rowloss")
         one = kept([P, 1], F32, "one")
         junk1 = kept([P, 1], F32, "junk1")
         xcod = [kept([P, GR, P], U32, "xcod%d" % i) for i in range(NT)]
         xscl = [kept([P, GR, P], U8, "xscl%d" % i) for i in range(NT)]
-        ocod = [kept([P, 2, P], U32, "ocod%d" % i) for i in range(NT // 2)]
-        oscl = [kept([P, 2, P], U8, "oscl%d" % i) for i in range(NT // 2)]
+        ocod = [kept([P, 2, P], U32, "ocod%d" % a) for a in range(NT // 2)]
+        oscl = [kept([P, 2, P], U8, "oscl%d" % a) for a in range(NT // 2)]
+
+        x_rows = x_rest_bytes.rearrange("(r i) k -> r i k", i=NT)
+        xo_rows = x_out.rearrange("(r i) k -> r i k", i=NT)
+        onl_rows = online.rearrange("(r i) j -> r i j", i=NT)
+        tgt_rows = target.rearrange("(r i) j -> r i j", i=NT)
+
+        wide, xt, grp, z, ex, mass, mt, mgrp, mcod, mscl, tg, tout = {}, {}, {}, {}, {}, {}, {}, {}, {}, {}, {}, {}
+
+        turn = {"tr": 0, "mm": 0}
+        ring = {"tr": [4, 5, 6, 7], "mm": [0, 1, 2, 3]}
+
+        def bank(kind, shape):
+            n = ring[kind][turn[kind] % len(ring[kind])]
+            turn[kind] = turn[kind] + 1
+            return psum.tile(shape, F32, name="bank%d" % n, tag="bank%d" % n, bufs=1)
+
+        def trbank():
+            return bank("tr", [P, 2, 2, P])
+
+        def mmbank():
+            return bank("mm", [P, HALF])
+
+        def load_x(i):
+            nc.sync.dma_start(out=xr[i][:], in_=x_rows[:, i, :])
+
+        def load_onl(i):
+            nc.sync.dma_start(out=onl[i][:], in_=onl_rows[:, i, :])
+
+        def load_xo(a):
+            nc.sync.dma_start(out=xo[a][:], in_=xo_rows[:, 2 * a : 2 * a + 2, :])
+
+        def load_w(h):
+            nc.sync.dma_start(out=wraw[h][:], in_=w_out.rearrange("(p j) n -> p j n", j=4)[:, :, HALF * h : HALF * (h + 1)])
+
+        def load_base(h):
+            nc.sync.dma_start(out=base[h][:], in_=base_words.rearrange("g p n -> p g n")[:, :, F * h : F * (h + 1)])
+
+        def load_scales(plane, rows):
+            for q in range(4):
+                nc.sync.dma_start(
+                    out=plane[32 * q : 32 * q + 4].bitcast(I32),
+                    in_=rows[:, 4 * q : 4 * q + 4, :].rearrange("g r n -> r g n").bitcast(I32),
+                )
+
+        def spread(g):
+            t = mmbank()
+            tg["s", g] = t
+            for j in range(4):
+                nc.tensor.transpose(t[:, P * j : P * (j + 1)], sc[:, g, j : j + 1].to_broadcast([P, P]), ident[:])
+
+        def spread_exit(g):
+            nc.scalar.copy(out=scb[g][:].rearrange("b (p j) -> b p j", j=4), in_=tg["s", g][:].rearrange("b (j p) -> b p j", j=4))
+
+        def widen(i, b):
+            if i not in wide:
+                wide[i] = work.tile([P, KR], BF16, name="wide", tag="wide", bufs=3)
+            if i < EARLY:
+                cols = slice(2 * HALF * b, 2 * HALF * (b + 1))
+                nc.vector.tensor_copy(out=wide[i][:, cols], in_=xr[i][:, cols].bitcast(FP8))
+                return
+            for g in (2 * b, 2 * b + 1):
+                cols = slice(HALF * g, HALF * (g + 1))
+                nc.vector.tensor_tensor(out=wide[i][:, cols], in0=xr[i][:, cols].bitcast(FP8), in1=scb[g][:], op=ALU.mult)
+
+        def xtrans(i, b):
+            t = trbank()
+            xt[i, b] = t
+            words = wide[i][:].bitcast(F32)
+            for gg in range(2):
+                g = 2 * b + gg
+                for u in range(2):
+                    nc.tensor.transpose(t[:, u, gg, :], words[:, 256 * g + u : 256 * (g + 1) : 2], ident[:])
+
+        def xexit(i, b):
+            if i not in grp:
+                grp[i] = work.tile([P, GR, P, 2, 2], BF16, name="grp", tag="grp", bufs=3, align_bytes=64)
+            if i < EARLY:
+                t = xt[i, b][:].rearrange("p u g r -> p (u g r)").bitcast(BF16).rearrange("p (u g r e) -> p g r u e", u=2, g=2, e=2)
+                s = sc[:, 2 * b : 2 * b + 2].rearrange("p g (u e) -> p g u e", u=2).unsqueeze(2).to_broadcast([P, 2, P, 2, 2])
+                nc.vector.tensor_tensor(out=grp[i][:, 2 * b : 2 * b + 2], in0=t, in1=s, op=ALU.mult)
+                return
+            nc.scalar.copy(
+                out=grp[i][:, 2 * b : 2 * b + 2].rearrange("p g r u e -> p (g r u e)").bitcast(F32).rearrange("p (g r u) -> p g r u", g=2, u=2),
+                in_=xt[i, b][:].rearrange("p u g r -> p g r u"),
+            )
+
+        def xquant(i):
+            nc.vector.quantize_mx(
+                out=xcod[i][:].rearrange("p g r -> p (g r)").bitcast(FP8X4),
+                scales=xscl[i][:].rearrange("p g r -> p (g r)"),
+                in_=grp[i][:].rearrange("p g r u e -> p (g r u e)"),
+            )
+
+        def otrans(a):
+            t = trbank()
+            xt["o", a] = t
+            for i in range(2):
+                words = xo[a][:, i, :].bitcast(F32)
+                for u in range(2):
+                    nc.tensor.transpose(t[:, u, i, :], words[:, u::2], ident[:])
+
+        def oexit(a):
+            grp["o", a] = work.tile([P, 2 * P * 4], BF16, name="ogrp", tag="ogrp", bufs=2, align_bytes=64)
+            nc.scalar.copy(
+                out=grp["o", a][:].bitcast(F32).rearrange("p (i r u) -> p i r u", i=2, u=2),
+                in_=xt["o", a][:].rearrange("p u i r -> p i r u"),
+            )
+
+        def oquant(a):
+            nc.vector.quantize_mx(
+                out=ocod[a][:].rearrange("p i r -> p (i r)").bitcast(FP8X4),
+                scales=oscl[a][:].rearrange("p i r -> p (i r)"),
+                in_=grp["o", a][:],
+            )
+
+        def wgroup(h):
+            nc.vector.tensor_copy(out=wgrp[h][:], in_=wraw[h][:].rearrange("p j n -> p n j"))
+
+        def wquant(h):
+            nc.vector.quantize_mx(out=wcod[h][:].bitcast(FP8X4), scales=wscl[h][:], in_=wgrp[h][:].rearrange("p n j -> p (n j)"))
+
+        def zrest(i, h):
+            t = bank("tr" if i == HELD else "mm", [P, HALF])
+            z[i, h] = t
+            for g in range(GR):
+                nc.tensor.matmul_mx(
+                    out=t[:],
+                    lhsT=xcod[i][:, g, :].bitcast(FP8X4),
+                    lhsT_scale=xscl[i][:, g, :],
+                    rhs=base[h][:, g, :].bitcast(FP4X4),
+                    rhs_scale=bsc[:, g, HALF * h : HALF * (h + 1)],
+                    start=(g == 0),
+                    stop=False,
+                )
+
+        def zout(i, h):
+            a, j = i // 2, i % 2
+            nc.tensor.matmul_mx(
+                out=z[i, h][:],
+                lhsT=ocod[a][:, j, :].bitcast(FP8X4),
+                lhsT_scale=oscl[a][:, j, :],
+                rhs=wcod[h][:].bitcast(FP8X4),
+                rhs_scale=wscl[h][:],
+                start=False,
+                stop=True,
+            )
+
+        def exp(i, h):
+            ex[i, h] = work.tile([P, 2, P, 2], F32, name="ex", tag="ex", bufs=6)
+            nc.scalar.activation(out=ex[i, h][:], in_=z[i, h][:].rearrange("b (p u e) -> b u p e", u=2, e=2), func=ACT.Exp)
+
+        def mul(i, h):
+            mass[i, h] = work.tile([P, 2, P, 2], BF16, name="mass", tag="mass", bufs=10)
+            nc.vector.tensor_tensor(
+                out=mass[i, h][:],
+                in0=ex[i, h][:],
+                in1=spc[:, HALF * h : HALF * (h + 1)].rearrange("b (p u e) -> b u p e", u=2, e=2),
+                op=ALU.mult,
+            )
+
+        def mtrans(i):
+            t = trbank()
+            mt[i] = t
+            for g in range(GM):
+                for u in range(2):
+                    nc.tensor.transpose(t[:, u, g, :], mass[i, g][:, u].rearrange("b p e -> b (p e)").bitcast(F32), ident[:])
+
+        def mexit(i):
+            mgrp[i] = work.tile([P, GM * P * 4], BF16, name="mgrp", tag="mgrp", bufs=2, align_bytes=64)
+            nc.scalar.copy(
+                out=mgrp[i][:].bitcast(F32).rearrange("p (g b u) -> p g b u", g=GM, u=2),
+                in_=mt[i][:].rearrange("p u g b -> p g b u"),
+            )
+
+        def mquant(i):
+            mcod[i] = work.tile([P, GM, P], U32, name="mcod", tag="mcod", bufs=6, align_bytes=64)
+            mscl[i] = work.tile([P, GM, P], U8, name="mscl", tag="mscl", bufs=6, align_bytes=64)
+            nc.vector.quantize_mx(
+                out=mcod[i][:].rearrange("p g b -> p (g b)").bitcast(FP8X4),
+                scales=mscl[i][:].rearrange("p g b -> p (g b)"),
+                in_=mgrp[i][:],
+            )
+
+        def tmat(i, h):
+            t = mmbank()
+            tg[i, h] = t
+            for g in range(GM):
+                nc.tensor.matmul_mx(
+                    out=t[:],
+                    lhsT=mcod[i][:, g, :].bitcast(FP8X4),
+                    lhsT_scale=mscl[i][:, g, :],
+                    rhs=proj[:, g, 2 * HALF * h : 2 * HALF * (h + 1)].bitcast(FP4X4),
+                    rhs_scale=psc[:, g, HALF * h : HALF * (h + 1)],
+                    start=(g == 0),
+                    stop=(g == GM - 1),
+                )
+
+        def tcopy(i, h):
+            if i not in tout:
+                tout[i] = work.tile([P, J], F32, name="tout", tag="tout", bufs=4)
+            cols = slice(HALF * h, HALF * (h + 1))
+            nc.scalar.copy(out=tout[i][:, cols], in_=tg[i, h][:])
+            nc.sync.dma_start(out=tgt_rows[:, i, cols], in_=tout[i][:, cols])
+
+        def lossp(i):
+            prods = work.tile([P, J], F32, name="prods", tag="prods", bufs=2)
+            nc.vector.scalar_tensor_tensor(
+                out=prods[:],
+                in0=tout[i][:],
+                scalar=-1.0 / J,
+                in1=logs[i][:],
+                op0=ALU.mult,
+                op1=ALU.mult,
+                accum_out=rowloss[:, i : i + 1],
+            )
+
+        def ln(i):
+            nc.scalar.activation(out=logs[i][:], in_=onl[i][:], func=ACT.Ln)
 
         with tc.manual_schedule():
             nc.vector.memset(one[:], 1.0)
             nc.vector.memset(bsc[:].rearrange("p g n -> p (g n)").bitcast(I32), 0)
             nc.vector.memset(psc[:].rearrange("p g n -> p (g n)").bitcast(I32), 0)
-            nc.vector.memset(lpad[:], 0.0)
             nc.scalar.activation(out=junk1[:], in_=one[:], func=ACT.Ln)
             make_identity(nc, ident[:])
-
-            def load_x(i):
-                if i == 0:
-                    nc.sync.dma_start(out=xr[i][:, 0:1024], in_=x_rest_bytes[0:P, 0:1024])
-                    nc.sync.dma_start(out=xr[i][:, 1024:2048], in_=x_rest_bytes[0:P, 1024:2048])
-                    return
-                nc.sync.dma_start(out=xr[i][:], in_=x_rest_bytes[P * i : P * (i + 1), :])
-
-            def load_onl(a):
-                nc.sync.dma_start(out=onl[a][:], in_=online[2 * P * a : 2 * P * (a + 1), :].rearrange("(i r) j -> r i j", r=P))
-
-            def load_xo(a):
-                nc.sync.dma_start(out=xo[a][:], in_=x_out[2 * P * a : 2 * P * (a + 1), :].rearrange("(i r) k -> r i k", r=P))
-
+            nc.sync.dma_start(out=sc[:], in_=x_rest_scale.rearrange("o (g p t) -> p (o g) t", p=P, t=4))
             load_x(0)
             load_x(1)
-            load_xo(0)
-            nc.sync.dma_start(out=sc[:].rearrange("p g u e -> p g (u e)"), in_=x_rest_scale.rearrange("o (g p t) -> p (o g) t", p=P, t=4))
-            nc.sync.dma_start(out=wraw[:], in_=w_out.rearrange("(p j) n -> p j n", j=4))
-            load_x(2)
             load_onl(0)
-            load_xo(1)
-            nc.sync.dma_start(out=base[:], in_=base_words.rearrange("g p n -> p g n"))
-            for q in range(4):
-                nc.sync.dma_start(
-                    out=bsc[32 * q : 32 * q + 4].bitcast(I32),
-                    in_=base_scales[:, 4 * q : 4 * q + 4, :].rearrange("g r n -> r g n").bitcast(I32),
-                )
+            load_base(0)
+            load_scales(bsc, base_scales)
             load_onl(1)
-            load_x(3)
+            load_x(2)
+            load_base(1)
             load_onl(2)
-            nc.sync.dma_start(out=scb[:], in_=x_rest_scale.rearrange("o k -> (o k)").partition_broadcast(P))
+            load_onl(3)
+            load_x(3)
+            load_xo(0)
+            load_onl(4)
+            load_w(0)
+            load_onl(5)
+            load_w(1)
+            load_xo(1)
+            load_onl(6)
+            load_onl(7)
             load_x(4)
-            load_x(7)
+            nc.sync.dma_start(out=spc[:], in_=spacing.partition_broadcast(P))
+            load_x(5)
             load_xo(2)
             load_x(6)
-            load_xo(3)
-            load_onl(3)
-            load_x(5)
-            nc.sync.dma_start(out=spc[:], in_=spacing.partition_broadcast(P))
             nc.sync.dma_start(out=proj[:], in_=proj_words.rearrange("g p n -> p g n"))
-            for q in range(4):
-                nc.sync.dma_start(
-                    out=psc[32 * q : 32 * q + 4].bitcast(I32),
-                    in_=proj_scales[:, 4 * q : 4 * q + 4, :].rearrange("g r n -> r g n").bitcast(I32),
-                )
+            load_scales(psc, proj_scales)
+            load_x(7)
+            load_xo(3)
 
-            wide = {}
-            xt = {}
-            grp = {}
-            z = {}
-            ex = {}
-            mass = {}
-            mt = {}
-            mgrp = {}
-            mcod = {}
-            mscl = {}
-            tg = {}
-            tout = {}
-
-            def cast(i):
-                if i in (3, 4, 5, 6, 7,):
-                    t = work.tile([P, KR], BF16, name="wide", tag="wide", bufs=4)
-                    wide[i] = t
-                    nc.vector.tensor_tensor(out=t[:], in0=xr[i][:].bitcast(FP8), in1=scb[:], op=ALU.mult)
-                    return
-                t = work.tile([P, KR], BF16, name="wide", tag="wide", bufs=4)
-                wide[i] = t
-                if i == 0:
-                    for c in (0, 1024):
-                        nc.scalar.copy(out=t[:, c : c + 512], in_=xr[i][:, c : c + 512].bitcast(FP8))
-                        nc.vector.tensor_copy(out=t[:, c + 512 : c + 1024], in_=xr[i][:, c + 512 : c + 1024].bitcast(FP8))
-                elif i == 1:
-                    nc.scalar.copy(out=t[:, 0:1024], in_=xr[i][:, 0:1024].bitcast(FP8))
-                    nc.vector.tensor_copy(out=t[:, 1024:2048], in_=xr[i][:, 1024:2048].bitcast(FP8))
-                else:
-                    nc.scalar.copy(out=t[:], in_=xr[i][:].bitcast(FP8))
-
-            def xtrans(i, b):
-                t = psum.tile([P, 2, 2, P], F32, name="xt", tag="xt", bufs=4)
-                xt[i, b] = t
-                words = wide[i][:].bitcast(F32)
-                for gg in range(2):
-                    g = 2 * b + gg
-                    for u in range(2):
-                        nc.tensor.transpose(t[:, u, gg, :], words[:, 256 * g + u : 256 * (g + 1) : 2], ident[:])
-
-            def prod(i, b):
-                if i not in grp:
-                    grp[i] = work.tile([P, GR, P, 2, 2], BF16, name="grp", tag="grp", bufs=4, align_bytes=64)
-                if i in (3, 4, 5, 6, 7,):
-                    nc.scalar.copy(
-                        out=grp[i][:, 2 * b : 2 * b + 2].rearrange("p g r u e -> p (g r u e)").bitcast(F32).rearrange("p (g r u) -> p g r u", g=2, u=2),
-                        in_=xt[i, b][:].rearrange("p u g r -> p g r u"),
-                    )
-                    return
-                t = xt[i, b][:].rearrange("p u g r -> p (u g r)").bitcast(BF16).rearrange("p (u g r e) -> p g r u e", u=2, g=2, e=2)
-                s = sc[:, 2 * b : 2 * b + 2].unsqueeze(2).to_broadcast([P, 2, P, 2, 2])
-                nc.vector.tensor_tensor(out=grp[i][:, 2 * b : 2 * b + 2], in0=t, in1=s, op=ALU.mult)
-
-            def xquant(i):
-                nc.vector.quantize_mx(
-                    out=xcod[i][:].rearrange("p g r -> p (g r)").bitcast(FP8X4),
-                    scales=xscl[i][:].rearrange("p g r -> p (g r)"),
-                    in_=grp[i][:].rearrange("p g r u e -> p (g r u e)"),
-                )
-
-            def otrans(a):
-                t = psum.tile([P, 2, 2, P], F32, name="xt", tag="xt", bufs=4)
-                xt["o", a] = t
-                for i in range(2):
-                    words = xo[a][:, i, :].bitcast(F32)
-                    for u in range(2):
-                        nc.tensor.transpose(t[:, u, i, :], words[:, u::2], ident[:])
-
-            def oexit(a):
-                grp["o", a] = work.tile([P, 2 * P * 4], BF16, name="ogrp", tag="ogrp", bufs=2, align_bytes=64)
-                nc.scalar.copy(
-                    out=grp["o", a][:].bitcast(F32).rearrange("p (i r u) -> p i r u", i=2, u=2),
-                    in_=xt["o", a][:].rearrange("p u i r -> p i r u"),
-                )
-
-            def oquant(a):
-                nc.vector.quantize_mx(
-                    out=ocod[a][:].rearrange("p i r -> p (i r)").bitcast(FP8X4),
-                    scales=oscl[a][:].rearrange("p i r -> p (i r)"),
-                    in_=grp["o", a][:],
-                )
-
-            def wgroup(h):
-                for c in range(0, HALF, P):
-                    nc.gpsimd.tensor_scalar(
-                        out=wgrp[h][:, c : c + P],
-                        in0=wraw[:, :, HALF * h + c : HALF * h + c + P].rearrange("p j n -> p n j"),
-                        scalar1=1.0,
-                        scalar2=0.0,
-                        op0=ALU.mult,
-                        op1=ALU.add,
-                    )
-
-            def wquant(h):
-                nc.vector.quantize_mx(out=wcod[h][:].bitcast(FP8X4), scales=wscl[h][:], in_=wgrp[h][:].rearrange("p n j -> p (n j)"))
-
-            def zrest(i, h):
-                t = psum.tile([P, HALF], F32, name="mm", tag="mm", bufs=4)
-                z[i, h] = t
-                for g in range(GR):
-                    nc.tensor.matmul_mx(
-                        out=t[:],
-                        lhsT=xcod[i][:, g, :].bitcast(FP8X4),
-                        lhsT_scale=xscl[i][:, g, :],
-                        rhs=base[:, g, 2 * HALF * h : 2 * HALF * (h + 1)].bitcast(FP4X4),
-                        rhs_scale=bsc[:, g, HALF * h : HALF * (h + 1)],
-                        start=(g == 0),
-                        stop=False,
-                    )
-
-            def zout(i, h):
-                a, j = i // 2, i % 2
-                nc.tensor.matmul_mx(
-                    out=z[i, h][:],
-                    lhsT=ocod[a][:, j, :].bitcast(FP8X4),
-                    lhsT_scale=oscl[a][:, j, :],
-                    rhs=wcod[h][:].bitcast(FP8X4),
-                    rhs_scale=wscl[h][:],
-                    start=False,
-                    stop=True,
-                )
-
-            def exp(i, h):
-                if i not in ex:
-                    ex[i] = work.tile([P, F], F32, name="ex", tag="ex", bufs=3)
-                nc.scalar.activation(out=ex[i][:, HALF * h : HALF * (h + 1)], in_=z[i, h][:], func=ACT.Exp)
-
-            def mul(i, h):
-                if i not in mass:
-                    mass[i] = work.tile([P, GM, 2, P, 2], BF16, name="mass", tag="mass", bufs=3)
-                eng = nc.vector
-                cols = slice(HALF * h, HALF * (h + 1))
-                eng.tensor_tensor(
-                    out=mass[i][:, h],
-                    in0=ex[i][:, cols].rearrange("b (p u e) -> b u p e", u=2, e=2),
-                    in1=spc[:, cols].rearrange("b (p u e) -> b u p e", u=2, e=2),
-                    op=ALU.mult,
-                )
-
-            def mtrans(i):
-                t = psum.tile([P, 2, 2, P], F32, name="xt", tag="xt", bufs=4)
-                mt[i] = t
-                for g in range(GM):
-                    for u in range(2):
-                        nc.tensor.transpose(t[:, u, g, :], mass[i][:, g, u].rearrange("b p e -> b (p e)").bitcast(F32), ident[:])
-
-            def mexit(i):
-                mgrp[i] = work.tile([P, GM * P * 4], BF16, name="mgrp", tag="mgrp", bufs=2, align_bytes=64)
-                nc.scalar.copy(
-                    out=mgrp[i][:].bitcast(F32).rearrange("p (g b u) -> p g b u", g=GM, u=2),
-                    in_=mt[i][:].rearrange("p u g b -> p g b u"),
-                )
-
-            def mquant(i):
-                mcod[i] = work.tile([P, GM, P], U32, name="mcod", tag="mcod", bufs=3, align_bytes=64)
-                mscl[i] = work.tile([P, GM, P], U8, name="mscl", tag="mscl", bufs=3, align_bytes=64)
-                nc.vector.quantize_mx(
-                    out=mcod[i][:].rearrange("p g b -> p (g b)").bitcast(FP8X4),
-                    scales=mscl[i][:].rearrange("p g b -> p (g b)"),
-                    in_=mgrp[i][:],
-                )
-
-            def tmat(i, h):
-                t = psum.tile([P, HALF], F32, name="mm", tag="mm", bufs=4)
-                tg[i, h] = t
-                for g in range(GM):
-                    nc.tensor.matmul_mx(
-                        out=t[:],
-                        lhsT=mcod[i][:, g, :].bitcast(FP8X4),
-                        lhsT_scale=mscl[i][:, g, :],
-                        rhs=proj[:, g, 2 * HALF * h : 2 * HALF * (h + 1)].bitcast(FP4X4),
-                        rhs_scale=psc[:, g, HALF * h : HALF * (h + 1)],
-                        start=(g == 0),
-                        stop=(g == GM - 1),
-                    )
-
-            def tcopy(i, h):
-                half = work.tile([P, HALF], F32, name="tout", tag="tout", bufs=8)
-                nc.scalar.copy(out=half[:], in_=tg[i, h][:])
-                nc.sync.dma_start(out=target[P * i : P * (i + 1), HALF * h : HALF * (h + 1)], in_=half[:])
-
-            def lossp(i, h):
-                prods = work.tile([P, HALF], F32, name="prods", tag="prods", bufs=2)
-                nc.vector.scalar_tensor_tensor(
-                    out=prods[:],
-                    in0=tg[i, h][:],
-                    scalar=-1.0 / J,
-                    in1=logs[:, i, HALF * h : HALF * (h + 1)],
-                    op0=ALU.mult,
-                    op1=ALU.mult,
-                    accum_out=acc[h][:, i : i + 1],
-                )
-
-            def ln(i):
-                nc.scalar.activation(out=logs[:, i, :], in_=onl[i // 2][:, i % 2, :], func=ACT.Ln)
-
-            cast(0)
-            wgroup(0)
-            xtrans(0, 0)
-            cast(1)
-            xtrans(0, 1)
-            prod(0, 0)
-            otrans(0)
-            oexit(0)
-            xtrans(1, 0)
-            xtrans(1, 1)
-            prod(0, 1)
-            oquant(0)
-            prod(1, 0)
-            cast(2)
-            ln(0)
+            for g in range(GR):
+                spread(g)
+                spread_exit(g)
+            for i in range(2):
+                for b in range(2):
+                    widen(i, b)
+                    xtrans(i, b)
+                    if b == 0:
+                        ln(i)
+                    xexit(i, b)
             xquant(0)
-            prod(1, 1)
-            xtrans(2, 0)
-            wquant(0)
-            xtrans(2, 1)
-            otrans(1)
-            xquant(1)
-            prod(2, 0)
-            ln(1)
             zrest(0, 0)
+            zrest(0, 1)
+            ln(2)
+            ln(3)
+            widen(2, 0)
+            xquant(1)
+            widen(2, 1)
+            xtrans(2, 0)
+            xtrans(2, 1)
+            otrans(0)
+            ln(4)
+            xexit(2, 0)
+            xexit(2, 1)
+            oexit(0)
+            widen(3, 0)
+            widen(3, 1)
+            zrest(1, 0)
+            zrest(1, 1)
+            wgroup(0)
+            xquant(2)
+            oquant(0)
+            ln(5)
+            ln(6)
+            xtrans(3, 0)
+            xtrans(3, 1)
+            otrans(1)
+            xexit(3, 0)
+            xexit(3, 1)
             oexit(1)
             wgroup(1)
-            prod(2, 1)
-            zrest(0, 1)
+            wquant(0)
             wquant(1)
-            xquant(2)
-            zout(0, 0)
-            ln(2)
-            zrest(1, 0)
-            zout(0, 1)
-            zout(1, 0)
-            zrest(1, 1)
-            zout(1, 1)
-            otrans(2)
-            ln(3)
-            cast(3)
-            ln(4)
-            ln(5)
-            xtrans(3, 0)
-            exp(0, 0)
-            xtrans(3, 1)
-            oquant(1)
             zrest(2, 0)
-            exp(0, 1)
-            oexit(2)
-            exp(1, 0)
-            exp(1, 1)
-            zout(2, 0)
             zrest(2, 1)
-            cast(4)
-            cast(5)
-            zout(2, 1)
-            prod(3, 0)
+            ln(7)
+            widen(4, 0)
+            oquant(1)
+            widen(4, 1)
+            xquant(3)
+            for i in range(3):
+                for h in range(2):
+                    zout(i, h)
             xtrans(4, 0)
             xtrans(4, 1)
-            xtrans(5, 0)
+            exp(0, 0)
+            exp(0, 1)
+            xexit(4, 0)
+            xexit(4, 1)
+            widen(5, 0)
+            widen(5, 1)
+            exp(1, 0)
+            exp(1, 1)
             exp(2, 0)
-            mul(0, 0)
-            prod(3, 1)
-            xtrans(5, 1)
             exp(2, 1)
-            xquant(3)
-            prod(4, 0)
-            otrans(3)
-            zrest(3, 0)
+            mul(0, 0)
             mul(0, 1)
-            prod(4, 1)
-            oquant(2)
-            ln(6)
-            prod(5, 0)
-            zout(3, 0)
-            mul(1, 0)
-            mul(1, 1)
-            prod(5, 1)
-            mul(2, 0)
-            xquant(4)
-            oexit(3)
-            zrest(3, 1)
-            cast(6)
-            mul(2, 1)
-            zrest(4, 0)
-            ln(7)
-            zrest(4, 1)
-            zout(3, 1)
-            xquant(5)
-            zout(4, 0)
-            mtrans(0)
-            cast(7)
-            xtrans(6, 0)
-            mtrans(1)
-            exp(3, 0)
-            xtrans(6, 1)
-            mexit(0)
-            mquant(0)
-            mul(3, 0)
-            exp(3, 1)
-            prod(6, 0)
-            mul(3, 1)
-            zrest(5, 0)
-            exp(4, 0)
-            mexit(1)
-            mul(4, 0)
-            zout(4, 1)
-            mquant(1)
-            zout(5, 0)
-            tmat(0, 0)
-            prod(6, 1)
-            xtrans(7, 0)
-            exp(4, 1)
-            exp(5, 0)
-            mtrans(2)
-            xquant(6)
-            lossp(0, 0)
-            prod(7, 0)
-            xtrans(7, 1)
-            mexit(2)
-            tcopy(0, 0)
-            mtrans(3)
-            tmat(0, 1)
-            tmat(1, 0)
-            lossp(0, 1)
-            mul(4, 1)
-            zrest(5, 1)
-            oquant(3)
-            mquant(2)
-            prod(7, 1)
-            lossp(1, 0)
-            tcopy(0, 1)
-            tcopy(1, 0)
-            zout(5, 1)
-            xquant(7)
-            zrest(6, 0)
-            tmat(1, 1)
-            zout(6, 0)
-            mul(5, 0)
-            exp(5, 1)
-            exp(6, 0)
-            mul(5, 1)
-            lossp(1, 1)
-            tmat(2, 0)
-            mexit(3)
-            zrest(6, 1)
-            zout(6, 1)
-            mtrans(4)
-            tcopy(1, 1)
-            exp(6, 1)
-            mexit(4)
-            mquant(3)
-            lossp(2, 0)
-            mtrans(5)
-            tmat(2, 1)
-            tcopy(2, 0)
-            mexit(5)
-            zrest(7, 0)
-            tmat(3, 0)
-            mul(6, 0)
-            lossp(2, 1)
-            mquant(4)
-            mul(6, 1)
-            tmat(3, 1)
-            tcopy(2, 1)
-            lossp(3, 0)
-            zout(7, 0)
-            exp(7, 0)
-            zrest(7, 1)
-            tcopy(3, 0)
-            mquant(5)
-            lossp(3, 1)
-            tmat(4, 0)
-            zout(7, 1)
-            mul(7, 0)
-            lossp(4, 0)
-            tmat(4, 1)
-            tcopy(3, 1)
-            exp(7, 1)
-            lossp(4, 1)
-            mtrans(6)
-            mul(7, 1)
-            mexit(6)
-            tmat(5, 0)
-            mquant(6)
-            tmat(5, 1)
-            tcopy(4, 0)
-            lossp(5, 0)
-            tcopy(4, 1)
-            mtrans(7)
-            mexit(7)
-            tcopy(5, 0)
-            lossp(5, 1)
-            tmat(6, 0)
-            tmat(6, 1)
-            tcopy(5, 1)
-            mquant(7)
-            lossp(6, 0)
-            tmat(7, 0)
-            tcopy(6, 0)
-            tmat(7, 1)
-            lossp(6, 1)
-            tcopy(6, 1)
-            lossp(7, 0)
-            tcopy(7, 0)
-            lossp(7, 1)
-            tcopy(7, 1)
-            nc.vector.tensor_tensor(out=lpad[:, 0:NT], in0=acc[0][:], in1=acc[1][:], op=ALU.add)
-            lt = psum.tile([P, 2, 2, P], F32, name="xt", tag="xt", bufs=4)
-            nc.tensor.transpose(lt[:, 0, 0, :], lpad[:], ident[:])
-            nc.scalar.copy(out=lrow[:], in_=lt[0:32, 0, 0, :])
-            nc.sync.dma_start(out=loss.rearrange("(i b) -> i b", b=P), in_=lrow[0:NT, :])
+
+            def turned(r):
+                return {3: [0], 4: [1], 5: [2], 6: [3, 4], 7: [5, 6], 8: [7]}.get(r, [])
+
+            for r in range(3, NT + LAG):
+                m = r - LAG
+                if r in (4, 5):
+                    oquant(r - 2)
+                if r < NT:
+                    zrest(r, 0)
+                    zout(r, 0)
+                if r + 1 < NT:
+                    xquant(r + 1)
+                if 1 <= r - 2 < 3:
+                    mul(r - 2, 0)
+                    mul(r - 2, 1)
+                if 0 <= m - 1:
+                    lossp(m - 1)
+                for i in turned(r - 1):
+                    mquant(i)
+                if r < NT:
+                    exp(r, 0)
+                    zrest(r, 1)
+                    zout(r, 1)
+                if r + 3 < NT:
+                    widen(r + 3, 0)
+                if 0 <= m:
+                    tmat(m, 0)
+                    tmat(m, 1)
+                if r < NT:
+                    mul(r, 0)
+                    exp(r, 1)
+                if r + 3 < NT:
+                    widen(r + 3, 1)
+                if r < NT:
+                    mul(r, 1)
+                if r + 2 < NT:
+                    xtrans(r + 2, 0)
+                    xtrans(r + 2, 1)
+                if r in (3, 4):
+                    otrans(r - 1)
+                for i in turned(r):
+                    mtrans(i)
+                if 0 <= m:
+                    tcopy(m, 0)
+                    tcopy(m, 1)
+                if r + 2 < NT:
+                    xexit(r + 2, 0)
+                    xexit(r + 2, 1)
+                if r in (3, 4):
+                    oexit(r - 1)
+                for i in turned(r):
+                    mexit(i)
+            lossp(NT - 1)
+            nc.sync.dma_start(out=loss.rearrange("(r i) -> r i", i=NT), in_=rowloss[:])

@@ -22,8 +22,8 @@ NT = B // P
 HALF = 512
 GR = KR // 512
 GM = F // 512
-EARLY = 0
-LAG = 5
+EARLY = 1
+LAG = 4
 HELD = 2
 
 
@@ -42,7 +42,7 @@ def tile_c51_shifted_log_loss_s3_kernel(
         xr = [kept([P, KR], U8, "xr%d" % i) for i in range(NT)]
         sc = kept([P, GR, 4], F32, "sc")
         scb = [kept([P, HALF], F32, "scb%d" % g) for g in range(GR)]
-        base = [kept([P, GR, F], U8, "base%d" % h) for h in range(2)]
+        base = [kept([P, 2, 2 * F], U8, "base%d" % b) for b in range(2)]
         bsc = kept([P, GR, F], U8, "bsc")
         proj = kept([P, GM, 2 * J], U8, "proj")
         psc = kept([P, GM, J], U8, "psc")
@@ -55,6 +55,8 @@ def tile_c51_shifted_log_loss_s3_kernel(
         logs = [kept([P, J], F32, "logs%d" % i) for i in range(NT)]
         spc = kept([P, F], BF16, "spc")
         ident = kept([P, P], F32, "ident")
+        zeros = kept([P, HALF], BF16, "zeros")
+        parts = kept([P, 2], F32, "parts")
         rowloss = kept([P, NT], F32, "rowloss")
         one = kept([P, 1], F32, "one")
         junk1 = kept([P, 1], F32, "junk1")
@@ -70,19 +72,18 @@ def tile_c51_shifted_log_loss_s3_kernel(
 
         wide, xt, grp, z, ex, mass, mt, mgrp, mcod, mscl, tg, tout = {}, {}, {}, {}, {}, {}, {}, {}, {}, {}, {}, {}
 
-        turn = {"tr": 0, "mm": 0}
-        ring = {"tr": [4, 5, 6, 7], "mm": [0, 1, 2, 3]}
+        sorted_x = {}
+        free = list(range(8))
+        owner = {}
 
-        def bank(kind, shape):
-            n = ring[kind][turn[kind] % len(ring[kind])]
-            turn[kind] = turn[kind] + 1
+        def bank(key, shape):
+            n = free[0]
+            free.remove(n)
+            owner[key] = n
             return psum.tile(shape, F32, name="bank%d" % n, tag="bank%d" % n, bufs=1)
 
-        def trbank():
-            return bank("tr", [P, 2, 2, P])
-
-        def mmbank():
-            return bank("mm", [P, HALF])
+        def emptied(key):
+            free.append(owner[key])
 
         def load_x(i):
             nc.sync.dma_start(out=xr[i][:], in_=x_rows[:, i, :])
@@ -97,7 +98,7 @@ def tile_c51_shifted_log_loss_s3_kernel(
             nc.sync.dma_start(out=wraw[h][:], in_=w_out.rearrange("(p j) n -> p j n", j=4)[:, :, HALF * h : HALF * (h + 1)])
 
         def load_base(h):
-            nc.sync.dma_start(out=base[h][:], in_=base_words.rearrange("g p n -> p g n")[:, :, F * h : F * (h + 1)])
+            nc.sync.dma_start(out=base[h][:], in_=base_words.rearrange("g p n -> p g n")[:, 2 * h : 2 * h + 2, :])
 
         def load_scales(plane, rows):
             for q in range(4):
@@ -107,13 +108,14 @@ def tile_c51_shifted_log_loss_s3_kernel(
                 )
 
         def spread(g):
-            t = mmbank()
+            t = bank(("s", g), [P, HALF])
             tg["s", g] = t
             for j in range(4):
                 nc.tensor.transpose(t[:, P * j : P * (j + 1)], sc[:, g, j : j + 1].to_broadcast([P, P]), ident[:])
 
         def spread_exit(g):
             nc.scalar.copy(out=scb[g][:].rearrange("b (p j) -> b p j", j=4), in_=tg["s", g][:].rearrange("b (j p) -> b p j", j=4))
+            emptied(("s", g))
 
         def widen(i, b):
             if i not in wide:
@@ -126,18 +128,28 @@ def tile_c51_shifted_log_loss_s3_kernel(
                 cols = slice(HALF * g, HALF * (g + 1))
                 nc.vector.tensor_tensor(out=wide[i][:, cols], in0=xr[i][:, cols].bitcast(FP8), in1=scb[g][:], op=ALU.mult)
 
+        def sort_words(i, b):
+            sorted_x[i, b] = work.tile([P, 2, 2, P], F32, name="sorted", tag="sorted", bufs=2)
+            nc.scalar.copy(out=sorted_x[i, b][:], in_=wide[i][:, 2 * HALF * b : 2 * HALF * (b + 1)].bitcast(F32).rearrange("r (g p u) -> r g u p", g=2, u=2))
+
+        def sort_out_words(a):
+            sorted_x["o", a] = work.tile([P, 2, 2, P], F32, name="sorted", tag="sorted", bufs=2)
+            nc.scalar.copy(out=sorted_x["o", a][:], in_=xo[a][:].rearrange("r i k -> r (i k)").bitcast(F32).rearrange("r (i p u) -> r i u p", i=2, u=2))
+
         def xtrans(i, b):
-            t = trbank()
+            t = bank(("x", i, b), [P, 2, 2, P])
             xt[i, b] = t
             words = wide[i][:].bitcast(F32)
             for gg in range(2):
                 g = 2 * b + gg
                 for u in range(2):
-                    nc.tensor.transpose(t[:, u, gg, :], words[:, 256 * g + u : 256 * (g + 1) : 2], ident[:])
+                    src = sorted_x[i, b][:, gg, u, :] if (i, b) in sorted_x else words[:, 256 * g + u : 256 * (g + 1) : 2]
+                    nc.tensor.transpose(t[:, u, gg, :], src, ident[:])
 
         def xexit(i, b):
             if i not in grp:
                 grp[i] = work.tile([P, GR, P, 2, 2], BF16, name="grp", tag="grp", bufs=3, align_bytes=64)
+            emptied(("x", i, b))
             if i < EARLY:
                 t = xt[i, b][:].rearrange("p u g r -> p (u g r)").bitcast(BF16).rearrange("p (u g r e) -> p g r u e", u=2, g=2, e=2)
                 s = sc[:, 2 * b : 2 * b + 2].rearrange("p g (u e) -> p g u e", u=2).unsqueeze(2).to_broadcast([P, 2, P, 2, 2])
@@ -156,14 +168,16 @@ def tile_c51_shifted_log_loss_s3_kernel(
             )
 
         def otrans(a):
-            t = trbank()
+            t = bank(("o", a), [P, 2, 2, P])
             xt["o", a] = t
             for i in range(2):
                 words = xo[a][:, i, :].bitcast(F32)
                 for u in range(2):
-                    nc.tensor.transpose(t[:, u, i, :], words[:, u::2], ident[:])
+                    src = sorted_x["o", a][:, i, u, :] if ("o", a) in sorted_x else words[:, u::2]
+                    nc.tensor.transpose(t[:, u, i, :], src, ident[:])
 
         def oexit(a):
+            emptied(("o", a))
             grp["o", a] = work.tile([P, 2 * P * 4], BF16, name="ogrp", tag="ogrp", bufs=2, align_bytes=64)
             nc.scalar.copy(
                 out=grp["o", a][:].bitcast(F32).rearrange("p (i r u) -> p i r u", i=2, u=2),
@@ -178,24 +192,37 @@ def tile_c51_shifted_log_loss_s3_kernel(
             )
 
         def wgroup(h):
-            nc.vector.tensor_copy(out=wgrp[h][:], in_=wraw[h][:].rearrange("p j n -> p n j"))
+            nc.vector.tensor_copy(
+                out=wgrp[h][:].rearrange("p (c i) j -> p c j i", i=4),
+                in_=wraw[h][:].rearrange("p j (c i) -> p c j i", i=4),
+            )
 
         def wquant(h):
             nc.vector.quantize_mx(out=wcod[h][:].bitcast(FP8X4), scales=wscl[h][:], in_=wgrp[h][:].rearrange("p n j -> p (n j)"))
 
+        def zpass(i, h, g):
+            if g == 0:
+                z[i, h] = bank(("z", i, h), [P, HALF])
+            nc.tensor.matmul_mx(
+                out=z[i, h][:],
+                lhsT=xcod[i][:, g, :].bitcast(FP8X4),
+                lhsT_scale=xscl[i][:, g, :],
+                rhs=base[g // 2][:, g % 2, F * h : F * (h + 1)].bitcast(FP4X4),
+                rhs_scale=bsc[:, g, HALF * h : HALF * (h + 1)],
+                start=(g == 0),
+                stop=False,
+            )
+
         def zrest(i, h):
-            t = bank("tr" if i == HELD else "mm", [P, HALF])
-            z[i, h] = t
             for g in range(GR):
-                nc.tensor.matmul_mx(
-                    out=t[:],
-                    lhsT=xcod[i][:, g, :].bitcast(FP8X4),
-                    lhsT_scale=xscl[i][:, g, :],
-                    rhs=base[h][:, g, :].bitcast(FP4X4),
-                    rhs_scale=bsc[:, g, HALF * h : HALF * (h + 1)],
-                    start=(g == 0),
-                    stop=False,
-                )
+                zpass(i, h, g)
+
+        def xquant_half(i, b):
+            nc.vector.quantize_mx(
+                out=xcod[i][:, 2 * b : 2 * b + 2].rearrange("p g r -> p (g r)").bitcast(FP8X4),
+                scales=xscl[i][:, 2 * b : 2 * b + 2].rearrange("p g r -> p (g r)"),
+                in_=grp[i][:, 2 * b : 2 * b + 2].rearrange("p g r u e -> p (g r u e)"),
+            )
 
         def zout(i, h):
             a, j = i // 2, i % 2
@@ -210,11 +237,12 @@ def tile_c51_shifted_log_loss_s3_kernel(
             )
 
         def exp(i, h):
-            ex[i, h] = work.tile([P, 2, P, 2], F32, name="ex", tag="ex", bufs=6)
+            emptied(("z", i, h))
+            ex[i, h] = work.tile([P, 2, P, 2], F32, name="ex", tag="ex", bufs=8)
             nc.scalar.activation(out=ex[i, h][:], in_=z[i, h][:].rearrange("b (p u e) -> b u p e", u=2, e=2), func=ACT.Exp)
 
         def mul(i, h):
-            mass[i, h] = work.tile([P, 2, P, 2], BF16, name="mass", tag="mass", bufs=10)
+            mass[i, h] = work.tile([P, 2, P, 2], BF16, name="mass", tag="mass", bufs=8)
             nc.vector.tensor_tensor(
                 out=mass[i, h][:],
                 in0=ex[i, h][:],
@@ -222,44 +250,65 @@ def tile_c51_shifted_log_loss_s3_kernel(
                 op=ALU.mult,
             )
 
-        def mtrans(i):
-            t = trbank()
-            mt[i] = t
-            for g in range(GM):
+        def mtrans(i, gs=(0, 1)):
+            t = bank(("m", i, gs), [P, 2, len(gs), P])
+            mt[i, gs] = t
+            for n, g in enumerate(gs):
                 for u in range(2):
-                    nc.tensor.transpose(t[:, u, g, :], mass[i, g][:, u].rearrange("b p e -> b (p e)").bitcast(F32), ident[:])
+                    nc.tensor.transpose(t[:, u, n, :], mass[i, g][:, u].rearrange("b p e -> b (p e)").bitcast(F32), ident[:])
 
-        def mexit(i):
-            mgrp[i] = work.tile([P, GM * P * 4], BF16, name="mgrp", tag="mgrp", bufs=2, align_bytes=64)
+        def mexit(i, gs=(0, 1)):
+            emptied(("m", i, gs))
+            mgrp[i, gs] = work.tile([P, len(gs) * P * 4], BF16, name="mgrp", tag="mgrp", bufs=3, align_bytes=64)
             nc.scalar.copy(
-                out=mgrp[i][:].bitcast(F32).rearrange("p (g b u) -> p g b u", g=GM, u=2),
-                in_=mt[i][:].rearrange("p u g b -> p g b u"),
+                out=mgrp[i, gs][:].bitcast(F32).rearrange("p (g b u) -> p g b u", g=len(gs), u=2),
+                in_=mt[i, gs][:].rearrange("p u g b -> p g b u"),
             )
 
-        def mquant(i):
-            mcod[i] = work.tile([P, GM, P], U32, name="mcod", tag="mcod", bufs=6, align_bytes=64)
-            mscl[i] = work.tile([P, GM, P], U8, name="mscl", tag="mscl", bufs=6, align_bytes=64)
+        def mquant(i, gs=(0, 1)):
+            cod = work.tile([P, len(gs), P], U32, name="mcod", tag="mcod", bufs=6, align_bytes=64)
+            scl = work.tile([P, len(gs), P], U8, name="mscl", tag="mscl", bufs=6, align_bytes=64)
+            for n, g in enumerate(gs):
+                mcod[i, g], mscl[i, g] = cod[:, n, :], scl[:, n, :]
             nc.vector.quantize_mx(
-                out=mcod[i][:].rearrange("p g b -> p (g b)").bitcast(FP8X4),
-                scales=mscl[i][:].rearrange("p g b -> p (g b)"),
-                in_=mgrp[i][:],
+                out=cod[:].rearrange("p g b -> p (g b)").bitcast(FP8X4),
+                scales=scl[:].rearrange("p g b -> p (g b)"),
+                in_=mgrp[i, gs][:],
+            )
+
+        def tpass(i, h, g):
+            if g == 0:
+                tg[i, h] = bank(("t", i, h), [P, HALF])
+            nc.tensor.matmul_mx(
+                out=tg[i, h][:],
+                lhsT=mcod[i, g].bitcast(FP8X4),
+                lhsT_scale=mscl[i, g],
+                rhs=proj[:, g, 2 * HALF * h : 2 * HALF * (h + 1)].bitcast(FP4X4),
+                rhs_scale=psc[:, g, HALF * h : HALF * (h + 1)],
+                start=(g == 0),
+                stop=(g == GM - 1),
             )
 
         def tmat(i, h):
-            t = mmbank()
-            tg[i, h] = t
             for g in range(GM):
-                nc.tensor.matmul_mx(
-                    out=t[:],
-                    lhsT=mcod[i][:, g, :].bitcast(FP8X4),
-                    lhsT_scale=mscl[i][:, g, :],
-                    rhs=proj[:, g, 2 * HALF * h : 2 * HALF * (h + 1)].bitcast(FP4X4),
-                    rhs_scale=psc[:, g, HALF * h : HALF * (h + 1)],
-                    start=(g == 0),
-                    stop=(g == GM - 1),
-                )
+                tpass(i, h, g)
+
+        def loss_half(i, h):
+            cols = slice(HALF * h, HALF * (h + 1))
+            nc.vector.scalar_tensor_tensor(
+                out=logs[i][:, cols],
+                in0=tout[i][:, cols],
+                scalar=-1.0 / J,
+                in1=logs[i][:, cols],
+                op0=ALU.mult,
+                op1=ALU.mult,
+                accum_out=parts[:, h : h + 1],
+            )
+            if h == 1:
+                nc.vector.tensor_tensor(out=rowloss[:, i : i + 1], in0=parts[:, 0:1], in1=parts[:, 1:2], op=ALU.add)
 
         def tcopy(i, h):
+            emptied(("t", i, h))
             if i not in tout:
                 tout[i] = work.tile([P, J], F32, name="tout", tag="tout", bufs=4)
             cols = slice(HALF * h, HALF * (h + 1))
@@ -267,9 +316,8 @@ def tile_c51_shifted_log_loss_s3_kernel(
             nc.sync.dma_start(out=tgt_rows[:, i, cols], in_=tout[i][:, cols])
 
         def lossp(i):
-            prods = work.tile([P, J], F32, name="prods", tag="prods", bufs=2)
             nc.vector.scalar_tensor_tensor(
-                out=prods[:],
+                out=logs[i][:],
                 in0=tout[i][:],
                 scalar=-1.0 / J,
                 in1=logs[i][:],
@@ -278,34 +326,41 @@ def tile_c51_shifted_log_loss_s3_kernel(
                 accum_out=rowloss[:, i : i + 1],
             )
 
+        def warm(n):
+            t = bank("w", [P, HALF])
+            for j in range(n):
+                nc.tensor.matmul(t[:], lhsT=zeros[:, 0:P], rhs=zeros[:], start=True, stop=True)
+            emptied("w")
+
         def ln(i):
             nc.scalar.activation(out=logs[i][:], in_=onl[i][:], func=ACT.Ln)
 
         with tc.manual_schedule():
             nc.vector.memset(one[:], 1.0)
+            nc.vector.memset(zeros[:].bitcast(I32), 0)
             nc.vector.memset(bsc[:].rearrange("p g n -> p (g n)").bitcast(I32), 0)
             nc.vector.memset(psc[:].rearrange("p g n -> p (g n)").bitcast(I32), 0)
             nc.scalar.activation(out=junk1[:], in_=one[:], func=ACT.Ln)
             make_identity(nc, ident[:])
-            nc.sync.dma_start(out=sc[:], in_=x_rest_scale.rearrange("o (g p t) -> p (o g) t", p=P, t=4))
             load_x(0)
-            load_x(1)
+            nc.sync.dma_start(out=sc[:], in_=x_rest_scale.rearrange("o (g p t) -> p (o g) t", p=P, t=4))
             load_onl(0)
+            load_onl(1)
+            load_x(1)
             load_base(0)
             load_scales(bsc, base_scales)
-            load_onl(1)
+            load_onl(2)
             load_x(2)
             load_base(1)
-            load_onl(2)
             load_onl(3)
-            load_x(3)
-            load_xo(0)
             load_onl(4)
-            load_w(0)
+            load_x(3)
             load_onl(5)
+            load_xo(0)
+            load_w(0)
+            load_onl(6)
             load_w(1)
             load_xo(1)
-            load_onl(6)
             load_onl(7)
             load_x(4)
             nc.sync.dma_start(out=spc[:], in_=spacing.partition_broadcast(P))
@@ -316,126 +371,239 @@ def tile_c51_shifted_log_loss_s3_kernel(
             load_scales(psc, proj_scales)
             load_x(7)
             load_xo(3)
-
-            for g in range(GR):
-                spread(g)
-                spread_exit(g)
-            for i in range(2):
-                for b in range(2):
-                    widen(i, b)
-                    xtrans(i, b)
-                    if b == 0:
-                        ln(i)
-                    xexit(i, b)
-            xquant(0)
-            zrest(0, 0)
-            zrest(0, 1)
+            warm(3)
+            widen(0, 0)
+            widen(0, 1)
+            xtrans(0, 0)
+            xtrans(0, 1)
+            warm(2)
+            ln(0)
+            ln(1)
+            spread(0)
+            spread_exit(0)
+            spread(1)
+            spread_exit(1)
+            spread(2)
+            spread_exit(2)
+            spread(3)
+            spread_exit(3)
+            warm(2)
+            xexit(0, 0)
+            xexit(0, 1)
+            xquant_half(0, 0)
+            xquant_half(0, 1)
+            widen(1, 0)
+            widen(1, 1)
+            for h in range(2):
+                zpass(0, h, 0)
+            xtrans(1, 0)
             ln(2)
+            xexit(1, 0)
+            for h in range(2):
+                zpass(0, h, 1)
+            xtrans(1, 1)
+            xexit(1, 1)
             ln(3)
+            for h in range(2):
+                zpass(0, h, 2)
+            for h in range(2):
+                zpass(0, h, 3)
             widen(2, 0)
-            xquant(1)
+            xquant_half(1, 0)
             widen(2, 1)
+            xquant_half(1, 1)
+            for g in (0, 1):
+                for h in range(2):
+                    zpass(1, h, g)
+            ln(4)
             xtrans(2, 0)
             xtrans(2, 1)
-            otrans(0)
-            ln(4)
             xexit(2, 0)
             xexit(2, 1)
-            oexit(0)
+            for g in (2, 3):
+                for h in range(2):
+                    zpass(1, h, g)
             widen(3, 0)
             widen(3, 1)
-            zrest(1, 0)
-            zrest(1, 1)
-            wgroup(0)
             xquant(2)
-            oquant(0)
             ln(5)
-            ln(6)
             xtrans(3, 0)
             xtrans(3, 1)
-            otrans(1)
+            ln(6)
             xexit(3, 0)
             xexit(3, 1)
+            wgroup(0)
+            zrest(2, 0)
+            otrans(0)
+            otrans(1)
+            oexit(0)
             oexit(1)
+            ln(7)
             wgroup(1)
             wquant(0)
             wquant(1)
-            zrest(2, 0)
-            zrest(2, 1)
-            ln(7)
-            widen(4, 0)
+            oquant(0)
             oquant(1)
-            widen(4, 1)
+            zrest(2, 1)
             xquant(3)
-            for i in range(3):
-                for h in range(2):
-                    zout(i, h)
-            xtrans(4, 0)
-            xtrans(4, 1)
+            widen(4, 0)
+            widen(4, 1)
+            zout(0, 0)
+            zout(0, 1)
+            zout(1, 0)
+            zout(1, 1)
+            zout(2, 0)
+            zout(2, 1)
+            zrest(3, 0)
+            zout(3, 0)
             exp(0, 0)
             exp(0, 1)
-            xexit(4, 0)
-            xexit(4, 1)
+            xtrans(4, 0)
+            xtrans(4, 1)
             widen(5, 0)
             widen(5, 1)
+            xexit(4, 0)
+            xexit(4, 1)
             exp(1, 0)
             exp(1, 1)
             exp(2, 0)
-            exp(2, 1)
+            zrest(3, 1)
+            zout(3, 1)
             mul(0, 0)
             mul(0, 1)
-
-            def turned(r):
-                return {3: [0], 4: [1], 5: [2], 6: [3, 4], 7: [5, 6], 8: [7]}.get(r, [])
-
-            for r in range(3, NT + LAG):
-                m = r - LAG
-                if r in (4, 5):
-                    oquant(r - 2)
-                if r < NT:
-                    zrest(r, 0)
-                    zout(r, 0)
-                if r + 1 < NT:
-                    xquant(r + 1)
-                if 1 <= r - 2 < 3:
-                    mul(r - 2, 0)
-                    mul(r - 2, 1)
-                if 0 <= m - 1:
-                    lossp(m - 1)
-                for i in turned(r - 1):
-                    mquant(i)
-                if r < NT:
-                    exp(r, 0)
-                    zrest(r, 1)
-                    zout(r, 1)
-                if r + 3 < NT:
-                    widen(r + 3, 0)
-                if 0 <= m:
-                    tmat(m, 0)
-                    tmat(m, 1)
-                if r < NT:
-                    mul(r, 0)
-                    exp(r, 1)
-                if r + 3 < NT:
-                    widen(r + 3, 1)
-                if r < NT:
-                    mul(r, 1)
-                if r + 2 < NT:
-                    xtrans(r + 2, 0)
-                    xtrans(r + 2, 1)
-                if r in (3, 4):
-                    otrans(r - 1)
-                for i in turned(r):
-                    mtrans(i)
-                if 0 <= m:
-                    tcopy(m, 0)
-                    tcopy(m, 1)
-                if r + 2 < NT:
-                    xexit(r + 2, 0)
-                    xexit(r + 2, 1)
-                if r in (3, 4):
-                    oexit(r - 1)
-                for i in turned(r):
-                    mexit(i)
-            lossp(NT - 1)
+            xquant(4)
+            otrans(2)
+            mtrans(0)
+            oexit(2)
+            exp(2, 1)
+            exp(3, 0)
+            exp(3, 1)
+            mexit(0)
+            mul(1, 0)
+            mul(1, 1)
+            oquant(2)
+            zrest(4, 0)
+            zout(4, 0)
+            widen(6, 0)
+            xtrans(5, 0)
+            xtrans(5, 1)
+            mquant(0)
+            mul(2, 0)
+            mul(2, 1)
+            exp(4, 0)
+            xexit(5, 0)
+            xexit(5, 1)
+            zrest(4, 1)
+            zout(4, 1)
+            widen(6, 1)
+            xquant(5)
+            tmat(0, 0)
+            tmat(0, 1)
+            exp(4, 1)
+            sort_words(6, 0)
+            sort_words(6, 1)
+            tcopy(0, 0)
+            tcopy(0, 1)
+            otrans(3)
+            mtrans(1)
+            oexit(3)
+            mexit(1)
+            mul(3, 0)
+            mul(3, 1)
+            zrest(5, 0)
+            zout(5, 0)
+            mul(4, 0)
+            mul(4, 1)
+            widen(7, 0)
+            oquant(3)
+            mquant(1)
+            xtrans(6, 0)
+            xtrans(6, 1)
+            mtrans(2)
+            mtrans(3)
+            exp(5, 0)
+            xexit(6, 0)
+            xexit(6, 1)
+            mexit(2)
+            mexit(3)
+            zrest(5, 1)
+            zout(5, 1)
+            xquant(6)
+            widen(7, 1)
+            tmat(1, 0)
+            tmat(1, 1)
+            exp(5, 1)
+            sort_words(7, 0)
+            sort_words(7, 1)
+            tcopy(1, 0)
+            tcopy(1, 1)
+            mul(5, 0)
+            mul(5, 1)
+            mquant(2)
+            mquant(3)
+            zrest(6, 0)
+            zout(6, 0)
+            lossp(0)
+            xtrans(7, 0)
+            xtrans(7, 1)
+            mtrans(4)
+            mtrans(5)
+            exp(6, 0)
+            xexit(7, 0)
+            xexit(7, 1)
+            mexit(4)
+            mexit(5)
+            zrest(6, 1)
+            zout(6, 1)
+            lossp(1)
+            xquant(7)
+            tmat(2, 0)
+            tmat(2, 1)
+            exp(6, 1)
+            tcopy(2, 0)
+            tcopy(2, 1)
+            mul(6, 0)
+            mul(6, 1)
+            mquant(4)
+            mquant(5)
+            zrest(7, 0)
+            zout(7, 0)
+            lossp(2)
+            exp(7, 0)
+            tmat(3, 0)
+            tmat(3, 1)
+            tcopy(3, 0)
+            tcopy(3, 1)
+            mtrans(6)
+            mexit(6)
+            zrest(7, 1)
+            zout(7, 1)
+            mul(7, 0)
+            lossp(3)
+            mquant(6)
+            exp(7, 1)
+            tmat(4, 0)
+            tmat(4, 1)
+            mul(7, 1)
+            tcopy(4, 0)
+            tcopy(4, 1)
+            tmat(5, 0)
+            tmat(5, 1)
+            mtrans(7)
+            mexit(7)
+            lossp(4)
+            tcopy(5, 0)
+            tcopy(5, 1)
+            mquant(7)
+            tmat(6, 0)
+            tmat(6, 1)
+            tcopy(6, 0)
+            tcopy(6, 1)
+            tmat(7, 0)
+            tmat(7, 1)
+            lossp(5)
+            tcopy(7, 0)
+            tcopy(7, 1)
+            lossp(6)
+            lossp(7)
             nc.sync.dma_start(out=loss.rearrange("(r i) -> r i", i=NT), in_=rowloss[:])

@@ -192,10 +192,7 @@ def tile_c51_shifted_log_loss_s3_kernel(
             )
 
         def wgroup(h):
-            nc.vector.tensor_copy(
-                out=wgrp[h][:].rearrange("p (c i) j -> p c j i", i=4),
-                in_=wraw[h][:].rearrange("p j (c i) -> p c j i", i=4),
-            )
+            nc.vector.tensor_copy(out=wgrp[h][:], in_=wraw[h][:].rearrange("p j n -> p n j"))
 
         def wquant(h):
             nc.vector.quantize_mx(out=wcod[h][:].bitcast(FP8X4), scales=wscl[h][:], in_=wgrp[h][:].rearrange("p n j -> p (n j)"))
@@ -337,7 +334,6 @@ def tile_c51_shifted_log_loss_s3_kernel(
 
         with tc.manual_schedule():
             nc.vector.memset(one[:], 1.0)
-            nc.vector.memset(zeros[:].bitcast(I32), 0)
             nc.vector.memset(bsc[:].rearrange("p g n -> p (g n)").bitcast(I32), 0)
             nc.vector.memset(psc[:].rearrange("p g n -> p (g n)").bitcast(I32), 0)
             nc.scalar.activation(out=junk1[:], in_=one[:], func=ACT.Ln)
@@ -346,21 +342,21 @@ def tile_c51_shifted_log_loss_s3_kernel(
             nc.sync.dma_start(out=sc[:], in_=x_rest_scale.rearrange("o (g p t) -> p (o g) t", p=P, t=4))
             load_onl(0)
             load_onl(1)
-            load_x(1)
             load_base(0)
             load_scales(bsc, base_scales)
+            load_x(1)
             load_onl(2)
             load_x(2)
-            load_base(1)
             load_onl(3)
-            load_onl(4)
+            load_base(1)
             load_x(3)
-            load_onl(5)
+            load_onl(4)
             load_xo(0)
+            load_onl(5)
+            load_xo(1)
             load_w(0)
             load_onl(6)
             load_w(1)
-            load_xo(1)
             load_onl(7)
             load_x(4)
             nc.sync.dma_start(out=spc[:], in_=spacing.partition_broadcast(P))
@@ -371,12 +367,10 @@ def tile_c51_shifted_log_loss_s3_kernel(
             load_scales(psc, proj_scales)
             load_x(7)
             load_xo(3)
-            warm(3)
             widen(0, 0)
             widen(0, 1)
             xtrans(0, 0)
             xtrans(0, 1)
-            warm(2)
             ln(0)
             ln(1)
             spread(0)
@@ -387,65 +381,57 @@ def tile_c51_shifted_log_loss_s3_kernel(
             spread_exit(2)
             spread(3)
             spread_exit(3)
-            warm(2)
             xexit(0, 0)
             xexit(0, 1)
             xquant_half(0, 0)
             xquant_half(0, 1)
             widen(1, 0)
             widen(1, 1)
-            for h in range(2):
-                zpass(0, h, 0)
-            xtrans(1, 0)
-            ln(2)
-            xexit(1, 0)
-            for h in range(2):
-                zpass(0, h, 1)
-            xtrans(1, 1)
-            xexit(1, 1)
-            ln(3)
-            for h in range(2):
-                zpass(0, h, 2)
-            for h in range(2):
-                zpass(0, h, 3)
-            widen(2, 0)
-            xquant_half(1, 0)
-            widen(2, 1)
-            xquant_half(1, 1)
             for g in (0, 1):
                 for h in range(2):
-                    zpass(1, h, g)
-            ln(4)
-            xtrans(2, 0)
-            xtrans(2, 1)
-            xexit(2, 0)
-            xexit(2, 1)
+                    zpass(0, h, g)
+            xtrans(1, 0)
+            xtrans(1, 1)
+            ln(2)
+            ln(3)
+            xexit(1, 0)
+            xexit(1, 1)
             for g in (2, 3):
                 for h in range(2):
-                    zpass(1, h, g)
+                    zpass(0, h, g)
+            widen(2, 0)
+            widen(2, 1)
+            xquant(1)
+            xtrans(2, 0)
+            xtrans(2, 1)
+            ln(4)
+            xexit(2, 0)
+            xexit(2, 1)
+            ln(5)
             widen(3, 0)
             widen(3, 1)
+            zrest(1, 0)
+            zrest(1, 1)
             xquant(2)
-            ln(5)
+            wgroup(0)
             xtrans(3, 0)
             xtrans(3, 1)
             ln(6)
             xexit(3, 0)
             xexit(3, 1)
-            wgroup(0)
+            ln(7)
             zrest(2, 0)
             otrans(0)
             otrans(1)
             oexit(0)
             oexit(1)
-            ln(7)
             wgroup(1)
             wquant(0)
             wquant(1)
+            xquant(3)
             oquant(0)
             oquant(1)
             zrest(2, 1)
-            xquant(3)
             widen(4, 0)
             widen(4, 1)
             zout(0, 0)
@@ -458,14 +444,14 @@ def tile_c51_shifted_log_loss_s3_kernel(
             zout(3, 0)
             exp(0, 0)
             exp(0, 1)
+            exp(1, 0)
+            exp(1, 1)
             xtrans(4, 0)
             xtrans(4, 1)
             widen(5, 0)
             widen(5, 1)
             xexit(4, 0)
             xexit(4, 1)
-            exp(1, 0)
-            exp(1, 1)
             exp(2, 0)
             zrest(3, 1)
             zout(3, 1)
@@ -587,14 +573,14 @@ def tile_c51_shifted_log_loss_s3_kernel(
             mul(7, 1)
             tcopy(4, 0)
             tcopy(4, 1)
-            tmat(5, 0)
-            tmat(5, 1)
             mtrans(7)
             mexit(7)
+            tmat(5, 0)
+            tmat(5, 1)
             lossp(4)
+            mquant(7)
             tcopy(5, 0)
             tcopy(5, 1)
-            mquant(7)
             tmat(6, 0)
             tmat(6, 1)
             tcopy(6, 0)

@@ -46,7 +46,7 @@ def tile_c51_shifted_log_loss_s3_kernel(
         bsc = kept([P, GR, F], U8, "bsc")
         proj = kept([P, GM, 2 * J], U8, "proj")
         psc = kept([P, GM, J], U8, "psc")
-        wraw = [kept([P, 4, HALF], BF16, "wraw%d" % h) for h in range(2)]
+        wraw = [work.tile([P, 4, HALF], BF16, name="wraw%d" % h, tag="scratch", bufs=2) for h in range(2)]
         wgrp = [kept([P, HALF, 4], BF16, "wgrp%d" % h) for h in range(2)]
         wcod = [kept([P, HALF], U32, "wcod%d" % h) for h in range(2)]
         wscl = [kept([P, HALF], U8, "wscl%d" % h) for h in range(2)]
@@ -56,7 +56,7 @@ def tile_c51_shifted_log_loss_s3_kernel(
         spc = kept([P, F], BF16, "spc")
         ident = kept([P, P], F32, "ident")
         zeros = kept([P, HALF], BF16, "zeros")
-        parts = kept([P, 2], F32, "parts")
+        parts = [kept([P, NT], F32, "parts%d" % h) for h in range(2)]
         rowloss = kept([P, NT], F32, "rowloss")
         one = kept([P, 1], F32, "one")
         junk1 = kept([P, 1], F32, "junk1")
@@ -130,11 +130,17 @@ def tile_c51_shifted_log_loss_s3_kernel(
 
         def sort_words(i, b):
             sorted_x[i, b] = work.tile([P, 2, 2, P], F32, name="sorted", tag="sorted", bufs=2)
-            nc.scalar.copy(out=sorted_x[i, b][:], in_=wide[i][:, 2 * HALF * b : 2 * HALF * (b + 1)].bitcast(F32).rearrange("r (g p u) -> r g u p", g=2, u=2))
+            nc.scalar.copy(
+                out=sorted_x[i, b][:].rearrange("r g u p -> r g p u"),
+                in_=wide[i][:, 2 * HALF * b : 2 * HALF * (b + 1)].bitcast(F32).rearrange("r (g p u) -> r g p u", g=2, u=2),
+            )
 
         def sort_out_words(a):
             sorted_x["o", a] = work.tile([P, 2, 2, P], F32, name="sorted", tag="sorted", bufs=2)
-            nc.scalar.copy(out=sorted_x["o", a][:], in_=xo[a][:].rearrange("r i k -> r (i k)").bitcast(F32).rearrange("r (i p u) -> r i u p", i=2, u=2))
+            nc.scalar.copy(
+                out=sorted_x["o", a][:].rearrange("r i u p -> r i p u"),
+                in_=xo[a][:].rearrange("r i k -> r (i k)").bitcast(F32).rearrange("r (i p u) -> r i p u", i=2, u=2),
+            )
 
         def xtrans(i, b):
             t = bank(("x", i, b), [P, 2, 2, P])
@@ -290,19 +296,21 @@ def tile_c51_shifted_log_loss_s3_kernel(
             for g in range(GM):
                 tpass(i, h, g)
 
-        def loss_half(i, h):
+        def loss_half(i, h, from_bank):
             cols = slice(HALF * h, HALF * (h + 1))
+            prods = work.tile([P, HALF], F32, name="prods", tag="scratch", bufs=2)
             nc.vector.scalar_tensor_tensor(
-                out=logs[i][:, cols],
-                in0=tout[i][:, cols],
+                out=prods[:],
+                in0=tg[i, h][:] if from_bank else tout[i][:, cols],
                 scalar=-1.0 / J,
                 in1=logs[i][:, cols],
                 op0=ALU.mult,
                 op1=ALU.mult,
-                accum_out=parts[:, h : h + 1],
+                accum_out=parts[h][:, i : i + 1],
             )
-            if h == 1:
-                nc.vector.tensor_tensor(out=rowloss[:, i : i + 1], in0=parts[:, 0:1], in1=parts[:, 1:2], op=ALU.add)
+
+        def loss_add(first):
+            nc.vector.tensor_tensor(out=rowloss[:, first:NT], in0=parts[0][:, first:NT], in1=parts[1][:, first:NT], op=ALU.add)
 
         def tcopy(i, h):
             emptied(("t", i, h))
@@ -313,8 +321,9 @@ def tile_c51_shifted_log_loss_s3_kernel(
             nc.sync.dma_start(out=tgt_rows[:, i, cols], in_=tout[i][:, cols])
 
         def lossp(i):
+            prods = work.tile([P, J], F32, name="prods", tag="scratch", bufs=2)
             nc.vector.scalar_tensor_tensor(
-                out=logs[i][:],
+                out=prods[:],
                 in0=tout[i][:],
                 scalar=-1.0 / J,
                 in1=logs[i][:],

@@ -22,7 +22,7 @@ NT = B // P
 HALF = 512
 GR = KR // 512
 GM = F // 512
-EARLY = 1
+EARLY = 0
 LAG = 4
 HELD = 2
 
@@ -54,8 +54,8 @@ def tile_c51_shifted_log_loss_s3_kernel(
         onl = [kept([P, J], BF16, "onl%d" % i) for i in range(NT)]
         logs = [kept([P, J], F32, "logs%d" % i) for i in range(NT)]
         spc = kept([P, F], BF16, "spc")
+        spacing_sorted = kept([P, GM, 2, P, 2], BF16, "spacing_sorted")
         ident = kept([P, P], F32, "ident")
-        zeros = kept([P, HALF], BF16, "zeros")
         parts = [kept([P, NT], F32, "parts%d" % h) for h in range(2)]
         rowloss = kept([P, NT], F32, "rowloss")
         one = kept([P, 1], F32, "one")
@@ -244,12 +244,18 @@ def tile_c51_shifted_log_loss_s3_kernel(
             ex[i, h] = work.tile([P, 2, P, 2], F32, name="ex", tag="ex", bufs=8)
             nc.scalar.activation(out=ex[i, h][:], in_=z[i, h][:].rearrange("b (p u e) -> b u p e", u=2, e=2), func=ACT.Exp)
 
+        def sort_spacing():
+            nc.vector.tensor_copy(
+                out=spacing_sorted[:].rearrange("b g u p e -> b (g u p e)").bitcast(F32).rearrange("b (g u p) -> b g u p", g=GM, u=2),
+                in_=spc[:].bitcast(F32).rearrange("b (g p u) -> b g u p", g=GM, u=2),
+            )
+
         def mul(i, h):
             mass[i, h] = work.tile([P, 2, P, 2], BF16, name="mass", tag="mass", bufs=8)
             nc.vector.tensor_tensor(
                 out=mass[i, h][:],
                 in0=ex[i, h][:],
-                in1=spc[:, HALF * h : HALF * (h + 1)].rearrange("b (p u e) -> b u p e", u=2, e=2),
+                in1=spacing_sorted[:, h],
                 op=ALU.mult,
             )
 
@@ -332,12 +338,6 @@ def tile_c51_shifted_log_loss_s3_kernel(
                 accum_out=rowloss[:, i : i + 1],
             )
 
-        def warm(n):
-            t = bank("w", [P, HALF])
-            for j in range(n):
-                nc.tensor.matmul(t[:], lhsT=zeros[:, 0:P], rhs=zeros[:], start=True, stop=True)
-            emptied("w")
-
         def ln(i):
             nc.scalar.activation(out=logs[i][:], in_=onl[i][:], func=ACT.Ln)
 
@@ -347,25 +347,25 @@ def tile_c51_shifted_log_loss_s3_kernel(
             nc.vector.memset(psc[:].rearrange("p g n -> p (g n)").bitcast(I32), 0)
             nc.scalar.activation(out=junk1[:], in_=one[:], func=ACT.Ln)
             make_identity(nc, ident[:])
-            load_x(0)
             nc.sync.dma_start(out=sc[:], in_=x_rest_scale.rearrange("o (g p t) -> p (o g) t", p=P, t=4))
+            load_x(0)
+            load_x(1)
             load_onl(0)
-            load_onl(1)
             load_base(0)
             load_scales(bsc, base_scales)
-            load_x(1)
-            load_onl(2)
+            load_onl(1)
             load_x(2)
-            load_onl(3)
             load_base(1)
+            load_onl(2)
+            load_onl(3)
             load_x(3)
-            load_onl(4)
             load_xo(0)
+            load_onl(4)
+            load_w(0)
             load_onl(5)
             load_xo(1)
-            load_w(0)
-            load_onl(6)
             load_w(1)
+            load_onl(6)
             load_onl(7)
             load_x(4)
             nc.sync.dma_start(out=spc[:], in_=spacing.partition_broadcast(P))
@@ -376,12 +376,6 @@ def tile_c51_shifted_log_loss_s3_kernel(
             load_scales(psc, proj_scales)
             load_x(7)
             load_xo(3)
-            widen(0, 0)
-            widen(0, 1)
-            xtrans(0, 0)
-            xtrans(0, 1)
-            ln(0)
-            ln(1)
             spread(0)
             spread_exit(0)
             spread(1)
@@ -390,57 +384,62 @@ def tile_c51_shifted_log_loss_s3_kernel(
             spread_exit(2)
             spread(3)
             spread_exit(3)
+            widen(0, 0)
+            xtrans(0, 0)
+            ln(0)
             xexit(0, 0)
+            widen(0, 1)
+            xtrans(0, 1)
             xexit(0, 1)
-            xquant_half(0, 0)
-            xquant_half(0, 1)
             widen(1, 0)
+            xtrans(1, 0)
+            ln(1)
+            xexit(1, 0)
             widen(1, 1)
+            xtrans(1, 1)
+            xexit(1, 1)
+            xquant(0)
             for g in (0, 1):
                 for h in range(2):
                     zpass(0, h, g)
-            xtrans(1, 0)
-            xtrans(1, 1)
-            ln(2)
-            ln(3)
-            xexit(1, 0)
-            xexit(1, 1)
             for g in (2, 3):
                 for h in range(2):
                     zpass(0, h, g)
+            ln(2)
+            ln(3)
             widen(2, 0)
-            widen(2, 1)
             xquant(1)
+            widen(2, 1)
             xtrans(2, 0)
             xtrans(2, 1)
+            otrans(0)
             ln(4)
             xexit(2, 0)
             xexit(2, 1)
-            ln(5)
+            oexit(0)
             widen(3, 0)
             widen(3, 1)
             zrest(1, 0)
             zrest(1, 1)
-            xquant(2)
             wgroup(0)
+            xquant(2)
+            oquant(0)
+            ln(5)
+            ln(6)
             xtrans(3, 0)
             xtrans(3, 1)
-            ln(6)
+            otrans(1)
             xexit(3, 0)
             xexit(3, 1)
-            ln(7)
-            zrest(2, 0)
-            otrans(0)
-            otrans(1)
-            oexit(0)
             oexit(1)
+            ln(7)
             wgroup(1)
             wquant(0)
             wquant(1)
-            xquant(3)
-            oquant(0)
-            oquant(1)
+            zrest(2, 0)
             zrest(2, 1)
+            xquant(3)
+            oquant(1)
             widen(4, 0)
             widen(4, 1)
             zout(0, 0)
@@ -457,116 +456,117 @@ def tile_c51_shifted_log_loss_s3_kernel(
             exp(1, 1)
             xtrans(4, 0)
             xtrans(4, 1)
+            otrans(2)
             widen(5, 0)
             widen(5, 1)
             xexit(4, 0)
             xexit(4, 1)
+            oexit(2)
             exp(2, 0)
+            exp(2, 1)
             zrest(3, 1)
             zout(3, 1)
+            sort_spacing()
             mul(0, 0)
             mul(0, 1)
             xquant(4)
-            otrans(2)
-            mtrans(0)
-            oexit(2)
-            exp(2, 1)
+            oquant(2)
             exp(3, 0)
             exp(3, 1)
-            mexit(0)
             mul(1, 0)
             mul(1, 1)
-            oquant(2)
             zrest(4, 0)
             zout(4, 0)
             widen(6, 0)
             xtrans(5, 0)
             xtrans(5, 1)
-            mquant(0)
+            mtrans(0)
+            mtrans(1)
             mul(2, 0)
             mul(2, 1)
             exp(4, 0)
             xexit(5, 0)
             xexit(5, 1)
+            mexit(0)
+            mexit(1)
             zrest(4, 1)
             zout(4, 1)
             widen(6, 1)
             xquant(5)
-            tmat(0, 0)
-            tmat(0, 1)
+            mquant(0)
+            mquant(1)
             exp(4, 1)
             sort_words(6, 0)
             sort_words(6, 1)
-            tcopy(0, 0)
-            tcopy(0, 1)
-            otrans(3)
-            mtrans(1)
-            oexit(3)
-            mexit(1)
             mul(3, 0)
             mul(3, 1)
             zrest(5, 0)
             zout(5, 0)
+            tmat(0, 0)
+            tmat(0, 1)
             mul(4, 0)
             mul(4, 1)
             widen(7, 0)
-            oquant(3)
-            mquant(1)
             xtrans(6, 0)
             xtrans(6, 1)
+            otrans(3)
             mtrans(2)
-            mtrans(3)
             exp(5, 0)
             xexit(6, 0)
             xexit(6, 1)
+            oexit(3)
+            tcopy(0, 0)
+            tcopy(0, 1)
             mexit(2)
-            mexit(3)
             zrest(5, 1)
             zout(5, 1)
-            xquant(6)
-            widen(7, 1)
             tmat(1, 0)
             tmat(1, 1)
+            widen(7, 1)
+            xquant(6)
+            oquant(3)
             exp(5, 1)
             sort_words(7, 0)
             sort_words(7, 1)
             tcopy(1, 0)
             tcopy(1, 1)
+            mquant(2)
             mul(5, 0)
             mul(5, 1)
-            mquant(2)
-            mquant(3)
             zrest(6, 0)
             zout(6, 0)
+            tmat(2, 0)
+            tmat(2, 1)
             lossp(0)
             xtrans(7, 0)
             xtrans(7, 1)
+            mtrans(3)
             mtrans(4)
             mtrans(5)
             exp(6, 0)
             xexit(7, 0)
             xexit(7, 1)
-            mexit(4)
-            mexit(5)
+            tcopy(2, 0)
+            tcopy(2, 1)
+            mexit(3)
             zrest(6, 1)
             zout(6, 1)
             lossp(1)
             xquant(7)
-            tmat(2, 0)
-            tmat(2, 1)
-            exp(6, 1)
-            tcopy(2, 0)
-            tcopy(2, 1)
             mul(6, 0)
+            mquant(3)
+            exp(6, 1)
+            mexit(4)
+            mexit(5)
             mul(6, 1)
+            lossp(2)
             mquant(4)
             mquant(5)
             zrest(7, 0)
             zout(7, 0)
-            lossp(2)
-            exp(7, 0)
             tmat(3, 0)
             tmat(3, 1)
+            exp(7, 0)
             tcopy(3, 0)
             tcopy(3, 1)
             mtrans(6)

@@ -22,9 +22,7 @@ NT = B // P
 HALF = 512
 GR = KR // 512
 GM = F // 512
-EARLY = 0
-LAG = 4
-HELD = 2
+W_FIRST = 256
 
 
 def tile_c51_shifted_log_loss_s3_kernel(
@@ -34,36 +32,35 @@ def tile_c51_shifted_log_loss_s3_kernel(
     with ExitStack() as ctx:
         keep = ctx.enter_context(tc.tile_pool(name="keep", bufs=1))
         work = ctx.enter_context(tc.tile_pool(name="work", bufs=3))
-        psum = ctx.enter_context(tc.psum_pool(name="psum", bufs=4))
+        psum = ctx.enter_context(tc.psum_pool(name="psum", bufs=1))
 
         def kept(shape, dtype, name):
             return keep.tile(shape, dtype, name=name, tag=name, align_bytes=64)
 
         xr = [kept([P, KR], U8, "xr%d" % i) for i in range(NT)]
         sc = kept([P, GR, 4], F32, "sc")
-        scb = [kept([P, HALF], F32, "scb%d" % g) for g in range(GR)]
+        scb = kept([P, KR], F32, "scb")
         base = [kept([P, 2, 2 * F], U8, "base%d" % b) for b in range(2)]
         bsc = kept([P, GR, F], U8, "bsc")
         proj = kept([P, GM, 2 * J], U8, "proj")
         psc = kept([P, GM, J], U8, "psc")
-        wraw = [work.tile([P, 4, HALF], BF16, name="wraw%d" % h, tag="scratch", bufs=2) for h in range(2)]
-        wgrp = [kept([P, HALF, 4], BF16, "wgrp%d" % h) for h in range(2)]
-        wcod = [kept([P, HALF], U32, "wcod%d" % h) for h in range(2)]
-        wscl = [kept([P, HALF], U8, "wscl%d" % h) for h in range(2)]
-        xo = [kept([P, 2, KO], BF16, "xo%d" % a) for a in range(NT // 2)]
+        w_cols = [(0, W_FIRST), (W_FIRST, F)]
+        wraw = [work.tile([P, 4, c1 - c0], BF16, name="wraw%d" % n, tag="scratch", bufs=2) for n, (c0, c1) in enumerate(w_cols)]
+        wgrp = kept([P, F, 4], BF16, "wgrp")
+        wcod = kept([P, F], U32, "wcod")
+        wscl = kept([P, F], U8, "wscl")
+        xo = [kept([P, 4, KO], BF16, "xo%d" % a) for a in range(2)]
         onl = [kept([P, J], BF16, "onl%d" % i) for i in range(NT)]
         logs = [kept([P, J], F32, "logs%d" % i) for i in range(NT)]
         spc = kept([P, F], BF16, "spc")
-        spacing_sorted = kept([P, GM, 2, P, 2], BF16, "spacing_sorted")
         ident = kept([P, P], F32, "ident")
-        parts = [kept([P, NT], F32, "parts%d" % h) for h in range(2)]
         rowloss = kept([P, NT], F32, "rowloss")
         one = kept([P, 1], F32, "one")
         junk1 = kept([P, 1], F32, "junk1")
         xcod = [kept([P, GR, P], U32, "xcod%d" % i) for i in range(NT)]
         xscl = [kept([P, GR, P], U8, "xscl%d" % i) for i in range(NT)]
-        ocod = [kept([P, 2, P], U32, "ocod%d" % a) for a in range(NT // 2)]
-        oscl = [kept([P, 2, P], U8, "oscl%d" % a) for a in range(NT // 2)]
+        ocod = [kept([P, 4, P], U32, "ocod%d" % a) for a in range(2)]
+        oscl = [kept([P, 4, P], U8, "oscl%d" % a) for a in range(2)]
 
         x_rows = x_rest_bytes.rearrange("(r i) k -> r i k", i=NT)
         xo_rows = x_out.rearrange("(r i) k -> r i k", i=NT)
@@ -71,7 +68,6 @@ def tile_c51_shifted_log_loss_s3_kernel(
         tgt_rows = target.rearrange("(r i) j -> r i j", i=NT)
 
         wide, xt, grp, z, ex, mass, mt, mgrp, mcod, mscl, tg, tout = {}, {}, {}, {}, {}, {}, {}, {}, {}, {}, {}, {}
-
         sorted_x = {}
         free = list(range(8))
         owner = {}
@@ -92,13 +88,13 @@ def tile_c51_shifted_log_loss_s3_kernel(
             nc.sync.dma_start(out=onl[i][:], in_=onl_rows[:, i, :])
 
         def load_xo(a):
-            nc.sync.dma_start(out=xo[a][:], in_=xo_rows[:, 2 * a : 2 * a + 2, :])
+            nc.sync.dma_start(out=xo[a][:], in_=xo_rows[:, 4 * a : 4 * a + 4, :])
 
-        def load_w(h):
-            nc.sync.dma_start(out=wraw[h][:], in_=w_out.rearrange("(p j) n -> p j n", j=4)[:, :, HALF * h : HALF * (h + 1)])
+        def load_w(n):
+            nc.sync.dma_start(out=wraw[n][:], in_=w_out.rearrange("(p j) n -> p j n", j=4)[:, :, w_cols[n][0] : w_cols[n][1]])
 
-        def load_base(h):
-            nc.sync.dma_start(out=base[h][:], in_=base_words.rearrange("g p n -> p g n")[:, 2 * h : 2 * h + 2, :])
+        def load_base(b):
+            nc.sync.dma_start(out=base[b][:], in_=base_words.rearrange("g p n -> p g n")[:, 2 * b : 2 * b + 2, :])
 
         def load_scales(plane, rows):
             for q in range(4):
@@ -108,39 +104,17 @@ def tile_c51_shifted_log_loss_s3_kernel(
                 )
 
         def spread(g):
-            t = bank(("s", g), [P, HALF])
-            tg["s", g] = t
+            t = bank(("s", g), [P, 4, P])
             for j in range(4):
-                nc.tensor.transpose(t[:, P * j : P * (j + 1)], sc[:, g, j : j + 1].to_broadcast([P, P]), ident[:])
-
-        def spread_exit(g):
-            nc.scalar.copy(out=scb[g][:].rearrange("b (p j) -> b p j", j=4), in_=tg["s", g][:].rearrange("b (j p) -> b p j", j=4))
+                nc.tensor.transpose(t[:, j, :], sc[:, g, j : j + 1].to_broadcast([P, P]), ident[:])
+            nc.scalar.copy(out=scb[:, HALF * g : HALF * (g + 1)].rearrange("b (p j) -> b p j", j=4), in_=t[:].rearrange("b j p -> b p j"))
             emptied(("s", g))
 
-        def widen(i, b):
+        def widen(i, g0=0, g1=GR):
             if i not in wide:
                 wide[i] = work.tile([P, KR], BF16, name="wide", tag="wide", bufs=3)
-            if i < EARLY:
-                cols = slice(2 * HALF * b, 2 * HALF * (b + 1))
-                nc.vector.tensor_copy(out=wide[i][:, cols], in_=xr[i][:, cols].bitcast(FP8))
-                return
-            for g in (2 * b, 2 * b + 1):
-                cols = slice(HALF * g, HALF * (g + 1))
-                nc.vector.tensor_tensor(out=wide[i][:, cols], in0=xr[i][:, cols].bitcast(FP8), in1=scb[g][:], op=ALU.mult)
-
-        def sort_words(i, b):
-            sorted_x[i, b] = work.tile([P, 2, 2, P], F32, name="sorted", tag="sorted", bufs=2)
-            nc.scalar.copy(
-                out=sorted_x[i, b][:].rearrange("r g u p -> r g p u"),
-                in_=wide[i][:, 2 * HALF * b : 2 * HALF * (b + 1)].bitcast(F32).rearrange("r (g p u) -> r g p u", g=2, u=2),
-            )
-
-        def sort_out_words(a):
-            sorted_x["o", a] = work.tile([P, 2, 2, P], F32, name="sorted", tag="sorted", bufs=2)
-            nc.scalar.copy(
-                out=sorted_x["o", a][:].rearrange("r i u p -> r i p u"),
-                in_=xo[a][:].rearrange("r i k -> r (i k)").bitcast(F32).rearrange("r (i p u) -> r i p u", i=2, u=2),
-            )
+            cols = slice(HALF * g0, HALF * g1)
+            nc.vector.tensor_tensor(out=wide[i][:, cols], in0=xr[i][:, cols].bitcast(FP8), in1=scb[:, cols], op=ALU.mult)
 
         def xtrans(i, b):
             t = bank(("x", i, b), [P, 2, 2, P])
@@ -154,15 +128,10 @@ def tile_c51_shifted_log_loss_s3_kernel(
 
         def xexit(i, b):
             if i not in grp:
-                grp[i] = work.tile([P, GR, P, 2, 2], BF16, name="grp", tag="grp", bufs=3, align_bytes=64)
+                grp[i] = work.tile([P, GR * P * 4], BF16, name="grp", tag="grp", bufs=3, align_bytes=64)
             emptied(("x", i, b))
-            if i < EARLY:
-                t = xt[i, b][:].rearrange("p u g r -> p (u g r)").bitcast(BF16).rearrange("p (u g r e) -> p g r u e", u=2, g=2, e=2)
-                s = sc[:, 2 * b : 2 * b + 2].rearrange("p g (u e) -> p g u e", u=2).unsqueeze(2).to_broadcast([P, 2, P, 2, 2])
-                nc.vector.tensor_tensor(out=grp[i][:, 2 * b : 2 * b + 2], in0=t, in1=s, op=ALU.mult)
-                return
             nc.scalar.copy(
-                out=grp[i][:, 2 * b : 2 * b + 2].rearrange("p g r u e -> p (g r u e)").bitcast(F32).rearrange("p (g r u) -> p g r u", g=2, u=2),
+                out=grp[i][:, 2 * HALF * b : 2 * HALF * (b + 1)].bitcast(F32).rearrange("p (g r u) -> p g r u", g=2, u=2),
                 in_=xt[i, b][:].rearrange("p u g r -> p g r u"),
             )
 
@@ -170,23 +139,23 @@ def tile_c51_shifted_log_loss_s3_kernel(
             nc.vector.quantize_mx(
                 out=xcod[i][:].rearrange("p g r -> p (g r)").bitcast(FP8X4),
                 scales=xscl[i][:].rearrange("p g r -> p (g r)"),
-                in_=grp[i][:].rearrange("p g r u e -> p (g r u e)"),
+                in_=grp[i][:],
             )
 
         def otrans(a):
             t = bank(("o", a), [P, 2, 2, P])
             xt["o", a] = t
             for i in range(2):
-                words = xo[a][:, i, :].bitcast(F32)
+                words = xo[a // 2][:, 2 * (a % 2) + i, :].bitcast(F32)
                 for u in range(2):
-                    src = sorted_x["o", a][:, i, u, :] if ("o", a) in sorted_x else words[:, u::2]
-                    nc.tensor.transpose(t[:, u, i, :], src, ident[:])
+                    nc.tensor.transpose(t[:, u, i, :], words[:, u::2], ident[:])
 
         def oexit(a):
             emptied(("o", a))
-            grp["o", a] = work.tile([P, 2 * P * 4], BF16, name="ogrp", tag="ogrp", bufs=2, align_bytes=64)
+            if a % 2 == 0:
+                grp["o", a // 2] = work.tile([P, 4 * P * 4], BF16, name="grp", tag="grp", bufs=3, align_bytes=64)
             nc.scalar.copy(
-                out=grp["o", a][:].bitcast(F32).rearrange("p (i r u) -> p i r u", i=2, u=2),
+                out=grp["o", a // 2][:, 2 * HALF * (a % 2) : 2 * HALF * (a % 2 + 1)].bitcast(F32).rearrange("p (i r u) -> p i r u", i=2, u=2),
                 in_=xt["o", a][:].rearrange("p u i r -> p i r u"),
             )
 
@@ -197,11 +166,16 @@ def tile_c51_shifted_log_loss_s3_kernel(
                 in_=grp["o", a][:],
             )
 
-        def wgroup(h):
-            nc.vector.tensor_copy(out=wgrp[h][:], in_=wraw[h][:].rearrange("p j n -> p n j"))
+        def wgroup(c0, c1, on_scalar=False):
+            n = 0 if c1 <= W_FIRST else 1
+            src = wraw[n][:, :, c0 - w_cols[n][0] : c1 - w_cols[n][0]].rearrange("p j n -> p n j")
+            if on_scalar:
+                nc.scalar.copy(out=wgrp[:, c0:c1], in_=src)
+            else:
+                nc.vector.tensor_copy(out=wgrp[:, c0:c1], in_=src)
 
-        def wquant(h):
-            nc.vector.quantize_mx(out=wcod[h][:].bitcast(FP8X4), scales=wscl[h][:], in_=wgrp[h][:].rearrange("p n j -> p (n j)"))
+        def wquant():
+            nc.vector.quantize_mx(out=wcod[:].bitcast(FP8X4), scales=wscl[:], in_=wgrp[:].rearrange("p n j -> p (n j)"))
 
         def zpass(i, h, g):
             if g == 0:
@@ -220,103 +194,82 @@ def tile_c51_shifted_log_loss_s3_kernel(
             for g in range(GR):
                 zpass(i, h, g)
 
-        def xquant_half(i, b):
-            nc.vector.quantize_mx(
-                out=xcod[i][:, 2 * b : 2 * b + 2].rearrange("p g r -> p (g r)").bitcast(FP8X4),
-                scales=xscl[i][:, 2 * b : 2 * b + 2].rearrange("p g r -> p (g r)"),
-                in_=grp[i][:, 2 * b : 2 * b + 2].rearrange("p g r u e -> p (g r u e)"),
-            )
-
         def zout(i, h):
-            a, j = i // 2, i % 2
             nc.tensor.matmul_mx(
                 out=z[i, h][:],
-                lhsT=ocod[a][:, j, :].bitcast(FP8X4),
-                lhsT_scale=oscl[a][:, j, :],
-                rhs=wcod[h][:].bitcast(FP8X4),
-                rhs_scale=wscl[h][:],
+                lhsT=ocod[i // 4][:, i % 4, :].bitcast(FP8X4),
+                lhsT_scale=oscl[i // 4][:, i % 4, :],
+                rhs=wcod[:, HALF * h : HALF * (h + 1)].bitcast(FP8X4),
+                rhs_scale=wscl[:, HALF * h : HALF * (h + 1)],
                 start=False,
                 stop=True,
             )
 
         def exp(i, h):
             emptied(("z", i, h))
-            ex[i, h] = work.tile([P, 2, P, 2], F32, name="ex", tag="ex", bufs=8)
-            nc.scalar.activation(out=ex[i, h][:], in_=z[i, h][:].rearrange("b (p u e) -> b u p e", u=2, e=2), func=ACT.Exp)
-
-        def sort_spacing():
-            nc.vector.tensor_copy(
-                out=spacing_sorted[:].rearrange("b g u p e -> b (g u p e)").bitcast(F32).rearrange("b (g u p) -> b g u p", g=GM, u=2),
-                in_=spc[:].bitcast(F32).rearrange("b (g p u) -> b g u p", g=GM, u=2),
-            )
+            if i not in ex:
+                ex[i] = work.tile([P, 2, GM, P, 2], F32, name="ex", tag="ex", bufs=4)
+            nc.scalar.activation(out=ex[i][:, :, h], in_=z[i, h][:].rearrange("b (p u e) -> b u p e", u=2, e=2), func=ACT.Exp)
 
         def mul(i, h):
-            mass[i, h] = work.tile([P, 2, P, 2], BF16, name="mass", tag="mass", bufs=8)
+            if i not in mass:
+                mass[i] = work.tile([P, 2, GM, P, 2], BF16, name="mass", tag="mass", bufs=4)
             nc.vector.tensor_tensor(
-                out=mass[i, h][:],
-                in0=ex[i, h][:],
-                in1=spacing_sorted[:, h],
+                out=mass[i][:, :, h],
+                in0=ex[i][:, :, h],
+                in1=spc[:, HALF * h : HALF * (h + 1)].rearrange("b (p u e) -> b u p e", u=2, e=2),
                 op=ALU.mult,
             )
 
-        def mtrans(i, gs=(0, 1)):
-            t = bank(("m", i, gs), [P, 2, len(gs), P])
-            mt[i, gs] = t
-            for n, g in enumerate(gs):
+        def mul_tile(i):
+            mass[i] = work.tile([P, 2, GM, P, 2], BF16, name="mass", tag="mass", bufs=4)
+            nc.vector.tensor_tensor(
+                out=mass[i][:].rearrange("b u g p e -> b u (g p) e"),
+                in0=ex[i][:].rearrange("b u g p e -> b u (g p) e"),
+                in1=spc[:].rearrange("b (q u e) -> b u q e", u=2, e=2),
+                op=ALU.mult,
+            )
+
+        def mtrans(i):
+            t = bank(("m", i), [P, 2, GM, P])
+            mt[i] = t
+            for g in range(GM):
                 for u in range(2):
-                    nc.tensor.transpose(t[:, u, n, :], mass[i, g][:, u].rearrange("b p e -> b (p e)").bitcast(F32), ident[:])
+                    nc.tensor.transpose(t[:, u, g, :], mass[i][:, u, g].rearrange("b p e -> b (p e)").bitcast(F32), ident[:])
 
-        def mexit(i, gs=(0, 1)):
-            emptied(("m", i, gs))
-            mgrp[i, gs] = work.tile([P, len(gs) * P * 4], BF16, name="mgrp", tag="mgrp", bufs=3, align_bytes=64)
+        def mexit(i, tiles):
+            emptied(("m", i))
+            n = tiles.index(i)
+            if n == 0:
+                mgrp[tiles] = work.tile([P, len(tiles) * F], BF16, name="mgrp", tag="mgrp", bufs=2, align_bytes=64)
             nc.scalar.copy(
-                out=mgrp[i, gs][:].bitcast(F32).rearrange("p (g b u) -> p g b u", g=len(gs), u=2),
-                in_=mt[i, gs][:].rearrange("p u g b -> p g b u"),
+                out=mgrp[tiles][:, F * n : F * (n + 1)].bitcast(F32).rearrange("p (g b u) -> p g b u", g=GM, u=2),
+                in_=mt[i][:].rearrange("p u g b -> p g b u"),
             )
 
-        def mquant(i, gs=(0, 1)):
-            cod = work.tile([P, len(gs), P], U32, name="mcod", tag="mcod", bufs=6, align_bytes=64)
-            scl = work.tile([P, len(gs), P], U8, name="mscl", tag="mscl", bufs=6, align_bytes=64)
-            for n, g in enumerate(gs):
-                mcod[i, g], mscl[i, g] = cod[:, n, :], scl[:, n, :]
+        def mquant(tiles):
+            cod = work.tile([P, len(tiles), GM, P], U32, name="mcod", tag="mcod", bufs=3, align_bytes=64)
+            scl = work.tile([P, len(tiles), GM, P], U8, name="mscl", tag="mscl", bufs=3, align_bytes=64)
+            for n, i in enumerate(tiles):
+                mcod[i], mscl[i] = cod[:, n], scl[:, n]
             nc.vector.quantize_mx(
-                out=cod[:].rearrange("p g b -> p (g b)").bitcast(FP8X4),
-                scales=scl[:].rearrange("p g b -> p (g b)"),
-                in_=mgrp[i, gs][:],
-            )
-
-        def tpass(i, h, g):
-            if g == 0:
-                tg[i, h] = bank(("t", i, h), [P, HALF])
-            nc.tensor.matmul_mx(
-                out=tg[i, h][:],
-                lhsT=mcod[i, g].bitcast(FP8X4),
-                lhsT_scale=mscl[i, g],
-                rhs=proj[:, g, 2 * HALF * h : 2 * HALF * (h + 1)].bitcast(FP4X4),
-                rhs_scale=psc[:, g, HALF * h : HALF * (h + 1)],
-                start=(g == 0),
-                stop=(g == GM - 1),
+                out=cod[:].rearrange("p i g b -> p (i g b)").bitcast(FP8X4),
+                scales=scl[:].rearrange("p i g b -> p (i g b)"),
+                in_=mgrp[tiles][:],
             )
 
         def tmat(i, h):
+            tg[i, h] = bank(("t", i, h), [P, HALF])
             for g in range(GM):
-                tpass(i, h, g)
-
-        def loss_half(i, h, from_bank):
-            cols = slice(HALF * h, HALF * (h + 1))
-            prods = work.tile([P, HALF], F32, name="prods", tag="scratch", bufs=2)
-            nc.vector.scalar_tensor_tensor(
-                out=prods[:],
-                in0=tg[i, h][:] if from_bank else tout[i][:, cols],
-                scalar=-1.0 / J,
-                in1=logs[i][:, cols],
-                op0=ALU.mult,
-                op1=ALU.mult,
-                accum_out=parts[h][:, i : i + 1],
-            )
-
-        def loss_add(first):
-            nc.vector.tensor_tensor(out=rowloss[:, first:NT], in0=parts[0][:, first:NT], in1=parts[1][:, first:NT], op=ALU.add)
+                nc.tensor.matmul_mx(
+                    out=tg[i, h][:],
+                    lhsT=mcod[i][:, g, :].bitcast(FP8X4),
+                    lhsT_scale=mscl[i][:, g, :],
+                    rhs=proj[:, g, 2 * HALF * h : 2 * HALF * (h + 1)].bitcast(FP4X4),
+                    rhs_scale=psc[:, g, HALF * h : HALF * (h + 1)],
+                    start=(g == 0),
+                    stop=(g == GM - 1),
+                )
 
         def tcopy(i, h):
             emptied(("t", i, h))
@@ -348,6 +301,7 @@ def tile_c51_shifted_log_loss_s3_kernel(
             nc.scalar.activation(out=junk1[:], in_=one[:], func=ACT.Ln)
             make_identity(nc, ident[:])
             nc.sync.dma_start(out=sc[:], in_=x_rest_scale.rearrange("o (g p t) -> p (o g) t", p=P, t=4))
+            load_w(0)
             load_x(0)
             load_x(1)
             load_onl(0)
@@ -359,43 +313,39 @@ def tile_c51_shifted_log_loss_s3_kernel(
             load_onl(2)
             load_onl(3)
             load_x(3)
-            load_xo(0)
             load_onl(4)
-            load_w(0)
-            load_onl(5)
-            load_xo(1)
             load_w(1)
+            load_onl(5)
             load_onl(6)
-            load_onl(7)
+            load_xo(0)
             load_x(4)
+            load_onl(7)
+            load_xo(1)
             nc.sync.dma_start(out=spc[:], in_=spacing.partition_broadcast(P))
             load_x(5)
-            load_xo(2)
             load_x(6)
             nc.sync.dma_start(out=proj[:], in_=proj_words.rearrange("g p n -> p g n"))
             load_scales(psc, proj_scales)
             load_x(7)
-            load_xo(3)
+            wgroup(0, 256)
             spread(0)
-            spread_exit(0)
             spread(1)
-            spread_exit(1)
             spread(2)
-            spread_exit(2)
             spread(3)
-            spread_exit(3)
-            widen(0, 0)
+            widen(0, 0, 1)
+            widen(0, 1, 2)
             xtrans(0, 0)
             ln(0)
             xexit(0, 0)
-            widen(0, 1)
+            widen(0, 2, 3)
+            widen(0, 3, 4)
             xtrans(0, 1)
             xexit(0, 1)
-            widen(1, 0)
+            widen(1, 0, 2)
             xtrans(1, 0)
             ln(1)
             xexit(1, 0)
-            widen(1, 1)
+            widen(1, 2, 4)
             xtrans(1, 1)
             xexit(1, 1)
             xquant(0)
@@ -407,41 +357,35 @@ def tile_c51_shifted_log_loss_s3_kernel(
                     zpass(0, h, g)
             ln(2)
             ln(3)
-            widen(2, 0)
+            ln(4)
+            widen(2)
             xquant(1)
-            widen(2, 1)
             xtrans(2, 0)
             xtrans(2, 1)
-            otrans(0)
-            ln(4)
             xexit(2, 0)
             xexit(2, 1)
-            oexit(0)
-            widen(3, 0)
-            widen(3, 1)
+            widen(3)
             zrest(1, 0)
             zrest(1, 1)
-            wgroup(0)
+            wgroup(256, 1024)
             xquant(2)
-            oquant(0)
             ln(5)
             ln(6)
             xtrans(3, 0)
             xtrans(3, 1)
+            otrans(0)
             otrans(1)
             xexit(3, 0)
             xexit(3, 1)
+            oexit(0)
             oexit(1)
             ln(7)
-            wgroup(1)
-            wquant(0)
-            wquant(1)
+            wquant()
             zrest(2, 0)
             zrest(2, 1)
             xquant(3)
-            oquant(1)
-            widen(4, 0)
-            widen(4, 1)
+            oquant(0)
+            widen(4)
             zout(0, 0)
             zout(0, 1)
             zout(1, 0)
@@ -457,125 +401,106 @@ def tile_c51_shifted_log_loss_s3_kernel(
             xtrans(4, 0)
             xtrans(4, 1)
             otrans(2)
-            widen(5, 0)
-            widen(5, 1)
+            otrans(3)
+            widen(5)
             xexit(4, 0)
             xexit(4, 1)
             oexit(2)
+            oexit(3)
             exp(2, 0)
             exp(2, 1)
             zrest(3, 1)
             zout(3, 1)
-            sort_spacing()
-            mul(0, 0)
-            mul(0, 1)
+            mul_tile(0)
             xquant(4)
-            oquant(2)
+            oquant(1)
+            mul_tile(1)
             exp(3, 0)
             exp(3, 1)
-            mul(1, 0)
-            mul(1, 1)
             zrest(4, 0)
             zout(4, 0)
-            widen(6, 0)
+            widen(6)
             xtrans(5, 0)
             xtrans(5, 1)
             mtrans(0)
             mtrans(1)
-            mul(2, 0)
-            mul(2, 1)
-            exp(4, 0)
             xexit(5, 0)
             xexit(5, 1)
-            mexit(0)
-            mexit(1)
+            exp(4, 0)
+            mexit(0, (0, 1,))
+            mexit(1, (0, 1,))
             zrest(4, 1)
             zout(4, 1)
-            widen(6, 1)
             xquant(5)
-            mquant(0)
-            mquant(1)
+            mquant((0, 1,))
+            mul_tile(2)
             exp(4, 1)
-            sort_words(6, 0)
-            sort_words(6, 1)
-            mul(3, 0)
-            mul(3, 1)
+            mul_tile(3)
             zrest(5, 0)
             zout(5, 0)
             tmat(0, 0)
             tmat(0, 1)
-            mul(4, 0)
-            mul(4, 1)
-            widen(7, 0)
-            xtrans(6, 0)
-            xtrans(6, 1)
-            otrans(3)
-            mtrans(2)
+            widen(7)
             exp(5, 0)
-            xexit(6, 0)
-            xexit(6, 1)
-            oexit(3)
             tcopy(0, 0)
             tcopy(0, 1)
-            mexit(2)
+            xtrans(6, 0)
+            xtrans(6, 1)
+            mtrans(2)
+            mtrans(3)
+            xexit(6, 0)
+            xexit(6, 1)
+            mexit(2, (2, 3,))
+            mexit(3, (2, 3,))
             zrest(5, 1)
             zout(5, 1)
             tmat(1, 0)
             tmat(1, 1)
-            widen(7, 1)
             xquant(6)
-            oquant(3)
+            mul_tile(4)
+            mquant((2, 3,))
+            lossp(0)
             exp(5, 1)
-            sort_words(7, 0)
-            sort_words(7, 1)
             tcopy(1, 0)
             tcopy(1, 1)
-            mquant(2)
-            mul(5, 0)
-            mul(5, 1)
             zrest(6, 0)
             zout(6, 0)
             tmat(2, 0)
             tmat(2, 1)
-            lossp(0)
-            xtrans(7, 0)
-            xtrans(7, 1)
-            mtrans(3)
-            mtrans(4)
-            mtrans(5)
             exp(6, 0)
-            xexit(7, 0)
-            xexit(7, 1)
             tcopy(2, 0)
             tcopy(2, 1)
-            mexit(3)
+            xtrans(7, 0)
+            xtrans(7, 1)
+            mtrans(4)
+            mul_tile(5)
+            xexit(7, 0)
+            xexit(7, 1)
+            mexit(4, (4, 5,))
             zrest(6, 1)
             zout(6, 1)
-            lossp(1)
-            xquant(7)
-            mul(6, 0)
-            mquant(3)
-            exp(6, 1)
-            mexit(4)
-            mexit(5)
-            mul(6, 1)
-            lossp(2)
-            mquant(4)
-            mquant(5)
-            zrest(7, 0)
-            zout(7, 0)
             tmat(3, 0)
             tmat(3, 1)
-            exp(7, 0)
+            lossp(1)
+            lossp(2)
+            xquant(7)
+            exp(6, 1)
             tcopy(3, 0)
             tcopy(3, 1)
+            mul_tile(6)
+            zrest(7, 0)
+            zout(7, 0)
+            mtrans(5)
             mtrans(6)
-            mexit(6)
+            mexit(5, (4, 5,))
+            exp(7, 0)
+            mexit(6, (6,))
+            lossp(3)
+            mquant((4, 5,))
             zrest(7, 1)
             zout(7, 1)
             mul(7, 0)
-            lossp(3)
-            mquant(6)
+            mquant((6,))
             exp(7, 1)
             tmat(4, 0)
             tmat(4, 1)
@@ -583,11 +508,11 @@ def tile_c51_shifted_log_loss_s3_kernel(
             tcopy(4, 0)
             tcopy(4, 1)
             mtrans(7)
-            mexit(7)
+            mexit(7, (7,))
             tmat(5, 0)
             tmat(5, 1)
             lossp(4)
-            mquant(7)
+            mquant((7,))
             tcopy(5, 0)
             tcopy(5, 1)
             tmat(6, 0)

@@ -18,11 +18,15 @@ ACT = mybir.ActivationFunctionType
 ALU = mybir.AluOpType
 
 P = 128
-NT = B // P
-HALF = 512
-GR = KR // 512
-GM = F // 512
-W_FIRST = 256
+TILES = B // P
+PASS = 512
+BANK = 512
+REST_PASSES = KR // PASS
+MASS_PASSES = F // PASS
+QUAD = 4
+HELD = 3
+SORTED_FROM = HELD + 3
+FIRST_LOG = 128
 
 
 def tile_c51_shifted_log_loss_s3_kernel(
@@ -37,493 +41,416 @@ def tile_c51_shifted_log_loss_s3_kernel(
         def kept(shape, dtype, name):
             return keep.tile(shape, dtype, name=name, tag=name, align_bytes=64)
 
-        xr = [kept([P, KR], U8, "xr%d" % i) for i in range(NT)]
-        sc = kept([P, GR, 4], F32, "sc")
-        scb = kept([P, KR], F32, "scb")
+        x_bytes = [kept([P, KR], U8, "x_bytes%d" % i) for i in range(TILES)]
+        k_scale = kept([P, REST_PASSES, 4], F32, "k_scale")
+        k_scale_rows = kept([P, KR], F32, "k_scale_rows")
         base = [kept([P, 2, 2 * F], U8, "base%d" % b) for b in range(2)]
-        bsc = kept([P, GR, F], U8, "bsc")
-        proj = kept([P, GM, 2 * J], U8, "proj")
-        psc = kept([P, GM, J], U8, "psc")
-        w_cols = [(0, W_FIRST), (W_FIRST, F)]
-        wraw = [work.tile([P, 4, c1 - c0], BF16, name="wraw%d" % n, tag="scratch", bufs=2) for n, (c0, c1) in enumerate(w_cols)]
-        wgrp = kept([P, F, 4], BF16, "wgrp")
-        wcod = kept([P, F], U32, "wcod")
-        wscl = kept([P, F], U8, "wscl")
-        xo = [kept([P, 4, KO], BF16, "xo%d" % a) for a in range(2)]
-        onl = [kept([P, J], BF16, "onl%d" % i) for i in range(NT)]
-        logs = [kept([P, J], F32, "logs%d" % i) for i in range(NT)]
-        spc = kept([P, F], BF16, "spc")
+        base_sc = kept([P, REST_PASSES, F], U8, "base_sc")
+        proj = kept([P, MASS_PASSES, 2 * J], U8, "proj")
+        proj_sc = kept([P, MASS_PASSES, J], U8, "proj_sc")
+        w_rows = kept([P, 4, F], BF16, "w_rows")
+        w_groups = kept([P, F, 4], BF16, "w_groups")
+        w_codes = kept([P, F], U32, "w_codes")
+        w_sc = kept([P, F], U8, "w_sc")
+        xo = [kept([P, QUAD, KO], BF16, "xo%d" % a) for a in range(TILES // QUAD)]
+        onl = [kept([P, J], BF16, "onl%d" % i) for i in range(TILES)]
+        logs = [kept([P, J], F32, "logs%d" % i) for i in range(TILES)]
+        spacing_rows = kept([P, F], BF16, "spacing_rows")
         ident = kept([P, P], F32, "ident")
-        rowloss = kept([P, NT], F32, "rowloss")
-        one = kept([P, 1], F32, "one")
-        junk1 = kept([P, 1], F32, "junk1")
-        xcod = [kept([P, GR, P], U32, "xcod%d" % i) for i in range(NT)]
-        xscl = [kept([P, GR, P], U8, "xscl%d" % i) for i in range(NT)]
-        ocod = [kept([P, 4, P], U32, "ocod%d" % a) for a in range(2)]
-        oscl = [kept([P, 4, P], U8, "oscl%d" % a) for a in range(2)]
+        row_loss = kept([P, TILES], F32, "row_loss")
+        x_codes = [kept([P, REST_PASSES, P], U32, "x_codes%d" % i) for i in range(TILES)]
+        x_sc = [kept([P, REST_PASSES, P], U8, "x_sc%d" % i) for i in range(TILES)]
+        xo_codes = [kept([P, QUAD, P], U32, "xo_codes%d" % a) for a in range(TILES // QUAD)]
+        xo_sc = [kept([P, QUAD, P], U8, "xo_sc%d" % a) for a in range(TILES // QUAD)]
 
-        x_rows = x_rest_bytes.rearrange("(r i) k -> r i k", i=NT)
-        xo_rows = x_out.rearrange("(r i) k -> r i k", i=NT)
-        onl_rows = online.rearrange("(r i) j -> r i j", i=NT)
-        tgt_rows = target.rearrange("(r i) j -> r i j", i=NT)
+        x_hbm = x_rest_bytes.rearrange("(r i) k -> r i k", i=TILES)
+        xo_hbm = x_out.rearrange("(r i) k -> r i k", i=TILES)
+        online_hbm = online.rearrange("(r i) j -> r i j", i=TILES)
+        target_hbm = target.rearrange("(r i) j -> r i j", i=TILES)
 
-        wide, xt, grp, z, ex, mass, mt, mgrp, mcod, mscl, tg, tout = {}, {}, {}, {}, {}, {}, {}, {}, {}, {}, {}, {}
-        sorted_x = {}
-        free = list(range(8))
-        owner = {}
+        scaled, sorted_pairs, groups, exps, mass, mass_codes, mass_sc, target_sb = {}, {}, {}, {}, {}, {}, {}, {}
 
-        def bank(key, shape):
-            n = free[0]
-            free.remove(n)
-            owner[key] = n
-            return psum.tile(shape, F32, name="bank%d" % n, tag="bank%d" % n, bufs=1)
+        free_banks = list(range(8))
+        bank_of, banks = {}, {}
 
-        def emptied(key):
-            free.append(owner[key])
+        def take_bank(key, shape):
+            n = free_banks[0]
+            free_banks.remove(n)
+            bank_of[key] = n
+            banks[key] = psum.tile(shape, F32, name="bank%d" % n, tag="bank%d" % n, bufs=1)
+            return banks[key]
+
+        def give_back(key):
+            free_banks.append(bank_of[key])
+            return banks[key]
 
         def load_x(i):
-            nc.sync.dma_start(out=xr[i][:], in_=x_rows[:, i, :])
+            nc.sync.dma_start(out=x_bytes[i][:], in_=x_hbm[:, i, :])
 
-        def load_onl(i):
-            nc.sync.dma_start(out=onl[i][:], in_=onl_rows[:, i, :])
+        def load_online(i, cols=slice(0, J)):
+            nc.sync.dma_start(out=onl[i][:, cols], in_=online_hbm[:, i, cols])
 
         def load_xo(a):
-            nc.sync.dma_start(out=xo[a][:], in_=xo_rows[:, 4 * a : 4 * a + 4, :])
-
-        def load_w(n):
-            nc.sync.dma_start(out=wraw[n][:], in_=w_out.rearrange("(p j) n -> p j n", j=4)[:, :, w_cols[n][0] : w_cols[n][1]])
+            nc.sync.dma_start(out=xo[a][:], in_=xo_hbm[:, QUAD * a : QUAD * (a + 1), :])
 
         def load_base(b):
             nc.sync.dma_start(out=base[b][:], in_=base_words.rearrange("g p n -> p g n")[:, 2 * b : 2 * b + 2, :])
 
-        def load_scales(plane, rows):
+        def load_scale_bytes(tile, rows):
             for q in range(4):
                 nc.sync.dma_start(
-                    out=plane[32 * q : 32 * q + 4].bitcast(I32),
+                    out=tile[32 * q : 32 * q + 4].bitcast(I32),
                     in_=rows[:, 4 * q : 4 * q + 4, :].rearrange("g r n -> r g n").bitcast(I32),
                 )
 
-        def spread(g):
-            t = bank(("s", g), [P, 4, P])
-            for j in range(4):
-                nc.tensor.transpose(t[:, j, :], sc[:, g, j : j + 1].to_broadcast([P, P]), ident[:])
-            nc.scalar.copy(out=scb[:, HALF * g : HALF * (g + 1)].rearrange("b (p j) -> b p j", j=4), in_=t[:].rearrange("b j p -> b p j"))
-            emptied(("s", g))
+        def log(i, cols=slice(0, J)):
+            nc.scalar.activation(out=logs[i][:, cols], in_=onl[i][:, cols], func=ACT.Ln)
 
-        def widen(i, g0=0, g1=GR):
-            if i not in wide:
-                wide[i] = work.tile([P, KR], BF16, name="wide", tag="wide", bufs=3)
-            cols = slice(HALF * g0, HALF * g1)
-            nc.vector.tensor_tensor(out=wide[i][:, cols], in0=xr[i][:, cols].bitcast(FP8), in1=scb[:, cols], op=ALU.mult)
+        def spread_scale(g):
+            bank = take_bank(("scale", g), [P, 4, P])
+            for t in range(4):
+                nc.tensor.transpose(bank[:, t, :], k_scale[:, g, t : t + 1].to_broadcast([P, P]), ident[:])
+            nc.scalar.copy(
+                out=k_scale_rows[:, PASS * g : PASS * (g + 1)].rearrange("r (p t) -> r p t", t=4),
+                in_=give_back(("scale", g))[:].rearrange("r t p -> r p t"),
+            )
 
-        def xtrans(i, b):
-            t = bank(("x", i, b), [P, 2, 2, P])
-            xt[i, b] = t
-            words = wide[i][:].bitcast(F32)
+        def scale_x(i, g0=0, g1=REST_PASSES):
+            if g0 == 0:
+                scaled[i] = work.tile([P, KR], BF16, name="scaled", tag="wide", bufs=3)
+            cols = slice(PASS * g0, PASS * g1)
+            nc.vector.tensor_tensor(out=scaled[i][:, cols], in0=x_bytes[i][:, cols].bitcast(FP8), in1=k_scale_rows[:, cols], op=ALU.mult)
+
+        def sort_x(i):
+            for b in range(2):
+                sorted_pairs[i, b] = work.tile([P, 2, 2, P], F32, name="sorted", tag="sorted", bufs=2)
+                nc.scalar.copy(
+                    out=sorted_pairs[i, b][:].rearrange("r g u p -> r g p u"),
+                    in_=scaled[i][:, 2 * PASS * b : 2 * PASS * (b + 1)].bitcast(F32).rearrange("r (g p u) -> r g p u", g=2, u=2),
+                )
+
+        def turn_x(i, b):
+            bank = take_bank(("x", i, b), [P, 2, 2, P])
+            pairs = scaled[i][:].bitcast(F32)
             for gg in range(2):
-                g = 2 * b + gg
+                first = (PASS // 2) * (2 * b + gg)
                 for u in range(2):
-                    src = sorted_x[i, b][:, gg, u, :] if (i, b) in sorted_x else words[:, 256 * g + u : 256 * (g + 1) : 2]
-                    nc.tensor.transpose(t[:, u, gg, :], src, ident[:])
+                    src = sorted_pairs[i, b][:, gg, u, :] if i >= SORTED_FROM else pairs[:, first + u : first + PASS // 2 : 2]
+                    nc.tensor.transpose(bank[:, u, gg, :], src, ident[:])
 
-        def xexit(i, b):
-            if i not in grp:
-                grp[i] = work.tile([P, GR * P * 4], BF16, name="grp", tag="grp", bufs=3, align_bytes=64)
-            emptied(("x", i, b))
+        def leave_bank(key, into, n, parts):
+            if n == 0:
+                groups[into] = work.tile([P, parts * 2 * PASS], BF16, name="groups", tag="groups", bufs=3, align_bytes=64)
             nc.scalar.copy(
-                out=grp[i][:, 2 * HALF * b : 2 * HALF * (b + 1)].bitcast(F32).rearrange("p (g r u) -> p g r u", g=2, u=2),
-                in_=xt[i, b][:].rearrange("p u g r -> p g r u"),
+                out=groups[into][:, 2 * PASS * n : 2 * PASS * (n + 1)].bitcast(F32).rearrange("p (c r u) -> p c r u", c=2, u=2),
+                in_=give_back(key)[:].rearrange("p u c r -> p c r u"),
             )
 
-        def xquant(i):
+        def leave_x(i, b):
+            leave_bank(("x", i, b), ("x", i), b, 2)
+
+        def quantise_x(i, g0=0, g1=REST_PASSES):
             nc.vector.quantize_mx(
-                out=xcod[i][:].rearrange("p g r -> p (g r)").bitcast(FP8X4),
-                scales=xscl[i][:].rearrange("p g r -> p (g r)"),
-                in_=grp[i][:],
+                out=x_codes[i][:, g0:g1].rearrange("p g r -> p (g r)").bitcast(FP8X4),
+                scales=x_sc[i][:, g0:g1].rearrange("p g r -> p (g r)"),
+                in_=groups["x", i][:, PASS * g0 : PASS * g1],
             )
 
-        def otrans(a):
-            t = bank(("o", a), [P, 2, 2, P])
-            xt["o", a] = t
-            for i in range(2):
-                words = xo[a // 2][:, 2 * (a % 2) + i, :].bitcast(F32)
+        def turn_xo(a, b):
+            bank = take_bank(("xo", a, b), [P, 2, 2, P])
+            for c in range(2):
+                pairs = xo[a][:, 2 * b + c, :].bitcast(F32)
                 for u in range(2):
-                    nc.tensor.transpose(t[:, u, i, :], words[:, u::2], ident[:])
+                    nc.tensor.transpose(bank[:, u, c, :], pairs[:, u::2], ident[:])
 
-        def oexit(a):
-            emptied(("o", a))
-            if a % 2 == 0:
-                grp["o", a // 2] = work.tile([P, 4 * P * 4], BF16, name="grp", tag="grp", bufs=3, align_bytes=64)
-            nc.scalar.copy(
-                out=grp["o", a // 2][:, 2 * HALF * (a % 2) : 2 * HALF * (a % 2 + 1)].bitcast(F32).rearrange("p (i r u) -> p i r u", i=2, u=2),
-                in_=xt["o", a][:].rearrange("p u i r -> p i r u"),
-            )
+        def leave_xo(a, b):
+            leave_bank(("xo", a, b), ("xo", a), b, 2)
 
-        def oquant(a):
+        def quantise_xo(a):
             nc.vector.quantize_mx(
-                out=ocod[a][:].rearrange("p i r -> p (i r)").bitcast(FP8X4),
-                scales=oscl[a][:].rearrange("p i r -> p (i r)"),
-                in_=grp["o", a][:],
+                out=xo_codes[a][:].rearrange("p i r -> p (i r)").bitcast(FP8X4),
+                scales=xo_sc[a][:].rearrange("p i r -> p (i r)"),
+                in_=groups["xo", a][:],
             )
 
-        def wgroup(c0, c1, on_scalar=False):
-            n = 0 if c1 <= W_FIRST else 1
-            src = wraw[n][:, :, c0 - w_cols[n][0] : c1 - w_cols[n][0]].rearrange("p j n -> p n j")
-            if on_scalar:
-                nc.scalar.copy(out=wgrp[:, c0:c1], in_=src)
-            else:
-                nc.vector.tensor_copy(out=wgrp[:, c0:c1], in_=src)
-
-        def wquant():
-            nc.vector.quantize_mx(out=wcod[:].bitcast(FP8X4), scales=wscl[:], in_=wgrp[:].rearrange("p n j -> p (n j)"))
-
-        def zpass(i, h, g):
+        def rest_pass(i, h, g):
             if g == 0:
-                z[i, h] = bank(("z", i, h), [P, HALF])
+                take_bank(("logits", i, h), [P, BANK])
             nc.tensor.matmul_mx(
-                out=z[i, h][:],
-                lhsT=xcod[i][:, g, :].bitcast(FP8X4),
-                lhsT_scale=xscl[i][:, g, :],
-                rhs=base[g // 2][:, g % 2, F * h : F * (h + 1)].bitcast(FP4X4),
-                rhs_scale=bsc[:, g, HALF * h : HALF * (h + 1)],
+                out=banks["logits", i, h][:],
+                lhsT=x_codes[i][:, g, :].bitcast(FP8X4),
+                lhsT_scale=x_sc[i][:, g, :],
+                rhs=base[g // 2][:, g % 2, 2 * BANK * h : 2 * BANK * (h + 1)].bitcast(FP4X4),
+                rhs_scale=base_sc[:, g, BANK * h : BANK * (h + 1)],
                 start=(g == 0),
                 stop=False,
             )
 
-        def zrest(i, h):
-            for g in range(GR):
-                zpass(i, h, g)
+        def rest_passes(i, h):
+            for g in range(REST_PASSES):
+                rest_pass(i, h, g)
 
-        def zout(i, h):
+        def out_pass(i, h):
             nc.tensor.matmul_mx(
-                out=z[i, h][:],
-                lhsT=ocod[i // 4][:, i % 4, :].bitcast(FP8X4),
-                lhsT_scale=oscl[i // 4][:, i % 4, :],
-                rhs=wcod[:, HALF * h : HALF * (h + 1)].bitcast(FP8X4),
-                rhs_scale=wscl[:, HALF * h : HALF * (h + 1)],
+                out=banks["logits", i, h][:],
+                lhsT=xo_codes[i // QUAD][:, i % QUAD, :].bitcast(FP8X4),
+                lhsT_scale=xo_sc[i // QUAD][:, i % QUAD, :],
+                rhs=w_codes[:, BANK * h : BANK * (h + 1)].bitcast(FP8X4),
+                rhs_scale=w_sc[:, BANK * h : BANK * (h + 1)],
                 start=False,
                 stop=True,
             )
 
+        def logits(i, h):
+            rest_passes(i, h)
+            out_pass(i, h)
+
         def exp(i, h):
-            emptied(("z", i, h))
-            if i not in ex:
-                ex[i] = work.tile([P, 2, GM, P, 2], F32, name="ex", tag="ex", bufs=4)
-            nc.scalar.activation(out=ex[i][:, :, h], in_=z[i, h][:].rearrange("b (p u e) -> b u p e", u=2, e=2), func=ACT.Exp)
+            if h == 0:
+                exps[i] = work.tile([P, 2, MASS_PASSES, P, 2], F32, name="exps", tag="exps", bufs=HELD + 1)
+            nc.scalar.activation(
+                out=exps[i][:, :, h], in_=give_back(("logits", i, h))[:].rearrange("r (p u e) -> r u p e", u=2, e=2), func=ACT.Exp
+            )
 
-        def mul(i, h):
-            if i not in mass:
-                mass[i] = work.tile([P, 2, GM, P, 2], BF16, name="mass", tag="mass", bufs=4)
+        def weigh(i, h0=0, h1=MASS_PASSES):
+            if h0 == 0:
+                mass[i] = work.tile([P, 2, MASS_PASSES, P, 2], BF16, name="mass", tag="mass", bufs=HELD + 1)
             nc.vector.tensor_tensor(
-                out=mass[i][:, :, h],
-                in0=ex[i][:, :, h],
-                in1=spc[:, HALF * h : HALF * (h + 1)].rearrange("b (p u e) -> b u p e", u=2, e=2),
+                out=mass[i][:, :, h0:h1].rearrange("r u g p e -> r u (g p) e"),
+                in0=exps[i][:, :, h0:h1].rearrange("r u g p e -> r u (g p) e"),
+                in1=spacing_rows[:, PASS * h0 : PASS * h1].rearrange("r (gp u e) -> r u gp e", u=2, e=2),
                 op=ALU.mult,
             )
 
-        def mul_tile(i):
-            mass[i] = work.tile([P, 2, GM, P, 2], BF16, name="mass", tag="mass", bufs=4)
-            nc.vector.tensor_tensor(
-                out=mass[i][:].rearrange("b u g p e -> b u (g p) e"),
-                in0=ex[i][:].rearrange("b u g p e -> b u (g p) e"),
-                in1=spc[:].rearrange("b (q u e) -> b u q e", u=2, e=2),
-                op=ALU.mult,
-            )
-
-        def mtrans(i):
-            t = bank(("m", i), [P, 2, GM, P])
-            mt[i] = t
-            for g in range(GM):
+        def turn_mass(i):
+            bank = take_bank(("mass", i), [P, 2, MASS_PASSES, P])
+            for g in range(MASS_PASSES):
                 for u in range(2):
-                    nc.tensor.transpose(t[:, u, g, :], mass[i][:, u, g].rearrange("b p e -> b (p e)").bitcast(F32), ident[:])
+                    nc.tensor.transpose(bank[:, u, g, :], mass[i][:, u, g].rearrange("r p e -> r (p e)").bitcast(F32), ident[:])
 
-        def mexit(i, tiles):
-            emptied(("m", i))
-            n = tiles.index(i)
-            if n == 0:
-                mgrp[tiles] = work.tile([P, len(tiles) * F], BF16, name="mgrp", tag="mgrp", bufs=2, align_bytes=64)
-            nc.scalar.copy(
-                out=mgrp[tiles][:, F * n : F * (n + 1)].bitcast(F32).rearrange("p (g b u) -> p g b u", g=GM, u=2),
-                in_=mt[i][:].rearrange("p u g b -> p g b u"),
-            )
-
-        def mquant(tiles):
-            cod = work.tile([P, len(tiles), GM, P], U32, name="mcod", tag="mcod", bufs=3, align_bytes=64)
-            scl = work.tile([P, len(tiles), GM, P], U8, name="mscl", tag="mscl", bufs=3, align_bytes=64)
+        def leave_mass(tiles):
             for n, i in enumerate(tiles):
-                mcod[i], mscl[i] = cod[:, n], scl[:, n]
+                leave_bank(("mass", i), ("mass", tiles), n, len(tiles))
+
+        def quantise_mass(tiles):
+            codes = work.tile([P, len(tiles), MASS_PASSES, P], U32, name="mass_codes", tag="mass_codes", bufs=3, align_bytes=64)
+            scales = work.tile([P, len(tiles), MASS_PASSES, P], U8, name="mass_sc", tag="mass_sc", bufs=3, align_bytes=64)
+            for n, i in enumerate(tiles):
+                mass_codes[i], mass_sc[i] = codes[:, n], scales[:, n]
             nc.vector.quantize_mx(
-                out=cod[:].rearrange("p i g b -> p (i g b)").bitcast(FP8X4),
-                scales=scl[:].rearrange("p i g b -> p (i g b)"),
-                in_=mgrp[tiles][:],
+                out=codes[:].rearrange("p i g r -> p (i g r)").bitcast(FP8X4),
+                scales=scales[:].rearrange("p i g r -> p (i g r)"),
+                in_=groups["mass", tiles][:],
             )
 
-        def tmat(i, h):
-            tg[i, h] = bank(("t", i, h), [P, HALF])
-            for g in range(GM):
-                nc.tensor.matmul_mx(
-                    out=tg[i, h][:],
-                    lhsT=mcod[i][:, g, :].bitcast(FP8X4),
-                    lhsT_scale=mscl[i][:, g, :],
-                    rhs=proj[:, g, 2 * HALF * h : 2 * HALF * (h + 1)].bitcast(FP4X4),
-                    rhs_scale=psc[:, g, HALF * h : HALF * (h + 1)],
-                    start=(g == 0),
-                    stop=(g == GM - 1),
-                )
+        def project(i):
+            for h in range(2):
+                bank = take_bank(("target", i, h), [P, BANK])
+                for g in range(MASS_PASSES):
+                    nc.tensor.matmul_mx(
+                        out=bank[:],
+                        lhsT=mass_codes[i][:, g, :].bitcast(FP8X4),
+                        lhsT_scale=mass_sc[i][:, g, :],
+                        rhs=proj[:, g, 2 * BANK * h : 2 * BANK * (h + 1)].bitcast(FP4X4),
+                        rhs_scale=proj_sc[:, g, BANK * h : BANK * (h + 1)],
+                        start=(g == 0),
+                        stop=(g == MASS_PASSES - 1),
+                    )
 
-        def tcopy(i, h):
-            emptied(("t", i, h))
-            if i not in tout:
-                tout[i] = work.tile([P, J], F32, name="tout", tag="tout", bufs=4)
-            cols = slice(HALF * h, HALF * (h + 1))
-            nc.scalar.copy(out=tout[i][:, cols], in_=tg[i, h][:])
-            nc.sync.dma_start(out=tgt_rows[:, i, cols], in_=tout[i][:, cols])
+        def store_target(i):
+            target_sb[i] = work.tile([P, J], F32, name="target_sb", tag="target_sb", bufs=4)
+            for h in range(2):
+                cols = slice(BANK * h, BANK * (h + 1))
+                nc.scalar.copy(out=target_sb[i][:, cols], in_=give_back(("target", i, h))[:])
+                nc.sync.dma_start(out=target_hbm[:, i, cols], in_=target_sb[i][:, cols])
 
-        def lossp(i):
-            prods = work.tile([P, J], F32, name="prods", tag="scratch", bufs=2)
+        def reduce_loss(i):
+            products = work.tile([P, J], F32, name="products", tag="wide", bufs=3)
             nc.vector.scalar_tensor_tensor(
-                out=prods[:],
-                in0=tout[i][:],
+                out=products[:],
+                in0=target_sb[i][:],
                 scalar=-1.0 / J,
                 in1=logs[i][:],
                 op0=ALU.mult,
                 op1=ALU.mult,
-                accum_out=rowloss[:, i : i + 1],
+                accum_out=row_loss[:, i : i + 1],
             )
 
-        def ln(i):
-            nc.scalar.activation(out=logs[i][:], in_=onl[i][:], func=ACT.Ln)
-
         with tc.manual_schedule():
-            nc.vector.memset(one[:], 1.0)
-            nc.vector.memset(bsc[:].rearrange("p g n -> p (g n)").bitcast(I32), 0)
-            nc.vector.memset(psc[:].rearrange("p g n -> p (g n)").bitcast(I32), 0)
-            nc.scalar.activation(out=junk1[:], in_=one[:], func=ACT.Ln)
+            nc.vector.memset(base_sc[:].rearrange("p g n -> p (g n)").bitcast(I32), 0)
+            nc.vector.memset(proj_sc[:].rearrange("p g n -> p (g n)").bitcast(I32), 0)
             make_identity(nc, ident[:])
-            nc.sync.dma_start(out=sc[:], in_=x_rest_scale.rearrange("o (g p t) -> p (o g) t", p=P, t=4))
-            load_w(0)
+
+            nc.sync.dma_start(out=k_scale[:], in_=x_rest_scale.rearrange("o (g p t) -> p (o g) t", p=P, t=4))
+            load_online(0, slice(0, FIRST_LOG))
             load_x(0)
             load_x(1)
-            load_onl(0)
+            load_xo(0)
             load_base(0)
-            load_scales(bsc, base_scales)
-            load_onl(1)
+            load_scale_bytes(base_sc, base_scales)
+            load_online(0, slice(FIRST_LOG, J))
             load_x(2)
             load_base(1)
-            load_onl(2)
-            load_onl(3)
+            load_online(1)
+            load_online(2)
             load_x(3)
-            load_onl(4)
-            load_w(1)
-            load_onl(5)
-            load_onl(6)
-            load_xo(0)
+            load_online(3)
+            load_online(4)
+            nc.sync.dma_start(out=w_rows[:], in_=w_out.rearrange("(p t) n -> p t n", t=4))
+            for i in range(5, TILES):
+                load_online(i)
             load_x(4)
-            load_onl(7)
             load_xo(1)
-            nc.sync.dma_start(out=spc[:], in_=spacing.partition_broadcast(P))
+            nc.sync.dma_start(out=spacing_rows[:], in_=spacing.partition_broadcast(P))
             load_x(5)
             load_x(6)
             nc.sync.dma_start(out=proj[:], in_=proj_words.rearrange("g p n -> p g n"))
-            load_scales(psc, proj_scales)
+            load_scale_bytes(proj_sc, proj_scales)
             load_x(7)
-            wgroup(0, 256)
-            spread(0)
-            spread(1)
-            spread(2)
-            spread(3)
-            widen(0, 0, 1)
-            widen(0, 1, 2)
-            xtrans(0, 0)
-            ln(0)
-            xexit(0, 0)
-            widen(0, 2, 3)
-            widen(0, 3, 4)
-            xtrans(0, 1)
-            xexit(0, 1)
-            widen(1, 0, 2)
-            xtrans(1, 0)
-            ln(1)
-            xexit(1, 0)
-            widen(1, 2, 4)
-            xtrans(1, 1)
-            xexit(1, 1)
-            xquant(0)
-            for g in (0, 1):
+
+            log(0, slice(0, FIRST_LOG))
+            for g in range(REST_PASSES):
+                spread_scale(g)
+
+            for b in range(2):
+                scale_x(0, 2 * b, 2 * b + 1)
+                scale_x(0, 2 * b + 1, 2 * b + 2)
+                turn_x(0, b)
+                leave_x(0, b)
+                turn_xo(0, b)
+                leave_xo(0, b)
+
+            scale_x(1, 0, 2)
+            quantise_x(0, 0, 2)
+            turn_x(1, 0)
+            leave_x(1, 0)
+            scale_x(1, 2, 4)
+            quantise_x(0, 2, 4)
+            for b in range(2):
+                for g in (2 * b, 2 * b + 1):
+                    for h in range(2):
+                        rest_pass(0, h, g)
+                if b == 0:
+                    log(0, slice(FIRST_LOG, J))
+                    log(1)
+                    turn_x(1, 1)
+                    leave_x(1, 1)
+            scale_x(2)
+            quantise_xo(0)
+            log(2)
+
+            for b in range(2):
+                turn_x(2, b)
+            scale_x(3, 0, 2)
+            quantise_x(1)
+            scale_x(3, 2, 4)
+            for b in range(2):
+                leave_x(2, b)
+            for h in range(2):
+                rest_passes(1, h)
+            quantise_x(2)
+            nc.vector.tensor_copy(out=w_groups[:], in_=w_rows[:].rearrange("p t n -> p n t"))
+            for i in (3, 4, 5):
+                log(i)
+
+            for b in range(2):
+                turn_x(3, b)
+            for b in range(2):
+                leave_x(3, b)
+            for i in (6, 7):
+                log(i)
+            nc.vector.quantize_mx(out=w_codes[:].bitcast(FP8X4), scales=w_sc[:], in_=w_groups[:].rearrange("p n t -> p (n t)"))
+            for h in range(2):
+                rest_passes(2, h)
+            quantise_x(3)
+            scale_x(4)
+            for i in range(HELD):
                 for h in range(2):
-                    zpass(0, h, g)
-            for g in (2, 3):
+                    out_pass(i, h)
+
+            logits(HELD, 0)
+            for i in range(HELD - 1):
                 for h in range(2):
-                    zpass(0, h, g)
-            ln(2)
-            ln(3)
-            ln(4)
-            widen(2)
-            xquant(1)
-            xtrans(2, 0)
-            xtrans(2, 1)
-            xexit(2, 0)
-            xexit(2, 1)
-            widen(3)
-            zrest(1, 0)
-            zrest(1, 1)
-            wgroup(256, 1024)
-            xquant(2)
-            ln(5)
-            ln(6)
-            xtrans(3, 0)
-            xtrans(3, 1)
-            otrans(0)
-            otrans(1)
-            xexit(3, 0)
-            xexit(3, 1)
-            oexit(0)
-            oexit(1)
-            ln(7)
-            wquant()
-            zrest(2, 0)
-            zrest(2, 1)
-            xquant(3)
-            oquant(0)
-            widen(4)
-            zout(0, 0)
-            zout(0, 1)
-            zout(1, 0)
-            zout(1, 1)
-            zout(2, 0)
-            zout(2, 1)
-            zrest(3, 0)
-            zout(3, 0)
-            exp(0, 0)
-            exp(0, 1)
-            exp(1, 0)
-            exp(1, 1)
-            xtrans(4, 0)
-            xtrans(4, 1)
-            otrans(2)
-            otrans(3)
-            widen(5)
-            xexit(4, 0)
-            xexit(4, 1)
-            oexit(2)
-            oexit(3)
-            exp(2, 0)
-            exp(2, 1)
-            zrest(3, 1)
-            zout(3, 1)
-            mul_tile(0)
-            xquant(4)
-            oquant(1)
-            mul_tile(1)
-            exp(3, 0)
-            exp(3, 1)
-            zrest(4, 0)
-            zout(4, 0)
-            widen(6)
-            xtrans(5, 0)
-            xtrans(5, 1)
-            mtrans(0)
-            mtrans(1)
-            xexit(5, 0)
-            xexit(5, 1)
-            exp(4, 0)
-            mexit(0, (0, 1,))
-            mexit(1, (0, 1,))
-            zrest(4, 1)
-            zout(4, 1)
-            xquant(5)
-            mquant((0, 1,))
-            mul_tile(2)
-            exp(4, 1)
-            mul_tile(3)
-            zrest(5, 0)
-            zout(5, 0)
-            tmat(0, 0)
-            tmat(0, 1)
-            widen(7)
-            exp(5, 0)
-            tcopy(0, 0)
-            tcopy(0, 1)
-            xtrans(6, 0)
-            xtrans(6, 1)
-            mtrans(2)
-            mtrans(3)
-            xexit(6, 0)
-            xexit(6, 1)
-            mexit(2, (2, 3,))
-            mexit(3, (2, 3,))
-            zrest(5, 1)
-            zout(5, 1)
-            tmat(1, 0)
-            tmat(1, 1)
-            xquant(6)
-            mul_tile(4)
-            mquant((2, 3,))
-            lossp(0)
-            exp(5, 1)
-            tcopy(1, 0)
-            tcopy(1, 1)
-            zrest(6, 0)
-            zout(6, 0)
-            tmat(2, 0)
-            tmat(2, 1)
-            exp(6, 0)
-            tcopy(2, 0)
-            tcopy(2, 1)
-            xtrans(7, 0)
-            xtrans(7, 1)
-            mtrans(4)
-            mul_tile(5)
-            xexit(7, 0)
-            xexit(7, 1)
-            mexit(4, (4, 5,))
-            zrest(6, 1)
-            zout(6, 1)
-            tmat(3, 0)
-            tmat(3, 1)
-            lossp(1)
-            lossp(2)
-            xquant(7)
-            exp(6, 1)
-            tcopy(3, 0)
-            tcopy(3, 1)
-            mul_tile(6)
-            zrest(7, 0)
-            zout(7, 0)
-            mtrans(5)
-            mtrans(6)
-            mexit(5, (4, 5,))
-            exp(7, 0)
-            mexit(6, (6,))
-            lossp(3)
-            mquant((4, 5,))
-            zrest(7, 1)
-            zout(7, 1)
-            mul(7, 0)
-            mquant((6,))
-            exp(7, 1)
-            tmat(4, 0)
-            tmat(4, 1)
-            mul(7, 1)
-            tcopy(4, 0)
-            tcopy(4, 1)
-            mtrans(7)
-            mexit(7, (7,))
-            tmat(5, 0)
-            tmat(5, 1)
-            lossp(4)
-            mquant((7,))
-            tcopy(5, 0)
-            tcopy(5, 1)
-            tmat(6, 0)
-            tmat(6, 1)
-            tcopy(6, 0)
-            tcopy(6, 1)
-            tmat(7, 0)
-            tmat(7, 1)
-            lossp(5)
-            tcopy(7, 0)
-            tcopy(7, 1)
-            lossp(6)
-            lossp(7)
-            nc.sync.dma_start(out=loss.rearrange("(r i) -> r i", i=NT), in_=rowloss[:])
+                    exp(i, h)
+            for b in range(2):
+                turn_x(HELD + 1, b)
+            for b in range(2):
+                turn_xo(1, b)
+            scale_x(HELD + 2)
+            for b in range(2):
+                leave_x(HELD + 1, b)
+            for b in range(2):
+                leave_xo(1, b)
+            for h in range(2):
+                exp(HELD - 1, h)
+            logits(HELD, 1)
+            weigh(0)
+            quantise_x(HELD + 1)
+            quantise_xo(1)
+            weigh(1)
+            for h in range(2):
+                exp(HELD, h)
+
+            turned, stored = (), ()
+            for r in range(HELD + 1, TILES - 1):
+                ready, turned = turned, (2 * (r - HELD - 1), 2 * (r - HELD - 1) + 1)
+                logits(r, 0)
+                if ready:
+                    project(ready[0])
+                    weigh(r - 1)
+                if r + 2 < TILES:
+                    scale_x(r + 2)
+                for i in stored:
+                    reduce_loss(i)
+                exp(r, 0)
+                if ready:
+                    store_target(ready[0])
+                for b in range(2):
+                    turn_x(r + 1, b)
+                for i in turned:
+                    turn_mass(i)
+                for b in range(2):
+                    leave_x(r + 1, b)
+                leave_mass(turned)
+                logits(r, 1)
+                if ready:
+                    project(ready[1])
+                quantise_x(r + 1)
+                quantise_mass(turned)
+                if not ready:
+                    weigh(HELD - 1)
+                    weigh(HELD)
+                exp(r, 1)
+                if r + 2 < TILES:
+                    sort_x(r + 2)
+                if ready:
+                    store_target(ready[1])
+                stored = ready
+
+            last = TILES - 1
+            logits(last, 0)
+            weigh(last - 1)
+            for i in stored:
+                reduce_loss(i)
+            exp(last, 0)
+            turn_mass(last - 1)
+            leave_mass((last - 1,))
+            logits(last, 1)
+            weigh(last, 0, 1)
+            quantise_mass((last - 1,))
+            exp(last, 1)
+            project(turned[0])
+            weigh(last, 1, 2)
+            store_target(turned[0])
+            turn_mass(last)
+            leave_mass((last,))
+            project(turned[1])
+            reduce_loss(turned[0])
+            quantise_mass((last,))
+            store_target(turned[1])
+            for i in (last - 1, last):
+                project(i)
+                store_target(i)
+            for i in (turned[1], last - 1, last):
+                reduce_loss(i)
+            nc.sync.dma_start(out=loss.rearrange("(r i) -> r i", i=TILES), in_=row_loss[:])

@@ -26,7 +26,8 @@ MASS_PASSES = F // PASS
 QUAD = 4
 HELD = 3
 SORTED_FROM = HELD + 3
-FIRST_LOG = 128
+SPLIT_FROM = 5
+FIRST_LOG = 512
 
 
 def tile_c51_shifted_log_loss_s3_kernel(
@@ -58,6 +59,7 @@ def tile_c51_shifted_log_loss_s3_kernel(
         spacing_rows = kept([P, F], BF16, "spacing_rows")
         ident = kept([P, P], F32, "ident")
         row_loss = kept([P, TILES], F32, "row_loss")
+        half_loss = kept([P, 2, TILES - SPLIT_FROM], F32, "half_loss")
         x_codes = [kept([P, REST_PASSES, P], U32, "x_codes%d" % i) for i in range(TILES)]
         x_sc = [kept([P, REST_PASSES, P], U8, "x_sc%d" % i) for i in range(TILES)]
         xo_codes = [kept([P, QUAD, P], U32, "xo_codes%d" % a) for a in range(TILES // QUAD)]
@@ -122,12 +124,10 @@ def tile_c51_shifted_log_loss_s3_kernel(
             nc.vector.tensor_tensor(out=scaled[i][:, cols], in0=x_bytes[i][:, cols].bitcast(FP8), in1=k_scale_rows[:, cols], op=ALU.mult)
 
         def sort_x(i):
+            pairs = work.tile([P, REST_PASSES, 2, P], F32, name="sorted", tag="sorted", bufs=1)
+            nc.scalar.copy(out=pairs[:], in_=scaled[i][:].bitcast(F32).rearrange("r (g p u) -> r g u p", g=REST_PASSES, u=2))
             for b in range(2):
-                sorted_pairs[i, b] = work.tile([P, 2, 2, P], F32, name="sorted", tag="sorted", bufs=2)
-                nc.scalar.copy(
-                    out=sorted_pairs[i, b][:].rearrange("r g u p -> r g p u"),
-                    in_=scaled[i][:, 2 * PASS * b : 2 * PASS * (b + 1)].bitcast(F32).rearrange("r (g p u) -> r g p u", g=2, u=2),
-                )
+                sorted_pairs[i, b] = pairs[:, 2 * b : 2 * b + 2]
 
         def turn_x(i, b):
             bank = take_bank(("x", i, b), [P, 2, 2, P])
@@ -258,7 +258,7 @@ def tile_c51_shifted_log_loss_s3_kernel(
                     )
 
         def store_target(i):
-            target_sb[i] = work.tile([P, J], F32, name="target_sb", tag="target_sb", bufs=4)
+            target_sb[i] = work.tile([P, J], F32, name="target_sb", tag="target_sb", bufs=7)
             for h in range(2):
                 cols = slice(BANK * h, BANK * (h + 1))
                 nc.scalar.copy(out=target_sb[i][:, cols], in_=give_back(("target", i, h))[:])
@@ -276,6 +276,62 @@ def tile_c51_shifted_log_loss_s3_kernel(
                 accum_out=row_loss[:, i : i + 1],
             )
 
+        def turn_mass_pass(i, g):
+            bank = take_bank(("mass", i, g), [P, 2, P])
+            for u in range(2):
+                nc.tensor.transpose(bank[:, u, :], mass[i][:, u, g].rearrange("r p e -> r (p e)").bitcast(F32), ident[:])
+
+        def leave_mass_pass(i, g):
+            groups["mass", i, g] = work.tile([P, PASS], BF16, name="groups", tag="groups", bufs=3, align_bytes=64)
+            nc.scalar.copy(
+                out=groups["mass", i, g][:].bitcast(F32).rearrange("p (r u) -> p r u", u=2),
+                in_=give_back(("mass", i, g))[:].rearrange("p u r -> p r u"),
+            )
+
+        def quantise_mass_pass(i, g):
+            if g == 0:
+                codes = work.tile([P, MASS_PASSES, P], U32, name="mass_codes", tag="mass_codes", bufs=3, align_bytes=64)
+                scales = work.tile([P, MASS_PASSES, P], U8, name="mass_sc", tag="mass_sc", bufs=3, align_bytes=64)
+                mass_codes[i], mass_sc[i] = codes[:], scales[:]
+            nc.vector.quantize_mx(out=mass_codes[i][:, g].bitcast(FP8X4), scales=mass_sc[i][:, g], in_=groups["mass", i, g][:])
+
+        def project_pass(i, h, g):
+            if g == 0:
+                take_bank(("target", i, h), [P, BANK])
+            nc.tensor.matmul_mx(
+                out=banks["target", i, h][:],
+                lhsT=mass_codes[i][:, g, :].bitcast(FP8X4),
+                lhsT_scale=mass_sc[i][:, g, :],
+                rhs=proj[:, g, 2 * BANK * h : 2 * BANK * (h + 1)].bitcast(FP4X4),
+                rhs_scale=proj_sc[:, g, BANK * h : BANK * (h + 1)],
+                start=(g == 0),
+                stop=(g == MASS_PASSES - 1),
+            )
+
+        def project_half(i, h):
+            for g in range(MASS_PASSES):
+                project_pass(i, h, g)
+
+        def store_half(i, h):
+            if i not in target_sb:
+                target_sb[i] = work.tile([P, J], F32, name="target_sb", tag="target_sb", bufs=7)
+            cols = slice(BANK * h, BANK * (h + 1))
+            nc.scalar.copy(out=target_sb[i][:, cols], in_=give_back(("target", i, h))[:])
+            nc.sync.dma_start(out=target_hbm[:, i, cols], in_=target_sb[i][:, cols])
+
+        def reduce_half(i, h, from_psum=False):
+            cols = slice(BANK * h, BANK * (h + 1))
+            products = work.tile([P, BANK], F32, name="products", tag="wide", bufs=3)
+            nc.vector.scalar_tensor_tensor(
+                out=products[:],
+                in0=banks["target", i, h][:] if from_psum else target_sb[i][:, cols],
+                scalar=-1.0 / J,
+                in1=logs[i][:, cols],
+                op0=ALU.mult,
+                op1=ALU.mult,
+                accum_out=half_loss[:, h, i - SPLIT_FROM : i - SPLIT_FROM + 1],
+            )
+
         with tc.manual_schedule():
             nc.vector.memset(base_sc[:].rearrange("p g n -> p (g n)").bitcast(I32), 0)
             nc.vector.memset(proj_sc[:].rearrange("p g n -> p (g n)").bitcast(I32), 0)
@@ -285,22 +341,23 @@ def tile_c51_shifted_log_loss_s3_kernel(
             load_online(0, slice(0, FIRST_LOG))
             load_x(0)
             load_x(1)
+            load_online(0, slice(FIRST_LOG, J))
             load_xo(0)
             load_base(0)
             load_scale_bytes(base_sc, base_scales)
-            load_online(0, slice(FIRST_LOG, J))
+            load_online(1)
             load_x(2)
             load_base(1)
-            load_online(1)
             load_online(2)
             load_x(3)
             load_online(3)
             load_online(4)
             nc.sync.dma_start(out=w_rows[:], in_=w_out.rearrange("(p t) n -> p t n", t=4))
-            for i in range(5, TILES):
-                load_online(i)
-            load_x(4)
+            load_online(5)
+            load_online(6)
+            load_online(7)
             load_xo(1)
+            load_x(4)
             nc.sync.dma_start(out=spacing_rows[:], in_=spacing.partition_broadcast(P))
             load_x(5)
             load_x(6)
@@ -311,6 +368,7 @@ def tile_c51_shifted_log_loss_s3_kernel(
             log(0, slice(0, FIRST_LOG))
             for g in range(REST_PASSES):
                 spread_scale(g)
+            log(0, slice(FIRST_LOG, J))
 
             for b in range(2):
                 scale_x(0, 2 * b, 2 * b + 1)
@@ -331,13 +389,13 @@ def tile_c51_shifted_log_loss_s3_kernel(
                     for h in range(2):
                         rest_pass(0, h, g)
                 if b == 0:
-                    log(0, slice(FIRST_LOG, J))
                     log(1)
+                    log(2)
                     turn_x(1, 1)
                     leave_x(1, 1)
             scale_x(2)
             quantise_xo(0)
-            log(2)
+            log(3)
 
             for b in range(2):
                 turn_x(2, b)
@@ -350,107 +408,123 @@ def tile_c51_shifted_log_loss_s3_kernel(
                 rest_passes(1, h)
             quantise_x(2)
             nc.vector.tensor_copy(out=w_groups[:], in_=w_rows[:].rearrange("p t n -> p n t"))
-            for i in (3, 4, 5):
+            for i in (4, 5, 6):
                 log(i)
 
             for b in range(2):
                 turn_x(3, b)
             for b in range(2):
                 leave_x(3, b)
-            for i in (6, 7):
-                log(i)
+            log(7)
             nc.vector.quantize_mx(out=w_codes[:].bitcast(FP8X4), scales=w_sc[:], in_=w_groups[:].rearrange("p n t -> p (n t)"))
             for h in range(2):
                 rest_passes(2, h)
             quantise_x(3)
             scale_x(4)
-            for i in range(HELD):
-                for h in range(2):
-                    out_pass(i, h)
-
-            logits(HELD, 0)
-            for i in range(HELD - 1):
-                for h in range(2):
-                    exp(i, h)
-            for b in range(2):
-                turn_x(HELD + 1, b)
+            for h in range(2):
+                out_pass(0, h)
             for b in range(2):
                 turn_xo(1, b)
-            scale_x(HELD + 2)
-            for b in range(2):
-                leave_x(HELD + 1, b)
+            for i in range(1, HELD):
+                for h in range(2):
+                    out_pass(i, h)
+            for h in range(2):
+                exp(0, h)
+            logits(3, 0)
             for b in range(2):
                 leave_xo(1, b)
+            for b in range(2):
+                turn_x(4, b)
+            scale_x(5)
             for h in range(2):
-                exp(HELD - 1, h)
-            logits(HELD, 1)
+                exp(1, h)
+            for b in range(2):
+                leave_x(4, b)
+            logits(3, 1)
             weigh(0)
-            quantise_x(HELD + 1)
             quantise_xo(1)
             weigh(1)
+            quantise_x(4)
             for h in range(2):
-                exp(HELD, h)
+                exp(2, h)
+            exp(3, 0)
 
-            turned, stored = (), ()
-            for r in range(HELD + 1, TILES - 1):
-                ready, turned = turned, (2 * (r - HELD - 1), 2 * (r - HELD - 1) + 1)
-                logits(r, 0)
-                if ready:
-                    project(ready[0])
-                    weigh(r - 1)
-                if r + 2 < TILES:
-                    scale_x(r + 2)
-                for i in stored:
-                    reduce_loss(i)
-                exp(r, 0)
-                if ready:
-                    store_target(ready[0])
+            for r in (4, 5, 6):
+                pair = (2 * r - 8, 2 * r - 7)
                 for b in range(2):
                     turn_x(r + 1, b)
-                for i in turned:
+                for i in pair:
                     turn_mass(i)
+                if r == 4:
+                    exp(3, 1)
+                if r + 2 < TILES:
+                    scale_x(r + 2)
+                if r == 5:
+                    weigh(4)
+                if r == 6:
+                    reduce_loss(1)
+                leave_mass(pair)
                 for b in range(2):
                     leave_x(r + 1, b)
-                leave_mass(turned)
-                logits(r, 1)
-                if ready:
-                    project(ready[1])
+                logits(r, 0)
+                quantise_mass(pair)
+                if r == 4:
+                    weigh(2)
+                    weigh(3)
                 quantise_x(r + 1)
-                quantise_mass(turned)
-                if not ready:
-                    weigh(HELD - 1)
-                    weigh(HELD)
-                exp(r, 1)
+                if r == 5:
+                    reduce_loss(0)
+                exp(r, 0)
                 if r + 2 < TILES:
                     sort_x(r + 2)
-                if ready:
-                    store_target(ready[1])
-                stored = ready
+                logits(r, 1)
+                exp(r, 1)
+                if r > 4:
+                    project(pair[0] - 1)
+                    if r == 6:
+                        reduce_loss(2)
+                    weigh(r)
+                    store_target(pair[0] - 1)
+                if r < 6:
+                    project(pair[0])
+                    store_target(pair[0])
 
             last = TILES - 1
             logits(last, 0)
-            weigh(last - 1)
-            for i in stored:
-                reduce_loss(i)
+            project(4)
+            reduce_loss(3)
             exp(last, 0)
-            turn_mass(last - 1)
-            leave_mass((last - 1,))
-            logits(last, 1)
             weigh(last, 0, 1)
-            quantise_mass((last - 1,))
+            store_target(4)
+            logits(last, 1)
+            turn_mass(last - 1)
+            turn_mass_pass(last, 0)
             exp(last, 1)
-            project(turned[0])
+            reduce_loss(4)
             weigh(last, 1, 2)
-            store_target(turned[0])
-            turn_mass(last)
-            leave_mass((last,))
-            project(turned[1])
-            reduce_loss(turned[0])
-            quantise_mass((last,))
-            store_target(turned[1])
-            for i in (last - 1, last):
-                project(i)
-                store_target(i)
-            for i in (turned[1], last - 1, last):
-                reduce_loss(i)
+            leave_mass((last - 1,))
+            leave_mass_pass(last, 0)
+            project(5)
+            quantise_mass((last - 1,))
+            quantise_mass_pass(last, 0)
+            store_half(5, 0)
+            turn_mass_pass(last, 1)
+            leave_mass_pass(last, 1)
+            store_half(5, 1)
+            reduce_half(5, 0)
+            quantise_mass_pass(last, 1)
+            project(last - 1)
+            for g in range(2):
+                for h in (0, 1):
+                    project_pass(last, h, g)
+            reduce_half(5, 1)
+            store_half(last - 1, 0)
+            store_half(last - 1, 1)
+            reduce_half(last - 1, 0)
+            reduce_half(last - 1, 1)
+            store_half(last, 0)
+            store_half(last, 1)
+            reduce_half(last, 0)
+            reduce_half(last, 1)
+            nc.vector.tensor_tensor(out=row_loss[:, SPLIT_FROM:], in0=half_loss[:, 0], in1=half_loss[:, 1], op=ALU.add)
             nc.sync.dma_start(out=loss.rearrange("(r i) -> r i", i=TILES), in_=row_loss[:])

@@ -42,7 +42,9 @@ def tile_c51_shifted_log_loss_s3_kernel(
         def kept(shape, dtype, name):
             return keep.tile(shape, dtype, name=name, tag=name, align_bytes=64)
 
-        x_bytes = [kept([P, KR], U8, "x_bytes%d" % i) for i in range(TILES)]
+        x_first = [kept([P, KR], U8, "x_bytes%d" % i) for i in range(2)]
+        x_pairs = [kept([P, 2, KR], U8, "x_bytes_pair%d" % a) for a in range(1, TILES // 2)]
+        x_bytes = [t[:] for t in x_first] + [t[:, c] for t in x_pairs for c in range(2)]
         k_scale = kept([P, REST_PASSES, 4], F32, "k_scale")
         k_scale_rows = kept([P, KR], F32, "k_scale_rows")
         base = [kept([P, 2, 2 * F], U8, "base%d" % b) for b in range(2)]
@@ -54,8 +56,10 @@ def tile_c51_shifted_log_loss_s3_kernel(
         w_codes = kept([P, F], U32, "w_codes")
         w_sc = kept([P, F], U8, "w_sc")
         xo = [kept([P, QUAD, KO], BF16, "xo%d" % a) for a in range(TILES // QUAD)]
-        onl = [kept([P, J], BF16, "onl%d" % i) for i in range(TILES)]
+        onl_pairs = [kept([P, 2, J], BF16, "onl%d" % a) for a in range(TILES // 2)]
+        onl = [t[:, c] for t in onl_pairs for c in range(2)]
         logs = [kept([P, J], F32, "logs%d" % i) for i in range(TILES)]
+        spacing_cols = kept([P, 8], BF16, "spacing_cols")
         spacing_rows = kept([P, F], BF16, "spacing_rows")
         ident = kept([P, P], F32, "ident")
         row_loss = kept([P, TILES], F32, "row_loss")
@@ -87,7 +91,13 @@ def tile_c51_shifted_log_loss_s3_kernel(
             return banks[key]
 
         def load_x(i):
-            nc.sync.dma_start(out=x_bytes[i][:], in_=x_hbm[:, i, :])
+            nc.sync.dma_start(out=x_bytes[i], in_=x_hbm[:, i, :])
+
+        def load_x_pair(a):
+            nc.sync.dma_start(out=x_pairs[a - 1][:], in_=x_hbm[:, 2 * a : 2 * a + 2, :])
+
+        def load_online_pair(a):
+            nc.sync.dma_start(out=onl_pairs[a][:], in_=online_hbm[:, 2 * a : 2 * a + 2, :])
 
         def load_online(i, cols=slice(0, J)):
             nc.sync.dma_start(out=onl[i][:, cols], in_=online_hbm[:, i, cols])
@@ -117,6 +127,16 @@ def tile_c51_shifted_log_loss_s3_kernel(
                 in_=give_back(("scale", g))[:].rearrange("r t p -> r p t"),
             )
 
+        def spread_spacing():
+            bank = take_bank("spacing", [P, 4, P])
+            pairs = spacing_cols[:].bitcast(F32)
+            for c in range(4):
+                nc.tensor.transpose(bank[:, c, :], pairs[:, c : c + 1].to_broadcast([P, P]), ident[:])
+            nc.scalar.copy(
+                out=spacing_rows[:].bitcast(F32).rearrange("r (q c) -> r q c", c=4),
+                in_=give_back("spacing")[:].rearrange("r c q -> r q c"),
+            )
+
         def scale_x(i, g0=0, g1=REST_PASSES):
             if g0 == 0:
                 scaled[i] = work.tile([P, KR], BF16, name="scaled", tag="wide", bufs=3)
@@ -140,7 +160,7 @@ def tile_c51_shifted_log_loss_s3_kernel(
 
         def leave_bank(key, into, n, parts):
             if n == 0:
-                groups[into] = work.tile([P, parts * 2 * PASS], BF16, name="groups", tag="groups", bufs=3, align_bytes=64)
+                groups[into] = work.tile([P, parts * 2 * PASS], BF16, name="groups", tag="groups", bufs=4, align_bytes=64)
             nc.scalar.copy(
                 out=groups[into][:, 2 * PASS * n : 2 * PASS * (n + 1)].bitcast(F32).rearrange("p (c r u) -> p c r u", c=2, u=2),
                 in_=give_back(key)[:].rearrange("p u c r -> p c r u"),
@@ -172,6 +192,24 @@ def tile_c51_shifted_log_loss_s3_kernel(
                 scales=xo_sc[a][:].rearrange("p i r -> p (i r)"),
                 in_=groups["xo", a][:],
             )
+
+        def leave_xo_pair(a, b):
+            leave_bank(("xo", a, b), ("xo", a, b), 0, 1)
+
+        def quantise_xo_pair(a, b):
+            nc.vector.quantize_mx(
+                out=xo_codes[a][:, 2 * b : 2 * b + 2].rearrange("p i r -> p (i r)").bitcast(FP8X4),
+                scales=xo_sc[a][:, 2 * b : 2 * b + 2].rearrange("p i r -> p (i r)"),
+                in_=groups["xo", a, b][:],
+            )
+
+        def group_w(h):
+            cols = slice(BANK * h, BANK * (h + 1))
+            nc.vector.tensor_copy(out=w_groups[:, cols], in_=w_rows[:, :, cols].rearrange("p t n -> p n t"))
+
+        def quantise_w(h):
+            cols = slice(BANK * h, BANK * (h + 1))
+            nc.vector.quantize_mx(out=w_codes[:, cols].bitcast(FP8X4), scales=w_sc[:, cols], in_=w_groups[:, cols].rearrange("p n t -> p (n t)"))
 
         def rest_pass(i, h, g):
             if g == 0:
@@ -258,7 +296,7 @@ def tile_c51_shifted_log_loss_s3_kernel(
                     )
 
         def store_target(i):
-            target_sb[i] = work.tile([P, J], F32, name="target_sb", tag="target_sb", bufs=7)
+            target_sb[i] = work.tile([P, J], F32, name="target_sb", tag="target_sb", bufs=5)
             for h in range(2):
                 cols = slice(BANK * h, BANK * (h + 1))
                 nc.scalar.copy(out=target_sb[i][:, cols], in_=give_back(("target", i, h))[:])
@@ -282,7 +320,7 @@ def tile_c51_shifted_log_loss_s3_kernel(
                 nc.tensor.transpose(bank[:, u, :], mass[i][:, u, g].rearrange("r p e -> r (p e)").bitcast(F32), ident[:])
 
         def leave_mass_pass(i, g):
-            groups["mass", i, g] = work.tile([P, PASS], BF16, name="groups", tag="groups", bufs=3, align_bytes=64)
+            groups["mass", i, g] = work.tile([P, PASS], BF16, name="groups", tag="groups", bufs=4, align_bytes=64)
             nc.scalar.copy(
                 out=groups["mass", i, g][:].bitcast(F32).rearrange("p (r u) -> p r u", u=2),
                 in_=give_back(("mass", i, g))[:].rearrange("p u r -> p r u"),
@@ -314,7 +352,7 @@ def tile_c51_shifted_log_loss_s3_kernel(
 
         def store_half(i, h):
             if i not in target_sb:
-                target_sb[i] = work.tile([P, J], F32, name="target_sb", tag="target_sb", bufs=7)
+                target_sb[i] = work.tile([P, J], F32, name="target_sb", tag="target_sb", bufs=5)
             cols = slice(BANK * h, BANK * (h + 1))
             nc.scalar.copy(out=target_sb[i][:, cols], in_=give_back(("target", i, h))[:])
             nc.sync.dma_start(out=target_hbm[:, i, cols], in_=target_sb[i][:, cols])
@@ -340,13 +378,14 @@ def tile_c51_shifted_log_loss_s3_kernel(
             nc.sync.dma_start(out=k_scale[:], in_=x_rest_scale.rearrange("o (g p t) -> p (o g) t", p=P, t=4))
             load_online(0, slice(0, FIRST_LOG))
             load_x(0)
+            nc.sync.dma_start(out=spacing_cols[:], in_=spacing.rearrange("(q c) -> q c", c=8))
+            load_xo(0)
             load_x(1)
             load_online(0, slice(FIRST_LOG, J))
-            load_xo(0)
+            load_x(2)
             load_base(0)
             load_scale_bytes(base_sc, base_scales)
             load_online(1)
-            load_x(2)
             load_base(1)
             load_online(2)
             load_x(3)
@@ -354,21 +393,19 @@ def tile_c51_shifted_log_loss_s3_kernel(
             load_online(4)
             nc.sync.dma_start(out=w_rows[:], in_=w_out.rearrange("(p t) n -> p t n", t=4))
             load_online(5)
-            load_online(6)
-            load_online(7)
-            load_xo(1)
+            load_online_pair(3)
             load_x(4)
-            nc.sync.dma_start(out=spacing_rows[:], in_=spacing.partition_broadcast(P))
+            load_xo(1)
             load_x(5)
-            load_x(6)
+            load_x_pair(3)
             nc.sync.dma_start(out=proj[:], in_=proj_words.rearrange("g p n -> p g n"))
             load_scale_bytes(proj_sc, proj_scales)
-            load_x(7)
 
             log(0, slice(0, FIRST_LOG))
             for g in range(REST_PASSES):
                 spread_scale(g)
             log(0, slice(FIRST_LOG, J))
+            spread_spacing()
 
             for b in range(2):
                 scale_x(0, 2 * b, 2 * b + 1)
@@ -377,57 +414,50 @@ def tile_c51_shifted_log_loss_s3_kernel(
                 leave_x(0, b)
                 turn_xo(0, b)
                 leave_xo(0, b)
-
-            scale_x(1, 0, 2)
-            quantise_x(0, 0, 2)
-            turn_x(1, 0)
-            leave_x(1, 0)
-            scale_x(1, 2, 4)
-            quantise_x(0, 2, 4)
             for b in range(2):
-                for g in (2 * b, 2 * b + 1):
-                    for h in range(2):
-                        rest_pass(0, h, g)
-                if b == 0:
-                    log(1)
-                    log(2)
-                    turn_x(1, 1)
-                    leave_x(1, 1)
+                scale_x(1, 2 * b, 2 * b + 2)
+                turn_x(1, b)
+            quantise_x(0)
             scale_x(2)
-            quantise_xo(0)
-            log(3)
-
+            leave_x(1, 0)
+            log(1)
+            leave_x(1, 1)
+            log(2)
+            for g in range(REST_PASSES):
+                for h in range(2):
+                    rest_pass(0, h, g)
             for b in range(2):
                 turn_x(2, b)
-            scale_x(3, 0, 2)
             quantise_x(1)
-            scale_x(3, 2, 4)
+            scale_x(3)
+            log(3)
             for b in range(2):
                 leave_x(2, b)
             for h in range(2):
                 rest_passes(1, h)
+            quantise_xo(0)
             quantise_x(2)
-            nc.vector.tensor_copy(out=w_groups[:], in_=w_rows[:].rearrange("p t n -> p n t"))
-            for i in (4, 5, 6):
+            group_w(0)
+            for i in (4, 5):
                 log(i)
-
             for b in range(2):
                 turn_x(3, b)
+            group_w(1)
             for b in range(2):
                 leave_x(3, b)
-            log(7)
-            nc.vector.quantize_mx(out=w_codes[:].bitcast(FP8X4), scales=w_sc[:], in_=w_groups[:].rearrange("p n t -> p (n t)"))
+            for i in (6, 7):
+                log(i)
+            for h in range(2):
+                quantise_w(h)
             for h in range(2):
                 rest_passes(2, h)
             quantise_x(3)
             scale_x(4)
-            for h in range(2):
-                out_pass(0, h)
-            for b in range(2):
-                turn_xo(1, b)
-            for i in range(1, HELD):
+            for i in range(HELD):
                 for h in range(2):
                     out_pass(i, h)
+            for b in range(2):
+                turn_xo(1, b)
             for h in range(2):
                 exp(0, h)
             logits(3, 0)
@@ -468,6 +498,8 @@ def tile_c51_shifted_log_loss_s3_kernel(
                     leave_x(r + 1, b)
                 logits(r, 0)
                 quantise_mass(pair)
+                if r == 6:
+                    reduce_loss(2)
                 if r == 4:
                     weigh(2)
                     weigh(3)
@@ -481,8 +513,6 @@ def tile_c51_shifted_log_loss_s3_kernel(
                 exp(r, 1)
                 if r > 4:
                     project(pair[0] - 1)
-                    if r == 6:
-                        reduce_loss(2)
                     weigh(r)
                     store_target(pair[0] - 1)
                 if r < 6:

@@ -378,24 +378,24 @@ def tile_c51_shifted_log_loss_s3_kernel(
             nc.sync.dma_start(out=k_scale[:], in_=x_rest_scale.rearrange("o (g p t) -> p (o g) t", p=P, t=4))
             load_online(0, slice(0, FIRST_LOG))
             load_x(0)
-            nc.sync.dma_start(out=spacing_cols[:], in_=spacing.rearrange("(q c) -> q c", c=8))
             load_xo(0)
+            load_online(1)
+            nc.sync.dma_start(out=spacing_cols[:], in_=spacing.rearrange("(q c) -> q c", c=8))
             load_x(1)
             load_online(0, slice(FIRST_LOG, J))
+            load_scale_bytes(base_sc, base_scales)
             load_x(2)
             load_base(0)
-            load_scale_bytes(base_sc, base_scales)
-            load_online(1)
-            load_base(1)
             load_online(2)
             load_x(3)
             load_online(3)
+            load_base(1)
             load_online(4)
             nc.sync.dma_start(out=w_rows[:], in_=w_out.rearrange("(p t) n -> p t n", t=4))
             load_online(5)
             load_online_pair(3)
-            load_x(4)
             load_xo(1)
+            load_x(4)
             load_x(5)
             load_x_pair(3)
             nc.sync.dma_start(out=proj[:], in_=proj_words.rearrange("g p n -> p g n"))
@@ -404,125 +404,153 @@ def tile_c51_shifted_log_loss_s3_kernel(
             log(0, slice(0, FIRST_LOG))
             for g in range(REST_PASSES):
                 spread_scale(g)
+            for g in range(REST_PASSES):
+                scale_x(0, g, g + 1)
+            log(1)
             log(0, slice(FIRST_LOG, J))
-            spread_spacing()
-
             for b in range(2):
-                scale_x(0, 2 * b, 2 * b + 1)
-                scale_x(0, 2 * b + 1, 2 * b + 2)
-                turn_x(0, b)
-                leave_x(0, b)
                 turn_xo(0, b)
+            for b in range(2):
+                turn_x(0, b)
+            for b in range(2):
+                leave_x(0, b)
+            for b in range(2):
                 leave_xo(0, b)
+            spread_spacing()
             for b in range(2):
                 scale_x(1, 2 * b, 2 * b + 2)
                 turn_x(1, b)
+                leave_x(1, b)
             quantise_x(0)
             scale_x(2)
-            leave_x(1, 0)
-            log(1)
-            leave_x(1, 1)
-            log(2)
-            for g in range(REST_PASSES):
+            for g in range(2):
                 for h in range(2):
                     rest_pass(0, h, g)
+            for i in (2, 3):
+                log(i)
             for b in range(2):
                 turn_x(2, b)
             quantise_x(1)
             scale_x(3)
-            log(3)
             for b in range(2):
                 leave_x(2, b)
-            for h in range(2):
-                rest_passes(1, h)
+            for g in range(2, 4):
+                for h in range(2):
+                    rest_pass(0, h, g)
+            rest_passes(1, 0)
             quantise_xo(0)
             quantise_x(2)
-            group_w(0)
-            for i in (4, 5):
-                log(i)
+            log(4)
             for b in range(2):
                 turn_x(3, b)
-            group_w(1)
+            for h in range(2):
+                group_w(h)
             for b in range(2):
                 leave_x(3, b)
-            for i in (6, 7):
-                log(i)
-            for h in range(2):
-                quantise_w(h)
+            rest_passes(1, 1)
             for h in range(2):
                 rest_passes(2, h)
+            for i in (5, 6, 7):
+                log(i)
+            quantise_w(0)
             quantise_x(3)
+            quantise_w(1)
             scale_x(4)
+            turn_xo(1, 0)
             for i in range(HELD):
                 for h in range(2):
                     out_pass(i, h)
-            for b in range(2):
-                turn_xo(1, b)
+            logits(3, 0)
             for h in range(2):
                 exp(0, h)
-            logits(3, 0)
-            for b in range(2):
-                leave_xo(1, b)
             for b in range(2):
                 turn_x(4, b)
-            scale_x(5)
             for h in range(2):
                 exp(1, h)
+            leave_xo_pair(1, 0)
+            scale_x(5)
             for b in range(2):
                 leave_x(4, b)
             logits(3, 1)
             weigh(0)
-            quantise_xo(1)
-            weigh(1)
             quantise_x(4)
+            weigh(1)
+            quantise_xo_pair(1, 0)
             for h in range(2):
                 exp(2, h)
             exp(3, 0)
 
-            for r in (4, 5, 6):
-                pair = (2 * r - 8, 2 * r - 7)
-                for b in range(2):
-                    turn_x(r + 1, b)
-                for i in pair:
-                    turn_mass(i)
-                if r == 4:
-                    exp(3, 1)
-                if r + 2 < TILES:
-                    scale_x(r + 2)
-                if r == 5:
-                    weigh(4)
-                if r == 6:
-                    reduce_loss(1)
-                leave_mass(pair)
-                for b in range(2):
-                    leave_x(r + 1, b)
-                logits(r, 0)
-                quantise_mass(pair)
-                if r == 6:
-                    reduce_loss(2)
-                if r == 4:
-                    weigh(2)
-                    weigh(3)
-                quantise_x(r + 1)
-                if r == 5:
-                    reduce_loss(0)
-                exp(r, 0)
-                if r + 2 < TILES:
-                    sort_x(r + 2)
-                logits(r, 1)
-                exp(r, 1)
-                if r > 4:
-                    project(pair[0] - 1)
-                    weigh(r)
-                    store_target(pair[0] - 1)
-                if r < 6:
-                    project(pair[0])
-                    store_target(pair[0])
+            for b in range(2):
+                turn_x(5, b)
+            turn_mass(0)
+            scale_x(6, 0, 2)
+            leave_mass((0,))
+            exp(3, 1)
+            for b in range(2):
+                leave_x(5, b)
+            logits(4, 0)
+            turn_mass(1)
+            turn_xo(1, 1)
+            quantise_mass((0,))
+            scale_x(6, 2, 4)
+            leave_mass((1,))
+            exp(4, 0)
+            logits(4, 1)
+            weigh(2)
+            quantise_mass((1,))
+            weigh(3)
+            quantise_x(5)
+            sort_x(6)
+            exp(4, 1)
+            leave_xo_pair(1, 1)
+            for i in (0, 1):
+                project(i)
+                store_target(i)
+
+            for b in range(2):
+                turn_x(6, b)
+            for i in (2, 3):
+                turn_mass(i)
+            scale_x(7)
+            quantise_xo_pair(1, 1)
+            leave_mass((2, 3))
+            for b in range(2):
+                leave_x(6, b)
+            logits(5, 0)
+            quantise_mass((2, 3))
+            weigh(4)
+            quantise_x(6)
+            exp(5, 0)
+            logits(5, 1)
+            exp(5, 1)
+            sort_x(7)
+            for i in (2, 3):
+                project(i)
+            store_target(2)
+            weigh(5)
+            reduce_loss(0)
+            for b in range(2):
+                turn_x(7, b)
+            for i in (4, 5):
+                turn_mass(i)
+            reduce_loss(1)
+            for b in range(2):
+                leave_x(7, b)
+            leave_mass((4, 5))
+            store_target(3)
+            logits(6, 0)
+            quantise_x(7)
+            reduce_loss(2)
+            quantise_mass((4, 5))
+            exp(6, 0)
+            logits(6, 1)
+            exp(6, 1)
 
             last = TILES - 1
             logits(last, 0)
             project(4)
             reduce_loss(3)
+            weigh(6)
             exp(last, 0)
             weigh(last, 0, 1)
             store_target(4)

@@ -205,7 +205,10 @@ def tile_c51_shifted_log_loss_s3_kernel(
 
         def group_w(h):
             cols = slice(BANK * h, BANK * (h + 1))
-            nc.vector.tensor_copy(out=w_groups[:, cols], in_=w_rows[:, :, cols].rearrange("p t n -> p n t"))
+            nc.vector.tensor_copy(
+                out=w_groups[:, cols].rearrange("p (c i) t -> p c t i", i=4),
+                in_=w_rows[:, :, cols].rearrange("p t (c i) -> p c t i", i=4),
+            )
 
         def quantise_w(h):
             cols = slice(BANK * h, BANK * (h + 1))
@@ -567,8 +570,8 @@ def tile_c51_shifted_log_loss_s3_kernel(
             quantise_mass_pass(last, 0)
             store_half(5, 0)
             turn_mass_pass(last, 1)
-            leave_mass_pass(last, 1)
             store_half(5, 1)
+            leave_mass_pass(last, 1)
             reduce_half(5, 0)
             quantise_mass_pass(last, 1)
             project(last - 1)

@@ -109,10 +109,10 @@ def tile_c51_shifted_log_loss_s3_kernel(
             nc.sync.dma_start(out=base[b][:], in_=base_words.rearrange("g p n -> p g n")[:, 2 * b : 2 * b + 2, :])
 
         def load_scale_bytes(tile, rows):
-            for q in range(4):
+            for j in range(4):
                 nc.sync.dma_start(
-                    out=tile[32 * q : 32 * q + 4].bitcast(I32),
-                    in_=rows[:, 4 * q : 4 * q + 4, :].rearrange("g r n -> r g n").bitcast(I32),
+                    out=tile[j:P:32].bitcast(I32),
+                    in_=rows[:, j:16:4, :].rearrange("g q n -> q g n").bitcast(I32),
                 )
 
         def log(i, cols=slice(0, J)):

@@ -45,7 +45,7 @@ def tile_c51_shifted_log_loss_s3_kernel(
         x_first = [kept([P, KR], U8, "x_bytes%d" % i) for i in range(2)]
         x_pairs = [kept([P, 2, KR], U8, "x_bytes_pair%d" % a) for a in range(1, TILES // 2)]
         x_bytes = [t[:] for t in x_first] + [t[:, c] for t in x_pairs for c in range(2)]
-        k_scale = kept([P, REST_PASSES, 4], F32, "k_scale")
+        k_scale = kept([P, REST_PASSES, 8], F32, "k_scale")
         k_scale_rows = kept([P, KR], F32, "k_scale_rows")
         base = [kept([P, 2, 2 * F], U8, "base%d" % b) for b in range(2)]
         base_sc = kept([P, REST_PASSES, F], U8, "base_sc")
@@ -59,7 +59,6 @@ def tile_c51_shifted_log_loss_s3_kernel(
         onl_pairs = [kept([P, 2, J], BF16, "onl%d" % a) for a in range(TILES // 2)]
         onl = [t[:, c] for t in onl_pairs for c in range(2)]
         logs = [kept([P, J], F32, "logs%d" % i) for i in range(TILES)]
-        spacing_cols = kept([P, 8], BF16, "spacing_cols")
         spacing_rows = kept([P, F], BF16, "spacing_rows")
         ident = kept([P, P], F32, "ident")
         row_loss = kept([P, TILES], F32, "row_loss")
@@ -122,19 +121,10 @@ def tile_c51_shifted_log_loss_s3_kernel(
             bank = take_bank(("scale", g), [P, 4, P])
             for t in range(4):
                 nc.tensor.transpose(bank[:, t, :], k_scale[:, g, t : t + 1].to_broadcast([P, P]), ident[:])
-            nc.scalar.copy(
+            leave = nc.vector.tensor_copy if g == 0 else nc.scalar.copy
+            leave(
                 out=k_scale_rows[:, PASS * g : PASS * (g + 1)].rearrange("r (p t) -> r p t", t=4),
                 in_=give_back(("scale", g))[:].rearrange("r t p -> r p t"),
-            )
-
-        def spread_spacing():
-            bank = take_bank("spacing", [P, 4, P])
-            pairs = spacing_cols[:].bitcast(F32)
-            for c in range(4):
-                nc.tensor.transpose(bank[:, c, :], pairs[:, c : c + 1].to_broadcast([P, P]), ident[:])
-            nc.scalar.copy(
-                out=spacing_rows[:].bitcast(F32).rearrange("r (q c) -> r q c", c=4),
-                in_=give_back("spacing")[:].rearrange("r c q -> r q c"),
             )
 
         def scale_x(i, g0=0, g1=REST_PASSES):
@@ -378,12 +368,11 @@ def tile_c51_shifted_log_loss_s3_kernel(
             nc.vector.memset(proj_sc[:].rearrange("p g n -> p (g n)").bitcast(I32), 0)
             make_identity(nc, ident[:])
 
-            nc.sync.dma_start(out=k_scale[:], in_=x_rest_scale.rearrange("o (g p t) -> p (o g) t", p=P, t=4))
-            load_online(0, slice(0, FIRST_LOG))
+            nc.sync.dma_start(out=k_scale[:, :, 0:4], in_=x_rest_scale.rearrange("o (g p t) -> p (o g) t", p=P, t=4))
             load_x(0)
+            load_online(0, slice(0, FIRST_LOG))
             load_xo(0)
             load_online(1)
-            nc.sync.dma_start(out=spacing_cols[:], in_=spacing.rearrange("(q c) -> q c", c=8))
             load_x(1)
             load_online(0, slice(FIRST_LOG, J))
             load_scale_bytes(base_sc, base_scales)
@@ -400,6 +389,7 @@ def tile_c51_shifted_log_loss_s3_kernel(
             load_xo(1)
             load_x(4)
             load_x(5)
+            nc.sync.dma_start(out=spacing_rows[:], in_=spacing.partition_broadcast(P))
             load_x_pair(3)
             nc.sync.dma_start(out=proj[:], in_=proj_words.rearrange("g p n -> p g n"))
             load_scale_bytes(proj_sc, proj_scales)
@@ -419,7 +409,6 @@ def tile_c51_shifted_log_loss_s3_kernel(
                 leave_x(0, b)
             for b in range(2):
                 leave_xo(0, b)
-            spread_spacing()
             for b in range(2):
                 scale_x(1, 2 * b, 2 * b + 2)
                 turn_x(1, b)

@@ -25,9 +25,14 @@ REST_PASSES = KR // PASS
 MASS_PASSES = F // PASS
 QUAD = 4
 HELD = 3
-SORTED_FROM = HELD + 3
-SPLIT_FROM = 5
+SORTED_FROM = TILES - 2
+SPLIT_FROM = TILES - 3
 FIRST_LOG = 512
+W_ON_SCALAR = 192
+WIDE_BUFS = 3
+GROUP_BUFS = 4
+MASS_CODE_BUFS = 3
+TARGET_BUFS = 5
 
 
 def tile_c51_shifted_log_loss_s3_kernel(
@@ -36,7 +41,7 @@ def tile_c51_shifted_log_loss_s3_kernel(
     nc = tc.nc
     with ExitStack() as ctx:
         keep = ctx.enter_context(tc.tile_pool(name="keep", bufs=1))
-        work = ctx.enter_context(tc.tile_pool(name="work", bufs=3))
+        work = ctx.enter_context(tc.tile_pool(name="work", bufs=WIDE_BUFS))
         psum = ctx.enter_context(tc.psum_pool(name="psum", bufs=1))
 
         def kept(shape, dtype, name):
@@ -129,7 +134,7 @@ def tile_c51_shifted_log_loss_s3_kernel(
 
         def scale_x(i, g0=0, g1=REST_PASSES):
             if g0 == 0:
-                scaled[i] = work.tile([P, KR], BF16, name="scaled", tag="wide", bufs=3)
+                scaled[i] = work.tile([P, KR], BF16, name="scaled", tag="wide", bufs=WIDE_BUFS)
             cols = slice(PASS * g0, PASS * g1)
             nc.vector.tensor_tensor(out=scaled[i][:, cols], in0=x_bytes[i][:, cols].bitcast(FP8), in1=k_scale_rows[:, cols], op=ALU.mult)
 
@@ -150,7 +155,7 @@ def tile_c51_shifted_log_loss_s3_kernel(
 
         def leave_bank(key, into, n, parts):
             if n == 0:
-                groups[into] = work.tile([P, parts * 2 * PASS], BF16, name="groups", tag="groups", bufs=4, align_bytes=64)
+                groups[into] = work.tile([P, parts * 2 * PASS], BF16, name="groups", tag="groups", bufs=GROUP_BUFS, align_bytes=64)
             nc.scalar.copy(
                 out=groups[into][:, 2 * PASS * n : 2 * PASS * (n + 1)].bitcast(F32).rearrange("p (c r u) -> p c r u", c=2, u=2),
                 in_=give_back(key)[:].rearrange("p u c r -> p c r u"),
@@ -193,16 +198,14 @@ def tile_c51_shifted_log_loss_s3_kernel(
                 in_=groups["xo", a, b][:],
             )
 
-        def group_w(h):
-            cols = slice(BANK * h, BANK * (h + 1))
-            nc.vector.tensor_copy(
+        def group_w(copy, cols):
+            copy(
                 out=w_groups[:, cols].rearrange("p (c i) t -> p c t i", i=4),
                 in_=w_rows[:, :, cols].rearrange("p t (c i) -> p c t i", i=4),
             )
 
-        def quantise_w(h):
-            cols = slice(BANK * h, BANK * (h + 1))
-            nc.vector.quantize_mx(out=w_codes[:, cols].bitcast(FP8X4), scales=w_sc[:, cols], in_=w_groups[:, cols].rearrange("p n t -> p (n t)"))
+        def quantise_w():
+            nc.vector.quantize_mx(out=w_codes[:].bitcast(FP8X4), scales=w_sc[:], in_=w_groups[:].rearrange("p n t -> p (n t)"))
 
         def rest_pass(i, h, g):
             if g == 0:
@@ -264,8 +267,8 @@ def tile_c51_shifted_log_loss_s3_kernel(
                 leave_bank(("mass", i), ("mass", tiles), n, len(tiles))
 
         def quantise_mass(tiles):
-            codes = work.tile([P, len(tiles), MASS_PASSES, P], U32, name="mass_codes", tag="mass_codes", bufs=3, align_bytes=64)
-            scales = work.tile([P, len(tiles), MASS_PASSES, P], U8, name="mass_sc", tag="mass_sc", bufs=3, align_bytes=64)
+            codes = work.tile([P, len(tiles), MASS_PASSES, P], U32, name="mass_codes", tag="mass_codes", bufs=MASS_CODE_BUFS, align_bytes=64)
+            scales = work.tile([P, len(tiles), MASS_PASSES, P], U8, name="mass_sc", tag="mass_sc", bufs=MASS_CODE_BUFS, align_bytes=64)
             for n, i in enumerate(tiles):
                 mass_codes[i], mass_sc[i] = codes[:, n], scales[:, n]
             nc.vector.quantize_mx(
@@ -274,29 +277,8 @@ def tile_c51_shifted_log_loss_s3_kernel(
                 in_=groups["mass", tiles][:],
             )
 
-        def project(i):
-            for h in range(2):
-                bank = take_bank(("target", i, h), [P, BANK])
-                for g in range(MASS_PASSES):
-                    nc.tensor.matmul_mx(
-                        out=bank[:],
-                        lhsT=mass_codes[i][:, g, :].bitcast(FP8X4),
-                        lhsT_scale=mass_sc[i][:, g, :],
-                        rhs=proj[:, g, 2 * BANK * h : 2 * BANK * (h + 1)].bitcast(FP4X4),
-                        rhs_scale=proj_sc[:, g, BANK * h : BANK * (h + 1)],
-                        start=(g == 0),
-                        stop=(g == MASS_PASSES - 1),
-                    )
-
-        def store_target(i):
-            target_sb[i] = work.tile([P, J], F32, name="target_sb", tag="target_sb", bufs=5)
-            for h in range(2):
-                cols = slice(BANK * h, BANK * (h + 1))
-                nc.scalar.copy(out=target_sb[i][:, cols], in_=give_back(("target", i, h))[:])
-                nc.sync.dma_start(out=target_hbm[:, i, cols], in_=target_sb[i][:, cols])
-
         def reduce_loss(i):
-            products = work.tile([P, J], F32, name="products", tag="wide", bufs=3)
+            products = work.tile([P, J], F32, name="products", tag="wide", bufs=WIDE_BUFS)
             nc.vector.scalar_tensor_tensor(
                 out=products[:],
                 in0=target_sb[i][:],
@@ -313,7 +295,7 @@ def tile_c51_shifted_log_loss_s3_kernel(
                 nc.tensor.transpose(bank[:, u, :], mass[i][:, u, g].rearrange("r p e -> r (p e)").bitcast(F32), ident[:])
 
         def leave_mass_pass(i, g):
-            groups["mass", i, g] = work.tile([P, PASS], BF16, name="groups", tag="groups", bufs=4, align_bytes=64)
+            groups["mass", i, g] = work.tile([P, PASS], BF16, name="groups", tag="groups", bufs=GROUP_BUFS, align_bytes=64)
             nc.scalar.copy(
                 out=groups["mass", i, g][:].bitcast(F32).rearrange("p (r u) -> p r u", u=2),
                 in_=give_back(("mass", i, g))[:].rearrange("p u r -> p r u"),
@@ -321,8 +303,8 @@ def tile_c51_shifted_log_loss_s3_kernel(
 
         def quantise_mass_pass(i, g):
             if g == 0:
-                codes = work.tile([P, MASS_PASSES, P], U32, name="mass_codes", tag="mass_codes", bufs=3, align_bytes=64)
-                scales = work.tile([P, MASS_PASSES, P], U8, name="mass_sc", tag="mass_sc", bufs=3, align_bytes=64)
+                codes = work.tile([P, MASS_PASSES, P], U32, name="mass_codes", tag="mass_codes", bufs=MASS_CODE_BUFS, align_bytes=64)
+                scales = work.tile([P, MASS_PASSES, P], U8, name="mass_sc", tag="mass_sc", bufs=MASS_CODE_BUFS, align_bytes=64)
                 mass_codes[i], mass_sc[i] = codes[:], scales[:]
             nc.vector.quantize_mx(out=mass_codes[i][:, g].bitcast(FP8X4), scales=mass_sc[i][:, g], in_=groups["mass", i, g][:])
 
@@ -339,23 +321,28 @@ def tile_c51_shifted_log_loss_s3_kernel(
                 stop=(g == MASS_PASSES - 1),
             )
 
-        def project_half(i, h):
-            for g in range(MASS_PASSES):
-                project_pass(i, h, g)
+        def project(i):
+            for h in range(2):
+                for g in range(MASS_PASSES):
+                    project_pass(i, h, g)
 
         def store_half(i, h):
-            if i not in target_sb:
-                target_sb[i] = work.tile([P, J], F32, name="target_sb", tag="target_sb", bufs=5)
+            if h == 0:
+                target_sb[i] = work.tile([P, J], F32, name="target_sb", tag="target_sb", bufs=TARGET_BUFS)
             cols = slice(BANK * h, BANK * (h + 1))
             nc.scalar.copy(out=target_sb[i][:, cols], in_=give_back(("target", i, h))[:])
             nc.sync.dma_start(out=target_hbm[:, i, cols], in_=target_sb[i][:, cols])
 
-        def reduce_half(i, h, from_psum=False):
+        def store_target(i):
+            for h in range(2):
+                store_half(i, h)
+
+        def reduce_half(i, h):
             cols = slice(BANK * h, BANK * (h + 1))
-            products = work.tile([P, BANK], F32, name="products", tag="wide", bufs=3)
+            products = work.tile([P, BANK], F32, name="products", tag="wide", bufs=WIDE_BUFS)
             nc.vector.scalar_tensor_tensor(
                 out=products[:],
-                in0=banks["target", i, h][:] if from_psum else target_sb[i][:, cols],
+                in0=target_sb[i][:, cols],
                 scalar=-1.0 / J,
                 in1=logs[i][:, cols],
                 op0=ALU.mult,
@@ -435,8 +422,8 @@ def tile_c51_shifted_log_loss_s3_kernel(
             log(4)
             for b in range(2):
                 turn_x(3, b)
-            for h in range(2):
-                group_w(h)
+            group_w(nc.scalar.copy, slice(0, W_ON_SCALAR))
+            group_w(nc.vector.tensor_copy, slice(W_ON_SCALAR, F))
             for b in range(2):
                 leave_x(3, b)
             rest_passes(1, 1)
@@ -444,11 +431,11 @@ def tile_c51_shifted_log_loss_s3_kernel(
                 rest_passes(2, h)
             for i in (5, 6, 7):
                 log(i)
-            quantise_w(0)
             quantise_x(3)
-            quantise_w(1)
+            quantise_w()
             scale_x(4)
             turn_xo(1, 0)
+
             for i in range(HELD):
                 for h in range(2):
                     out_pass(i, h)
@@ -465,8 +452,8 @@ def tile_c51_shifted_log_loss_s3_kernel(
                 leave_x(4, b)
             logits(3, 1)
             weigh(0)
-            quantise_x(4)
             weigh(1)
+            quantise_x(4)
             quantise_xo_pair(1, 0)
             for h in range(2):
                 exp(2, h)
@@ -564,17 +551,13 @@ def tile_c51_shifted_log_loss_s3_kernel(
             reduce_half(5, 0)
             quantise_mass_pass(last, 1)
             project(last - 1)
-            for g in range(2):
-                for h in (0, 1):
+            for g in range(MASS_PASSES):
+                for h in range(2):
                     project_pass(last, h, g)
             reduce_half(5, 1)
-            store_half(last - 1, 0)
-            store_half(last - 1, 1)
-            reduce_half(last - 1, 0)
-            reduce_half(last - 1, 1)
-            store_half(last, 0)
-            store_half(last, 1)
-            reduce_half(last, 0)
-            reduce_half(last, 1)
+            for i in (last - 1, last):
+                store_target(i)
+                for h in range(2):
+                    reduce_half(i, h)
             nc.vector.tensor_tensor(out=row_loss[:, SPLIT_FROM:], in0=half_loss[:, 0], in1=half_loss[:, 1], op=ALU.add)
             nc.sync.dma_start(out=loss.rearrange("(r i) -> r i", i=TILES), in_=row_loss[:])

@@ -23,14 +23,10 @@ PASS = 512
 BANK = 512
 REST_PASSES = KR // PASS
 MASS_PASSES = F // PASS
-QUAD = 4
+QUAD = 2
 HELD = 3
-SORTED_FROM = TILES - 2
-SPLIT_FROM = TILES - 3
-FIRST_LOG = 512
-W_ON_SCALAR = 192
+SLOTS = 7
 WIDE_BUFS = 3
-GROUP_BUFS = 4
 MASS_CODE_BUFS = 3
 TARGET_BUFS = 5
 
@@ -47,17 +43,14 @@ def tile_c51_shifted_log_loss_s3_kernel(
         def kept(shape, dtype, name):
             return keep.tile(shape, dtype, name=name, tag=name, align_bytes=64)
 
-        x_first = [kept([P, KR], U8, "x_bytes%d" % i) for i in range(2)]
-        x_pairs = [kept([P, 2, KR], U8, "x_bytes_pair%d" % a) for a in range(1, TILES // 2)]
-        x_bytes = [t[:] for t in x_first] + [t[:, c] for t in x_pairs for c in range(2)]
+        x_bytes = [kept([P, KR], U8, "x_bytes%d" % i) for i in range(TILES)]
         k_scale = kept([P, REST_PASSES, 8], F32, "k_scale")
-        k_scale_rows = kept([P, KR], F32, "k_scale_rows")
+        one = kept([P, 1], F32, "one")
         base = [kept([P, 2, 2 * F], U8, "base%d" % b) for b in range(2)]
         base_sc = kept([P, REST_PASSES, F], U8, "base_sc")
         proj = kept([P, MASS_PASSES, 2 * J], U8, "proj")
         proj_sc = kept([P, MASS_PASSES, J], U8, "proj_sc")
         w_rows = kept([P, 4, F], BF16, "w_rows")
-        w_groups = kept([P, F, 4], BF16, "w_groups")
         w_codes = kept([P, F], U32, "w_codes")
         w_sc = kept([P, F], U8, "w_sc")
         xo = [kept([P, QUAD, KO], BF16, "xo%d" % a) for a in range(TILES // QUAD)]
@@ -65,9 +58,10 @@ def tile_c51_shifted_log_loss_s3_kernel(
         onl = [t[:, c] for t in onl_pairs for c in range(2)]
         logs = [kept([P, J], F32, "logs%d" % i) for i in range(TILES)]
         spacing_rows = kept([P, F], BF16, "spacing_rows")
+        spacing_sorted = kept([P, F], BF16, "spacing_sorted")
         ident = kept([P, P], F32, "ident")
         row_loss = kept([P, TILES], F32, "row_loss")
-        half_loss = kept([P, 2, TILES - SPLIT_FROM], F32, "half_loss")
+        half_loss = kept([P, 2, TILES], F32, "half_loss")
         x_codes = [kept([P, REST_PASSES, P], U32, "x_codes%d" % i) for i in range(TILES)]
         x_sc = [kept([P, REST_PASSES, P], U8, "x_sc%d" % i) for i in range(TILES)]
         xo_codes = [kept([P, QUAD, P], U32, "xo_codes%d" % a) for a in range(TILES // QUAD)]
@@ -78,7 +72,7 @@ def tile_c51_shifted_log_loss_s3_kernel(
         online_hbm = online.rearrange("(r i) j -> r i j", i=TILES)
         target_hbm = target.rearrange("(r i) j -> r i j", i=TILES)
 
-        scaled, sorted_pairs, groups, exps, mass, mass_codes, mass_sc, target_sb = {}, {}, {}, {}, {}, {}, {}, {}
+        wide, is_sorted, groups, exps, mass, mass_codes, mass_sc, target_sb = {}, {}, {}, {}, {}, {}, {}, {}
 
         free_banks = list(range(8))
         bank_of, banks = {}, {}
@@ -94,11 +88,31 @@ def tile_c51_shifted_log_loss_s3_kernel(
             free_banks.append(bank_of[key])
             return banks[key]
 
-        def load_x(i):
-            nc.sync.dma_start(out=x_bytes[i], in_=x_hbm[:, i, :])
+        free_slots = list(range(SLOTS))
+        slot_of = {}
 
-        def load_x_pair(a):
-            nc.sync.dma_start(out=x_pairs[a - 1][:], in_=x_hbm[:, 2 * a : 2 * a + 2, :])
+        def take_slot(key, width, newest=False):
+            n = free_slots[-1] if newest else free_slots[0]
+            free_slots.remove(n)
+            slot_of[key] = n
+            groups[key] = keep.tile([P, width], BF16, name="slot%d" % n, tag="slot%d" % n, align_bytes=64)
+            return groups[key]
+
+        def free_slot(key):
+            free_slots.append(slot_of[key])
+            return groups[key]
+
+        def load_x(i):
+            nc.sync.dma_start(out=x_bytes[i][:], in_=x_hbm[:, i, :])
+
+        def load_k_scale():
+            nc.sync.dma_start(out=k_scale[:, :, 0:4], in_=x_rest_scale.rearrange("o (g p t) -> p (o g) t", p=P, t=4))
+
+        def load_spacing():
+            nc.sync.dma_start(out=spacing_rows[:], in_=spacing.partition_broadcast(P))
+
+        def load_proj():
+            nc.sync.dma_start(out=proj[:], in_=proj_words.rearrange("g p n -> p g n"))
 
         def load_online_pair(a):
             nc.sync.dma_start(out=onl_pairs[a][:], in_=online_hbm[:, 2 * a : 2 * a + 2, :])
@@ -112,6 +126,9 @@ def tile_c51_shifted_log_loss_s3_kernel(
         def load_base(b):
             nc.sync.dma_start(out=base[b][:], in_=base_words.rearrange("g p n -> p g n")[:, 2 * b : 2 * b + 2, :])
 
+        def load_w(cols=slice(0, F)):
+            nc.sync.dma_start(out=w_rows[:, :, cols], in_=w_out.rearrange("(p t) n -> p t n", t=4)[:, :, cols])
+
         def load_scale_bytes(tile, rows):
             for j in range(4):
                 nc.sync.dma_start(
@@ -122,47 +139,48 @@ def tile_c51_shifted_log_loss_s3_kernel(
         def log(i, cols=slice(0, J)):
             nc.scalar.activation(out=logs[i][:, cols], in_=onl[i][:, cols], func=ACT.Ln)
 
-        def spread_scale(g):
-            bank = take_bank(("scale", g), [P, 4, P])
-            for t in range(4):
-                nc.tensor.transpose(bank[:, t, :], k_scale[:, g, t : t + 1].to_broadcast([P, P]), ident[:])
-            leave = nc.vector.tensor_copy if g == 0 else nc.scalar.copy
-            leave(
-                out=k_scale_rows[:, PASS * g : PASS * (g + 1)].rearrange("r (p t) -> r p t", t=4),
-                in_=give_back(("scale", g))[:].rearrange("r t p -> r p t"),
-            )
-
-        def scale_x(i, g0=0, g1=REST_PASSES):
-            if g0 == 0:
-                scaled[i] = work.tile([P, KR], BF16, name="scaled", tag="wide", bufs=WIDE_BUFS)
-            cols = slice(PASS * g0, PASS * g1)
-            nc.vector.tensor_tensor(out=scaled[i][:, cols], in0=x_bytes[i][:, cols].bitcast(FP8), in1=k_scale_rows[:, cols], op=ALU.mult)
-
-        def sort_x(i):
-            pairs = work.tile([P, REST_PASSES, 2, P], F32, name="sorted", tag="sorted", bufs=1)
-            nc.scalar.copy(out=pairs[:], in_=scaled[i][:].bitcast(F32).rearrange("r (g p u) -> r g u p", g=REST_PASSES, u=2))
-            for b in range(2):
-                sorted_pairs[i, b] = pairs[:, 2 * b : 2 * b + 2]
+        def widen(i, b, on_scalar=False):
+            if i not in wide:
+                wide[i] = work.tile([P, KR], BF16, name="wide", tag="wide", bufs=WIDE_BUFS)
+            is_sorted[i, b] = not on_scalar
+            cols = slice(2 * PASS * b, 2 * PASS * (b + 1))
+            if on_scalar:
+                nc.scalar.copy(out=wide[i][:, cols], in_=x_bytes[i][:, cols].bitcast(FP8))
+            else:
+                nc.vector.tensor_scalar(
+                    out=wide[i][:, cols].rearrange("r (u gp e) -> r gp u e", u=2, e=2),
+                    in0=x_bytes[i][:, cols].bitcast(FP8).rearrange("r (gp u e) -> r gp u e", u=2, e=2),
+                    scalar1=one[:],
+                    scalar2=None,
+                    op0=ALU.mult,
+                )
 
         def turn_x(i, b):
             bank = take_bank(("x", i, b), [P, 2, 2, P])
-            pairs = scaled[i][:].bitcast(F32)
+            pairs = wide[i][:, 2 * PASS * b : 2 * PASS * (b + 1)].bitcast(F32)
             for gg in range(2):
-                first = (PASS // 2) * (2 * b + gg)
                 for u in range(2):
-                    src = sorted_pairs[i, b][:, gg, u, :] if i >= SORTED_FROM else pairs[:, first + u : first + PASS // 2 : 2]
+                    first = P * (2 * u + gg)
+                    src = pairs[:, first : first + P] if is_sorted[i, b] else pairs[:, 2 * P * gg + u : 2 * P * (gg + 1) : 2]
                     nc.tensor.transpose(bank[:, u, gg, :], src, ident[:])
+
+        def scale_x(i, b):
+            if b == 0:
+                take_slot(("x", i), 4 * PASS)
+            nc.vector.tensor_tensor(
+                out=groups["x", i][:, 2 * PASS * b : 2 * PASS * (b + 1)].rearrange("p (c r u e) -> p c r u e", c=2, u=2, e=2),
+                in0=give_back(("x", i, b))[:].bitcast(BF16).rearrange("p u c (r e) -> p c r u e", e=2),
+                in1=k_scale[:, 2 * b : 2 * b + 2, 0:4].rearrange("p c (u e) -> p c u e", e=2).unsqueeze(2).to_broadcast([P, 2, P, 2, 2]),
+                op=ALU.mult,
+            )
 
         def leave_bank(key, into, n, parts):
             if n == 0:
-                groups[into] = work.tile([P, parts * 2 * PASS], BF16, name="groups", tag="groups", bufs=GROUP_BUFS, align_bytes=64)
+                take_slot(into, parts * 2 * PASS)
             nc.scalar.copy(
                 out=groups[into][:, 2 * PASS * n : 2 * PASS * (n + 1)].bitcast(F32).rearrange("p (c r u) -> p c r u", c=2, u=2),
                 in_=give_back(key)[:].rearrange("p u c r -> p c r u"),
             )
-
-        def leave_x(i, b):
-            leave_bank(("x", i, b), ("x", i), b, 2)
 
         def quantise_x(i, g0=0, g1=REST_PASSES):
             nc.vector.quantize_mx(
@@ -170,42 +188,46 @@ def tile_c51_shifted_log_loss_s3_kernel(
                 scales=x_sc[i][:, g0:g1].rearrange("p g r -> p (g r)"),
                 in_=groups["x", i][:, PASS * g0 : PASS * g1],
             )
+            if g1 == REST_PASSES:
+                free_slot(("x", i))
 
-        def turn_xo(a, b):
-            bank = take_bank(("xo", a, b), [P, 2, 2, P])
+        def turn_xo(a):
+            bank = take_bank(("xo", a), [P, 2, 2, P])
             for c in range(2):
-                pairs = xo[a][:, 2 * b + c, :].bitcast(F32)
+                pairs = xo[a][:, c, :].bitcast(F32)
                 for u in range(2):
                     nc.tensor.transpose(bank[:, u, c, :], pairs[:, u::2], ident[:])
 
-        def leave_xo(a, b):
-            leave_bank(("xo", a, b), ("xo", a), b, 2)
+        def leave_xo(a):
+            leave_bank(("xo", a), ("xo", a), 0, 1)
 
         def quantise_xo(a):
             nc.vector.quantize_mx(
                 out=xo_codes[a][:].rearrange("p i r -> p (i r)").bitcast(FP8X4),
                 scales=xo_sc[a][:].rearrange("p i r -> p (i r)"),
-                in_=groups["xo", a][:],
+                in_=free_slot(("xo", a))[:],
             )
 
-        def leave_xo_pair(a, b):
-            leave_bank(("xo", a, b), ("xo", a, b), 0, 1)
+        def group_w(engine, c0, c1):
+            piece = take_slot(("w", c0), 4 * (c1 - c0), newest=engine == "gpsimd")
+            if engine == "gpsimd":
+                nc.gpsimd.tensor_scalar(
+                    out=piece[:].rearrange("p (n t) -> p n t", t=4),
+                    in0=w_rows[:, :, c0:c1].rearrange("p t n -> p n t"),
+                    scalar1=1.0,
+                    scalar2=0.0,
+                    op0=ALU.mult,
+                    op1=ALU.add,
+                )
+            else:
+                copy = nc.scalar.copy if engine == "scalar" else nc.vector.tensor_copy
+                copy(
+                    out=piece[:].rearrange("p (c i t) -> p c t i", i=4, t=4),
+                    in_=w_rows[:, :, c0:c1].rearrange("p t (c i) -> p c t i", i=4),
+                )
 
-        def quantise_xo_pair(a, b):
-            nc.vector.quantize_mx(
-                out=xo_codes[a][:, 2 * b : 2 * b + 2].rearrange("p i r -> p (i r)").bitcast(FP8X4),
-                scales=xo_sc[a][:, 2 * b : 2 * b + 2].rearrange("p i r -> p (i r)"),
-                in_=groups["xo", a, b][:],
-            )
-
-        def group_w(copy, cols):
-            copy(
-                out=w_groups[:, cols].rearrange("p (c i) t -> p c t i", i=4),
-                in_=w_rows[:, :, cols].rearrange("p t (c i) -> p c t i", i=4),
-            )
-
-        def quantise_w():
-            nc.vector.quantize_mx(out=w_codes[:].bitcast(FP8X4), scales=w_sc[:], in_=w_groups[:].rearrange("p n t -> p (n t)"))
+        def quantise_w(c0, c1):
+            nc.vector.quantize_mx(out=w_codes[:, c0:c1].bitcast(FP8X4), scales=w_sc[:, c0:c1], in_=free_slot(("w", c0))[:])
 
         def rest_pass(i, h, g):
             if g == 0:
@@ -246,21 +268,36 @@ def tile_c51_shifted_log_loss_s3_kernel(
                 out=exps[i][:, :, h], in_=give_back(("logits", i, h))[:].rearrange("r (p u e) -> r u p e", u=2, e=2), func=ACT.Exp
             )
 
-        def weigh(i, h0=0, h1=MASS_PASSES):
-            if h0 == 0:
-                mass[i] = work.tile([P, 2, MASS_PASSES, P, 2], BF16, name="mass", tag="mass", bufs=HELD + 1)
+        def sort_spacing():
+            nc.scalar.copy(
+                out=spacing_sorted[:].bitcast(F32).rearrange("r (u gp) -> r u gp", u=2),
+                in_=spacing_rows[:].bitcast(F32).rearrange("r (gp u) -> r u gp", u=2),
+            )
+
+        def weigh(i, on_gpsimd=False):
+            mass[i] = take_slot(("m", i), F, newest=on_gpsimd)
+            engine = nc.gpsimd if on_gpsimd else nc.vector
+            engine.tensor_tensor(out=mass[i][:], in0=exps[i][:].rearrange("r u g p e -> r (u g p e)"), in1=spacing_sorted[:], op=ALU.mult)
+
+        def weigh_pass(i, g):
+            if g == 0:
+                mass[i] = take_slot(("m", i), F)
             nc.vector.tensor_tensor(
-                out=mass[i][:, :, h0:h1].rearrange("r u g p e -> r u (g p) e"),
-                in0=exps[i][:, :, h0:h1].rearrange("r u g p e -> r u (g p) e"),
-                in1=spacing_rows[:, PASS * h0 : PASS * h1].rearrange("r (gp u e) -> r u gp e", u=2, e=2),
+                out=mass[i][:].rearrange("r (u g c) -> r u g c", u=2, g=MASS_PASSES)[:, :, g],
+                in0=exps[i][:, :, g].rearrange("r u p e -> r u (p e)"),
+                in1=spacing_sorted[:].rearrange("r (u g c) -> r u g c", u=2, g=MASS_PASSES)[:, :, g],
                 op=ALU.mult,
             )
+
+        def mass_pairs(i, g, u):
+            return mass[i][:].bitcast(F32)[:, P * (MASS_PASSES * u + g) : P * (MASS_PASSES * u + g + 1)]
 
         def turn_mass(i):
             bank = take_bank(("mass", i), [P, 2, MASS_PASSES, P])
             for g in range(MASS_PASSES):
                 for u in range(2):
-                    nc.tensor.transpose(bank[:, u, g, :], mass[i][:, u, g].rearrange("r p e -> r (p e)").bitcast(F32), ident[:])
+                    nc.tensor.transpose(bank[:, u, g, :], mass_pairs(i, g, u), ident[:])
+            free_slot(("m", i))
 
         def leave_mass(tiles):
             for n, i in enumerate(tiles):
@@ -274,30 +311,19 @@ def tile_c51_shifted_log_loss_s3_kernel(
             nc.vector.quantize_mx(
                 out=codes[:].rearrange("p i g r -> p (i g r)").bitcast(FP8X4),
                 scales=scales[:].rearrange("p i g r -> p (i g r)"),
-                in_=groups["mass", tiles][:],
-            )
-
-        def reduce_loss(i):
-            products = work.tile([P, J], F32, name="products", tag="wide", bufs=WIDE_BUFS)
-            nc.vector.scalar_tensor_tensor(
-                out=products[:],
-                in0=target_sb[i][:],
-                scalar=-1.0 / J,
-                in1=logs[i][:],
-                op0=ALU.mult,
-                op1=ALU.mult,
-                accum_out=row_loss[:, i : i + 1],
+                in_=free_slot(("mass", tiles))[:],
             )
 
         def turn_mass_pass(i, g):
             bank = take_bank(("mass", i, g), [P, 2, P])
             for u in range(2):
-                nc.tensor.transpose(bank[:, u, :], mass[i][:, u, g].rearrange("r p e -> r (p e)").bitcast(F32), ident[:])
+                nc.tensor.transpose(bank[:, u, :], mass_pairs(i, g, u), ident[:])
+            if g == MASS_PASSES - 1:
+                free_slot(("m", i))
 
         def leave_mass_pass(i, g):
-            groups["mass", i, g] = work.tile([P, PASS], BF16, name="groups", tag="groups", bufs=GROUP_BUFS, align_bytes=64)
             nc.scalar.copy(
-                out=groups["mass", i, g][:].bitcast(F32).rearrange("p (r u) -> p r u", u=2),
+                out=take_slot(("mass", i, g), PASS)[:].bitcast(F32).rearrange("p (r u) -> p r u", u=2),
                 in_=give_back(("mass", i, g))[:].rearrange("p u r -> p r u"),
             )
 
@@ -306,7 +332,7 @@ def tile_c51_shifted_log_loss_s3_kernel(
                 codes = work.tile([P, MASS_PASSES, P], U32, name="mass_codes", tag="mass_codes", bufs=MASS_CODE_BUFS, align_bytes=64)
                 scales = work.tile([P, MASS_PASSES, P], U8, name="mass_sc", tag="mass_sc", bufs=MASS_CODE_BUFS, align_bytes=64)
                 mass_codes[i], mass_sc[i] = codes[:], scales[:]
-            nc.vector.quantize_mx(out=mass_codes[i][:, g].bitcast(FP8X4), scales=mass_sc[i][:, g], in_=groups["mass", i, g][:])
+            nc.vector.quantize_mx(out=mass_codes[i][:, g].bitcast(FP8X4), scales=mass_sc[i][:, g], in_=free_slot(("mass", i, g))[:])
 
         def project_pass(i, h, g):
             if g == 0:
@@ -326,238 +352,226 @@ def tile_c51_shifted_log_loss_s3_kernel(
                 for g in range(MASS_PASSES):
                     project_pass(i, h, g)
 
-        def store_half(i, h):
-            if h == 0:
+        def store_half(i, h, last_reader=True):
+            if i not in target_sb:
                 target_sb[i] = work.tile([P, J], F32, name="target_sb", tag="target_sb", bufs=TARGET_BUFS)
             cols = slice(BANK * h, BANK * (h + 1))
-            nc.scalar.copy(out=target_sb[i][:, cols], in_=give_back(("target", i, h))[:])
+            bank = give_back(("target", i, h)) if last_reader else banks["target", i, h]
+            nc.scalar.copy(out=target_sb[i][:, cols], in_=bank[:])
             nc.sync.dma_start(out=target_hbm[:, i, cols], in_=target_sb[i][:, cols])
 
-        def store_target(i):
+        def store_target(i, last_reader=True):
             for h in range(2):
-                store_half(i, h)
+                store_half(i, h, last_reader)
 
-        def reduce_half(i, h):
+        def reduce_half(i, h, source):
             cols = slice(BANK * h, BANK * (h + 1))
-            products = work.tile([P, BANK], F32, name="products", tag="wide", bufs=WIDE_BUFS)
+            products = work.tile([P, BANK], F32, name="products", tag="products", bufs=2)
             nc.vector.scalar_tensor_tensor(
                 out=products[:],
-                in0=target_sb[i][:, cols],
+                in0=target_sb[i][:, cols] if source == "sbuf" else (give_back(("target", i, h)) if source == "psum_last" else banks["target", i, h])[:],
                 scalar=-1.0 / J,
                 in1=logs[i][:, cols],
                 op0=ALU.mult,
                 op1=ALU.mult,
-                accum_out=half_loss[:, h, i - SPLIT_FROM : i - SPLIT_FROM + 1],
+                accum_out=half_loss[:, h, i : i + 1],
             )
+
+        def both(step, *args):
+            for h in range(2):
+                step(args[0], h, *args[1:])
 
         with tc.manual_schedule():
             nc.vector.memset(base_sc[:].rearrange("p g n -> p (g n)").bitcast(I32), 0)
+            nc.vector.memset(one[:], 1.0)
             nc.vector.memset(proj_sc[:].rearrange("p g n -> p (g n)").bitcast(I32), 0)
             make_identity(nc, ident[:])
-
-            nc.sync.dma_start(out=k_scale[:, :, 0:4], in_=x_rest_scale.rearrange("o (g p t) -> p (o g) t", p=P, t=4))
             load_x(0)
-            load_online(0, slice(0, FIRST_LOG))
-            load_xo(0)
-            load_online(1)
+            load_k_scale()
+            load_online(0, slice(0, BANK))
             load_x(1)
-            load_online(0, slice(FIRST_LOG, J))
             load_scale_bytes(base_sc, base_scales)
-            load_x(2)
+            load_online(1)
             load_base(0)
+            load_online(0, slice(BANK, J))
             load_online(2)
-            load_x(3)
+            load_x(2)
             load_online(3)
+            load_w(slice(0, BANK))
+            load_x(3)
             load_base(1)
             load_online(4)
-            nc.sync.dma_start(out=w_rows[:], in_=w_out.rearrange("(p t) n -> p t n", t=4))
+            load_xo(0)
             load_online(5)
+            load_w(slice(BANK, F))
             load_online_pair(3)
             load_xo(1)
             load_x(4)
+            load_spacing()
             load_x(5)
-            nc.sync.dma_start(out=spacing_rows[:], in_=spacing.partition_broadcast(P))
-            load_x_pair(3)
-            nc.sync.dma_start(out=proj[:], in_=proj_words.rearrange("g p n -> p g n"))
+            load_xo(2)
+            load_x(6)
+            load_proj()
             load_scale_bytes(proj_sc, proj_scales)
+            load_x(7)
+            load_xo(3)
 
-            log(0, slice(0, FIRST_LOG))
-            for g in range(REST_PASSES):
-                spread_scale(g)
-            for g in range(REST_PASSES):
-                scale_x(0, g, g + 1)
-            log(1)
-            log(0, slice(FIRST_LOG, J))
+            log(0, slice(0, BANK))
             for b in range(2):
-                turn_xo(0, b)
-            for b in range(2):
+                widen(0, b)
                 turn_x(0, b)
             for b in range(2):
-                leave_x(0, b)
-            for b in range(2):
-                leave_xo(0, b)
-            for b in range(2):
-                scale_x(1, 2 * b, 2 * b + 2)
+                widen(1, b, True)
+                scale_x(0, b)
                 turn_x(1, b)
-                leave_x(1, b)
-            quantise_x(0)
-            scale_x(2)
+            log(1)
+            log(0, slice(BANK, J))
+            log(2)
+            log(3)
+            for b in range(2):
+                quantise_x(0, 2 * b, 2 * b + 2)
+            both(scale_x, 1)
             for g in range(2):
-                for h in range(2):
-                    rest_pass(0, h, g)
-            for i in (2, 3):
-                log(i)
-            for b in range(2):
-                turn_x(2, b)
+                both(rest_pass, 0, g)
+            both(widen, 2)
             quantise_x(1)
-            scale_x(3)
-            for b in range(2):
-                leave_x(2, b)
-            for g in range(2, 4):
-                for h in range(2):
-                    rest_pass(0, h, g)
-            rest_passes(1, 0)
-            quantise_xo(0)
-            quantise_x(2)
+            both(turn_x, 2)
+            for g in range(2):
+                both(rest_pass, 1, g)
+            group_w("gpsimd", 0, 384)
+            both(scale_x, 2)
+            both(widen, 3, True)
+            for i in range(2):
+                for g in range(2, 4):
+                    both(rest_pass, i, g)
             log(4)
-            for b in range(2):
-                turn_x(3, b)
-            group_w(nc.scalar.copy, slice(0, W_ON_SCALAR))
-            group_w(nc.vector.tensor_copy, slice(W_ON_SCALAR, F))
-            for b in range(2):
-                leave_x(3, b)
-            rest_passes(1, 1)
-            for h in range(2):
-                rest_passes(2, h)
+            group_w("vector", 384, BANK)
+            quantise_w(0, 384)
+            quantise_x(2)
+            quantise_w(384, BANK)
+            turn_xo(0)
+            both(turn_x, 3)
+            leave_xo(0)
+            group_w("gpsimd", BANK, 896)
+            both(scale_x, 3)
+            both(rest_passes, 2)
             for i in (5, 6, 7):
                 log(i)
+            turn_xo(1)
+            leave_xo(1)
+            quantise_xo(0)
+            group_w("vector", 896, F)
+            quantise_w(BANK, 896)
             quantise_x(3)
-            quantise_w()
-            scale_x(4)
-            turn_xo(1, 0)
-
-            for i in range(HELD):
-                for h in range(2):
+            quantise_w(896, F)
+            for h in range(2):
+                for i in range(2):
                     out_pass(i, h)
-            logits(3, 0)
-            for h in range(2):
-                exp(0, h)
-            for b in range(2):
-                turn_x(4, b)
-            for h in range(2):
-                exp(1, h)
-            leave_xo_pair(1, 0)
-            scale_x(5)
-            for b in range(2):
-                leave_x(4, b)
-            logits(3, 1)
-            weigh(0)
-            weigh(1)
+            both(widen, 4)
+            quantise_xo(1)
+            both(turn_x, 4)
+            both(out_pass, 2)
+            both(exp, 0)
+            sort_spacing()
+            both(scale_x, 4)
+            both(exp, 1)
+
+            both(logits, 3)
+            both(exp, 2)
+            both(widen, 5)
             quantise_x(4)
-            quantise_xo_pair(1, 0)
-            for h in range(2):
-                exp(2, h)
-            exp(3, 0)
+            weigh(0)
+            both(turn_x, 5)
+            turn_xo(2)
+            leave_xo(2)
+            weigh(1, True)
+            both(scale_x, 5)
 
-            for b in range(2):
-                turn_x(5, b)
-            turn_mass(0)
-            scale_x(6, 0, 2)
-            leave_mass((0,))
-            exp(3, 1)
-            for b in range(2):
-                leave_x(5, b)
-            logits(4, 0)
-            turn_mass(1)
-            turn_xo(1, 1)
-            quantise_mass((0,))
-            scale_x(6, 2, 4)
-            leave_mass((1,))
-            exp(4, 0)
-            logits(4, 1)
+            rest_passes(4, 0)
+            both(exp, 3)
+            quantise_xo(2)
+            rest_passes(4, 1)
+            both(out_pass, 4)
+            both(widen, 6, True)
             weigh(2)
-            quantise_mass((1,))
-            weigh(3)
             quantise_x(5)
-            sort_x(6)
-            exp(4, 1)
-            leave_xo_pair(1, 1)
-            for i in (0, 1):
-                project(i)
-                store_target(i)
-
-            for b in range(2):
-                turn_x(6, b)
-            for i in (2, 3):
-                turn_mass(i)
-            scale_x(7)
-            quantise_xo_pair(1, 1)
-            leave_mass((2, 3))
-            for b in range(2):
-                leave_x(6, b)
+            turn_mass(0)
+            turn_mass(1)
+            turn_x(6, 0)
+            leave_mass((0, 1))
+            both(exp, 4)
             logits(5, 0)
-            quantise_mass((2, 3))
-            weigh(4)
-            quantise_x(6)
-            exp(5, 0)
+            turn_x(6, 1)
+            turn_mass(2)
+            weigh(3, True)
+            both(scale_x, 6)
+            quantise_mass((0, 1))
             logits(5, 1)
-            exp(5, 1)
-            sort_x(7)
-            for i in (2, 3):
-                project(i)
-            store_target(2)
-            weigh(5)
-            reduce_loss(0)
-            for b in range(2):
-                turn_x(7, b)
-            for i in (4, 5):
-                turn_mass(i)
-            reduce_loss(1)
-            for b in range(2):
-                leave_x(7, b)
-            leave_mass((4, 5))
-            store_target(3)
-            logits(6, 0)
-            quantise_x(7)
-            reduce_loss(2)
-            quantise_mass((4, 5))
-            exp(6, 0)
-            logits(6, 1)
-            exp(6, 1)
+            leave_mass((2,))
+            project(0)
+            project(1)
+            both(widen, 7)
+            quantise_x(6)
+            quantise_mass((2,))
 
-            last = TILES - 1
-            logits(last, 0)
-            project(4)
-            reduce_loss(3)
+            both(exp, 5)
+            turn_xo(3)
+            both(turn_x, 7)
+            turn_mass(3)
+            store_target(0)
+            leave_xo(3)
+            weigh(4, True)
+            both(scale_x, 7)
+            leave_mass((3,))
+            rest_passes(6, 0)
+            store_target(1)
+            quantise_xo(3)
+            quantise_mass((3,))
+            quantise_x(7)
+            rest_passes(6, 1)
+            both(out_pass, 6)
+            project(2)
+            weigh(5, True)
+            both(reduce_half, 2, "psum")
+            project(3)
+            both(reduce_half, 3, "psum")
+            store_target(2)
+
+            turn_mass(4)
+            turn_mass(5)
+            both(exp, 6)
+            leave_mass((4, 5))
+            logits(7, 0)
+            both(reduce_half, 0, "sbuf")
             weigh(6)
-            exp(last, 0)
-            weigh(last, 0, 1)
-            store_target(4)
-            logits(last, 1)
-            turn_mass(last - 1)
-            turn_mass_pass(last, 0)
-            exp(last, 1)
-            reduce_loss(4)
-            weigh(last, 1, 2)
-            leave_mass((last - 1,))
-            leave_mass_pass(last, 0)
+            quantise_mass((4, 5))
+            exp(7, 0)
+            store_target(3)
+            logits(7, 1)
+            weigh_pass(7, 0)
+            turn_mass(6)
+            turn_mass_pass(7, 0)
+            exp(7, 1)
+            project(4)
+            leave_mass((6,))
+            leave_mass_pass(7, 0)
+            both(reduce_half, 1, "sbuf")
+            weigh_pass(7, 1)
             project(5)
-            quantise_mass((last - 1,))
-            quantise_mass_pass(last, 0)
-            store_half(5, 0)
-            turn_mass_pass(last, 1)
-            store_half(5, 1)
-            leave_mass_pass(last, 1)
-            reduce_half(5, 0)
-            quantise_mass_pass(last, 1)
-            project(last - 1)
+            turn_mass_pass(7, 1)
+            quantise_mass((6,))
+            quantise_mass_pass(7, 0)
+            store_target(4)
+            leave_mass_pass(7, 1)
+            both(reduce_half, 4, "sbuf")
+            quantise_mass_pass(7, 1)
+            project(6)
+            store_target(5)
             for g in range(MASS_PASSES):
-                for h in range(2):
-                    project_pass(last, h, g)
-            reduce_half(5, 1)
-            for i in (last - 1, last):
+                both(project_pass, 7, g)
+            both(reduce_half, 5, "sbuf")
+            for i in (6, 7):
                 store_target(i)
-                for h in range(2):
-                    reduce_half(i, h)
-            nc.vector.tensor_tensor(out=row_loss[:, SPLIT_FROM:], in0=half_loss[:, 0], in1=half_loss[:, 1], op=ALU.add)
+                both(reduce_half, i, "sbuf")
+            nc.vector.tensor_tensor(out=row_loss[:], in0=half_loss[:, 0], in1=half_loss[:, 1], op=ALU.add)
             nc.sync.dma_start(out=loss.rearrange("(r i) -> r i", i=TILES), in_=row_loss[:])

@@ -24,11 +24,10 @@ BANK = 512
 REST_PASSES = KR // PASS
 MASS_PASSES = F // PASS
 QUAD = 2
-HELD = 3
-SLOTS = 7
-WIDE_BUFS = 3
-MASS_CODE_BUFS = 3
-TARGET_BUFS = 5
+SLOTS = 12
+WIDE_BUFS = 4
+MASS_CODE_BUFS = 4
+TARGET_BUFS = 4
 
 
 def tile_c51_shifted_log_loss_s3_kernel(
@@ -91,11 +90,11 @@ def tile_c51_shifted_log_loss_s3_kernel(
         free_slots = list(range(SLOTS))
         slot_of = {}
 
-        def take_slot(key, width, newest=False):
+        def take_slot(key, width, newest=False, dtype=BF16):
             n = free_slots[-1] if newest else free_slots[0]
             free_slots.remove(n)
             slot_of[key] = n
-            groups[key] = keep.tile([P, width], BF16, name="slot%d" % n, tag="slot%d" % n, align_bytes=64)
+            groups[key] = keep.tile([P, width], dtype, name="slot%d" % n, tag="slot%d" % n, align_bytes=64)
             return groups[key]
 
         def free_slot(key):
@@ -174,10 +173,10 @@ def tile_c51_shifted_log_loss_s3_kernel(
                 op=ALU.mult,
             )
 
-        def leave_bank(key, into, n, parts):
+        def leave_bank(key, into, n, parts, copy=nc.scalar.copy):
             if n == 0:
                 take_slot(into, parts * 2 * PASS)
-            nc.scalar.copy(
+            copy(
                 out=groups[into][:, 2 * PASS * n : 2 * PASS * (n + 1)].bitcast(F32).rearrange("p (c r u) -> p c r u", c=2, u=2),
                 in_=give_back(key)[:].rearrange("p u c r -> p c r u"),
             )
@@ -198,8 +197,8 @@ def tile_c51_shifted_log_loss_s3_kernel(
                 for u in range(2):
                     nc.tensor.transpose(bank[:, u, c, :], pairs[:, u::2], ident[:])
 
-        def leave_xo(a):
-            leave_bank(("xo", a), ("xo", a), 0, 1)
+        def leave_xo(a, copy=nc.scalar.copy):
+            leave_bank(("xo", a), ("xo", a), 0, 1, copy)
 
         def quantise_xo(a):
             nc.vector.quantize_mx(
@@ -263,7 +262,7 @@ def tile_c51_shifted_log_loss_s3_kernel(
 
         def exp(i, h):
             if h == 0:
-                exps[i] = work.tile([P, 2, MASS_PASSES, P, 2], F32, name="exps", tag="exps", bufs=HELD + 1)
+                exps[i] = take_slot(("e", i), F, dtype=F32)[:].rearrange("r (u g p e) -> r u g p e", u=2, g=MASS_PASSES, e=2)
             nc.scalar.activation(
                 out=exps[i][:, :, h], in_=give_back(("logits", i, h))[:].rearrange("r (p u e) -> r u p e", u=2, e=2), func=ACT.Exp
             )
@@ -277,7 +276,7 @@ def tile_c51_shifted_log_loss_s3_kernel(
         def weigh(i, on_gpsimd=False):
             mass[i] = take_slot(("m", i), F, newest=on_gpsimd)
             engine = nc.gpsimd if on_gpsimd else nc.vector
-            engine.tensor_tensor(out=mass[i][:], in0=exps[i][:].rearrange("r u g p e -> r (u g p e)"), in1=spacing_sorted[:], op=ALU.mult)
+            engine.tensor_tensor(out=mass[i][:], in0=free_slot(("e", i))[:], in1=spacing_sorted[:], op=ALU.mult)
 
         def weigh_pass(i, g):
             if g == 0:
@@ -299,9 +298,9 @@ def tile_c51_shifted_log_loss_s3_kernel(
                     nc.tensor.transpose(bank[:, u, g, :], mass_pairs(i, g, u), ident[:])
             free_slot(("m", i))
 
-        def leave_mass(tiles):
+        def leave_mass(tiles, copy=nc.scalar.copy):
             for n, i in enumerate(tiles):
-                leave_bank(("mass", i), ("mass", tiles), n, len(tiles))
+                leave_bank(("mass", i), ("mass", tiles), n, len(tiles), copy)
 
         def quantise_mass(tiles):
             codes = work.tile([P, len(tiles), MASS_PASSES, P], U32, name="mass_codes", tag="mass_codes", bufs=MASS_CODE_BUFS, align_bytes=64)
@@ -390,188 +389,312 @@ def tile_c51_shifted_log_loss_s3_kernel(
             load_k_scale()
             load_online(0, slice(0, BANK))
             load_x(1)
-            load_scale_bytes(base_sc, base_scales)
-            load_online(1)
-            load_base(0)
-            load_online(0, slice(BANK, J))
-            load_online(2)
             load_x(2)
-            load_online(3)
-            load_w(slice(0, BANK))
+            load_scale_bytes(base_sc, base_scales)
+            load_base(0)
             load_x(3)
-            load_base(1)
-            load_online(4)
             load_xo(0)
-            load_online(5)
-            load_w(slice(BANK, F))
-            load_online_pair(3)
-            load_xo(1)
             load_x(4)
-            load_spacing()
-            load_x(5)
+            load_xo(1)
+            load_w(slice(0, BANK))
+            load_online(0, slice(BANK, J))
+            load_online(1)
+            load_online(2)
+            load_base(1)
             load_xo(2)
+            load_online(3)
+            load_online(4)
+            load_w(slice(BANK, F))
+            load_online(5)
+            load_online(6)
+            load_online(7)
+            load_x(5)
             load_x(6)
+            load_spacing()
+            load_xo(3)
+            load_x(7)
             load_proj()
             load_scale_bytes(proj_sc, proj_scales)
-            load_x(7)
-            load_xo(3)
-
             log(0, slice(0, BANK))
-            for b in range(2):
-                widen(0, b)
-                turn_x(0, b)
-            for b in range(2):
-                widen(1, b, True)
-                scale_x(0, b)
-                turn_x(1, b)
-            log(1)
-            log(0, slice(BANK, J))
-            log(2)
-            log(3)
-            for b in range(2):
-                quantise_x(0, 2 * b, 2 * b + 2)
-            both(scale_x, 1)
-            for g in range(2):
-                both(rest_pass, 0, g)
-            both(widen, 2)
-            quantise_x(1)
-            both(turn_x, 2)
-            for g in range(2):
-                both(rest_pass, 1, g)
-            group_w("gpsimd", 0, 384)
-            both(scale_x, 2)
-            both(widen, 3, True)
-            for i in range(2):
-                for g in range(2, 4):
-                    both(rest_pass, i, g)
-            log(4)
-            group_w("vector", 384, BANK)
-            quantise_w(0, 384)
-            quantise_x(2)
-            quantise_w(384, BANK)
+            widen(0, 0)
+            turn_x(0, 0)
+            widen(0, 1)
+            turn_x(0, 1)
+            widen(1, 1, True)
+            widen(1, 0)
+            turn_x(1, 0)
+            scale_x(0, 0)
+            turn_x(1, 1)
+            widen(2, 0, True)
+            widen(2, 1, True)
+            scale_x(0, 1)
+            turn_x(2, 0)
+            quantise_x(0, 0, 2)
+            widen(3, 0, True)
+            widen(3, 1, True)
+            scale_x(1, 0)
+            scale_x(1, 1)
+            rest_pass(0, 0, 0)
+            rest_pass(0, 0, 1)
+            rest_pass(0, 1, 0)
+            rest_pass(0, 1, 1)
+            turn_x(2, 1)
             turn_xo(0)
-            both(turn_x, 3)
+            turn_x(3, 0)
+            widen(4, 0, True)
+            widen(4, 1, True)
+            quantise_x(0, 2, 4)
+            quantise_x(1)
+            group_w("gpsimd", 0, 512)
+            scale_x(2, 0)
+            scale_x(2, 1)
             leave_xo(0)
-            group_w("gpsimd", BANK, 896)
-            both(scale_x, 3)
-            both(rest_passes, 2)
-            for i in (5, 6, 7):
-                log(i)
+            rest_pass(1, 0, 0)
+            rest_pass(1, 0, 1)
+            rest_pass(1, 1, 0)
+            rest_pass(1, 1, 1)
+            turn_x(3, 1)
             turn_xo(1)
+            scale_x(3, 0)
+            scale_x(3, 1)
+            log(0, slice(BANK, J))
+            log(1)
+            log(2)
             leave_xo(1)
-            quantise_xo(0)
-            group_w("vector", 896, F)
-            quantise_w(BANK, 896)
-            quantise_x(3)
-            quantise_w(896, F)
-            for h in range(2):
-                for i in range(2):
-                    out_pass(i, h)
-            both(widen, 4)
-            quantise_xo(1)
-            both(turn_x, 4)
-            both(out_pass, 2)
-            both(exp, 0)
-            sort_spacing()
-            both(scale_x, 4)
-            both(exp, 1)
-
-            both(logits, 3)
-            both(exp, 2)
-            both(widen, 5)
-            quantise_x(4)
-            weigh(0)
-            both(turn_x, 5)
+            rest_pass(0, 0, 2)
+            rest_pass(0, 0, 3)
+            rest_pass(0, 1, 2)
+            rest_pass(0, 1, 3)
+            turn_x(4, 0)
+            turn_x(4, 1)
             turn_xo(2)
-            leave_xo(2)
-            weigh(1, True)
-            both(scale_x, 5)
-
-            rest_passes(4, 0)
-            both(exp, 3)
+            rest_pass(1, 0, 2)
+            rest_pass(1, 0, 3)
+            rest_pass(1, 1, 2)
+            rest_pass(1, 1, 3)
+            quantise_x(2)
+            quantise_x(3)
+            quantise_xo(0)
+            quantise_w(0, 512)
+            log(3)
+            log(4)
+            log(5)
+            rest_pass(2, 0, 0)
+            rest_pass(2, 0, 1)
+            rest_pass(2, 0, 2)
+            rest_pass(2, 0, 3)
+            group_w("gpsimd", 512, 896)
+            leave_xo(2, nc.vector.tensor_copy)
+            scale_x(4, 0)
+            scale_x(4, 1)
+            rest_pass(2, 1, 0)
+            rest_pass(2, 1, 1)
+            rest_pass(2, 1, 2)
+            rest_pass(2, 1, 3)
+            group_w("vector", 896, 1024)
+            quantise_xo(1)
+            quantise_w(512, 896)
+            quantise_w(896, 1024)
+            quantise_x(4)
             quantise_xo(2)
-            rest_passes(4, 1)
-            both(out_pass, 4)
-            both(widen, 6, True)
-            weigh(2)
-            quantise_x(5)
+            log(6)
+            log(7)
+            rest_pass(3, 0, 0)
+            rest_pass(3, 0, 1)
+            rest_pass(3, 0, 2)
+            rest_pass(3, 0, 3)
+            out_pass(0, 0)
+            out_pass(1, 0)
+            out_pass(2, 0)
+            out_pass(3, 0)
+            out_pass(0, 1)
+            out_pass(1, 1)
+            out_pass(2, 1)
+            rest_pass(3, 1, 0)
+            rest_pass(3, 1, 1)
+            rest_pass(3, 1, 2)
+            rest_pass(3, 1, 3)
+            out_pass(3, 1)
+            widen(5, 0)
+            widen(5, 1)
+            widen(6, 0)
+            widen(6, 1)
+            exp(0, 0)
+            exp(0, 1)
+            sort_spacing()
+            exp(1, 0)
+            exp(1, 1)
+            rest_pass(4, 0, 0)
+            rest_pass(4, 0, 1)
+            rest_pass(4, 0, 2)
+            rest_pass(4, 0, 3)
+            out_pass(4, 0)
+            weigh(0)
+            weigh(1)
+            exp(2, 0)
+            exp(2, 1)
+            weigh(2, True)
+            turn_x(5, 0)
+            turn_x(5, 1)
             turn_mass(0)
+            turn_xo(3)
+            exp(3, 0)
+            exp(3, 1)
+            widen(7, 0, True)
+            widen(7, 1, True)
+            rest_pass(4, 1, 0)
+            rest_pass(4, 1, 1)
+            rest_pass(4, 1, 2)
+            rest_pass(4, 1, 3)
+            out_pass(4, 1)
+            scale_x(5, 0)
+            scale_x(5, 1)
+            leave_mass((0,), nc.vector.tensor_copy)
             turn_mass(1)
             turn_x(6, 0)
-            leave_mass((0, 1))
-            both(exp, 4)
-            logits(5, 0)
             turn_x(6, 1)
             turn_mass(2)
+            leave_mass((1,))
+            exp(4, 0)
+            exp(4, 1)
+            leave_xo(3)
+            quantise_mass((0,))
+            quantise_x(5)
+            quantise_mass((1,))
             weigh(3, True)
-            both(scale_x, 6)
-            quantise_mass((0, 1))
-            logits(5, 1)
+            scale_x(6, 0)
+            scale_x(6, 1)
+            project_pass(0, 0, 0)
+            project_pass(0, 0, 1)
+            project_pass(0, 1, 0)
+            project_pass(0, 1, 1)
+            rest_pass(5, 0, 0)
+            rest_pass(5, 0, 1)
+            rest_pass(5, 0, 2)
+            rest_pass(5, 0, 3)
+            out_pass(5, 0)
+            store_half(0, 0)
             leave_mass((2,))
-            project(0)
-            project(1)
-            both(widen, 7)
+            store_half(0, 1, False)
+            rest_pass(5, 1, 0)
+            rest_pass(5, 1, 1)
+            rest_pass(5, 1, 2)
+            rest_pass(5, 1, 3)
+            out_pass(5, 1)
+            project_pass(1, 0, 0)
+            project_pass(1, 0, 1)
+            project_pass(1, 1, 0)
+            project_pass(1, 1, 1)
+            reduce_half(0, 1, "psum_last")
+            weigh(4)
             quantise_x(6)
             quantise_mass((2,))
-
-            both(exp, 5)
-            turn_xo(3)
-            both(turn_x, 7)
-            turn_mass(3)
-            store_target(0)
-            leave_xo(3)
-            weigh(4, True)
-            both(scale_x, 7)
-            leave_mass((3,))
-            rest_passes(6, 0)
-            store_target(1)
             quantise_xo(3)
+            exp(5, 0)
+            exp(5, 1)
+            weigh(5, True)
+            turn_mass(3)
+            turn_x(7, 0)
+            turn_x(7, 1)
+            turn_mass(4)
+            scale_x(7, 0)
+            scale_x(7, 1)
+            leave_mass((3,))
+            leave_mass((4,))
+            store_half(1, 0)
+            store_half(1, 1, False)
+            reduce_half(1, 1, "psum_last")
+            rest_pass(6, 0, 0)
+            rest_pass(6, 0, 1)
+            rest_pass(6, 0, 2)
+            rest_pass(6, 0, 3)
+            out_pass(6, 0)
+            project_pass(2, 0, 0)
+            project_pass(2, 0, 1)
+            project_pass(2, 1, 0)
+            project_pass(2, 1, 1)
+            rest_pass(6, 1, 0)
+            rest_pass(6, 1, 1)
+            rest_pass(6, 1, 2)
+            rest_pass(6, 1, 3)
+            out_pass(6, 1)
             quantise_mass((3,))
             quantise_x(7)
-            rest_passes(6, 1)
-            both(out_pass, 6)
-            project(2)
-            weigh(5, True)
-            both(reduce_half, 2, "psum")
-            project(3)
-            both(reduce_half, 3, "psum")
-            store_target(2)
-
-            turn_mass(4)
-            turn_mass(5)
-            both(exp, 6)
-            leave_mass((4, 5))
-            logits(7, 0)
-            both(reduce_half, 0, "sbuf")
-            weigh(6)
-            quantise_mass((4, 5))
+            reduce_half(0, 0, "sbuf")
+            reduce_half(1, 0, "sbuf")
+            quantise_mass((4,))
+            exp(6, 0)
+            store_half(2, 0, False)
+            store_half(2, 1, False)
+            exp(6, 1)
+            weigh(6, True)
+            reduce_half(2, 0, "psum_last")
+            reduce_half(2, 1, "psum_last")
+            project_pass(3, 0, 0)
+            project_pass(3, 0, 1)
+            project_pass(3, 1, 0)
+            project_pass(3, 1, 1)
+            rest_pass(7, 0, 0)
+            rest_pass(7, 0, 1)
+            rest_pass(7, 0, 2)
+            rest_pass(7, 0, 3)
+            out_pass(7, 0)
+            store_half(3, 0, False)
+            store_half(3, 1, False)
+            reduce_half(3, 0, "psum_last")
+            reduce_half(3, 1, "psum_last")
             exp(7, 0)
-            store_target(3)
-            logits(7, 1)
+            project_pass(4, 0, 0)
+            project_pass(4, 0, 1)
+            project_pass(4, 1, 0)
+            project_pass(4, 1, 1)
             weigh_pass(7, 0)
+            turn_mass(5)
             turn_mass(6)
             turn_mass_pass(7, 0)
-            exp(7, 1)
-            project(4)
+            rest_pass(7, 1, 0)
+            rest_pass(7, 1, 1)
+            rest_pass(7, 1, 2)
+            rest_pass(7, 1, 3)
+            out_pass(7, 1)
+            store_half(4, 0, False)
+            leave_mass((5,))
             leave_mass((6,))
             leave_mass_pass(7, 0)
-            both(reduce_half, 1, "sbuf")
-            weigh_pass(7, 1)
-            project(5)
-            turn_mass_pass(7, 1)
+            store_half(4, 1, False)
+            quantise_mass((5,))
+            reduce_half(4, 0, "psum_last")
             quantise_mass((6,))
             quantise_mass_pass(7, 0)
-            store_target(4)
+            exp(7, 1)
+            reduce_half(4, 1, "psum_last")
+            weigh_pass(7, 1)
+            project_pass(5, 0, 0)
+            project_pass(5, 0, 1)
+            project_pass(5, 1, 0)
+            project_pass(5, 1, 1)
+            project_pass(6, 0, 0)
+            project_pass(6, 0, 1)
+            turn_mass_pass(7, 1)
+            store_half(5, 0, False)
+            store_half(5, 1, False)
             leave_mass_pass(7, 1)
-            both(reduce_half, 4, "sbuf")
+            reduce_half(5, 0, "psum_last")
+            reduce_half(5, 1, "psum_last")
             quantise_mass_pass(7, 1)
-            project(6)
-            store_target(5)
-            for g in range(MASS_PASSES):
-                both(project_pass, 7, g)
-            both(reduce_half, 5, "sbuf")
-            for i in (6, 7):
-                store_target(i)
-                both(reduce_half, i, "sbuf")
+            project_pass(6, 1, 0)
+            project_pass(6, 1, 1)
+            project_pass(7, 0, 0)
+            project_pass(7, 1, 0)
+            project_pass(7, 0, 1)
+            project_pass(7, 1, 1)
+            store_half(6, 0, False)
+            store_half(6, 1, False)
+            store_half(7, 0, False)
+            store_half(7, 1, False)
+            reduce_half(6, 0, "psum_last")
+            reduce_half(6, 1, "psum_last")
+            reduce_half(7, 0, "psum_last")
+            reduce_half(7, 1, "psum_last")
             nc.vector.tensor_tensor(out=row_loss[:], in0=half_loss[:, 0], in1=half_loss[:, 1], op=ALU.add)
             nc.sync.dma_start(out=loss.rearrange("(r i) -> r i", i=TILES), in_=row_loss[:])

@@ -24,10 +24,11 @@ BANK = 512
 REST_PASSES = KR // PASS
 MASS_PASSES = F // PASS
 QUAD = 2
+FIRST_LOG = 128
 SLOTS = 12
 WIDE_BUFS = 4
 MASS_CODE_BUFS = 4
-TARGET_BUFS = 4
+TARGET_BUFS = 6
 
 
 def tile_c51_shifted_log_loss_s3_kernel(
@@ -118,6 +119,12 @@ def tile_c51_shifted_log_loss_s3_kernel(
 
         def load_online(i, cols=slice(0, J)):
             nc.sync.dma_start(out=onl[i][:, cols], in_=online_hbm[:, i, cols])
+
+        def load_online_rest():
+            nc.sync.dma_start(
+                out=onl_pairs[0][:].rearrange("r i j -> r (i j)")[:, FIRST_LOG:],
+                in_=online.rearrange("(r i) j -> r (i j)", i=TILES)[:, FIRST_LOG : 2 * J],
+            )
 
         def load_xo(a):
             nc.sync.dma_start(out=xo[a][:], in_=xo_hbm[:, QUAD * a : QUAD * (a + 1), :])
@@ -376,6 +383,10 @@ def tile_c51_shifted_log_loss_s3_kernel(
                 accum_out=half_loss[:, h, i : i + 1],
             )
 
+        def warm_up(n):
+            take_bank(("warm", n), [P, 2, P])
+            nc.tensor.matmul(give_back(("warm", n))[:], lhsT=ident[:], rhs=ident[:].unsqueeze(1).to_broadcast([P, 2, P]), start=True, stop=True)
+
         def both(step, *args):
             for h in range(2):
                 step(args[0], h, *args[1:])
@@ -387,7 +398,7 @@ def tile_c51_shifted_log_loss_s3_kernel(
             make_identity(nc, ident[:])
             load_x(0)
             load_k_scale()
-            load_online(0, slice(0, BANK))
+            load_online(0, slice(0, FIRST_LOG))
             load_x(1)
             load_x(2)
             load_scale_bytes(base_sc, base_scales)
@@ -397,10 +408,9 @@ def tile_c51_shifted_log_loss_s3_kernel(
             load_x(4)
             load_xo(1)
             load_w(slice(0, BANK))
-            load_online(0, slice(BANK, J))
-            load_online(1)
-            load_online(2)
+            load_online_rest()
             load_base(1)
+            load_online(2)
             load_xo(2)
             load_online(3)
             load_online(4)
@@ -415,7 +425,7 @@ def tile_c51_shifted_log_loss_s3_kernel(
             load_x(7)
             load_proj()
             load_scale_bytes(proj_sc, proj_scales)
-            log(0, slice(0, BANK))
+            log(0, slice(0, FIRST_LOG))
             widen(0, 0)
             turn_x(0, 0)
             widen(0, 1)
@@ -457,7 +467,7 @@ def tile_c51_shifted_log_loss_s3_kernel(
             turn_xo(1)
             scale_x(3, 0)
             scale_x(3, 1)
-            log(0, slice(BANK, J))
+            log(0, slice(FIRST_LOG, J))
             log(1)
             log(2)
             leave_xo(1)
@@ -483,7 +493,7 @@ def tile_c51_shifted_log_loss_s3_kernel(
             rest_pass(2, 0, 1)
             rest_pass(2, 0, 2)
             rest_pass(2, 0, 3)
-            group_w("gpsimd", 512, 896)
+            group_w("gpsimd", 512, 1024)
             leave_xo(2, nc.vector.tensor_copy)
             scale_x(4, 0)
             scale_x(4, 1)
@@ -491,10 +501,8 @@ def tile_c51_shifted_log_loss_s3_kernel(
             rest_pass(2, 1, 1)
             rest_pass(2, 1, 2)
             rest_pass(2, 1, 3)
-            group_w("vector", 896, 1024)
             quantise_xo(1)
-            quantise_w(512, 896)
-            quantise_w(896, 1024)
+            quantise_w(512, 1024)
             quantise_x(4)
             quantise_xo(2)
             log(6)
@@ -539,8 +547,8 @@ def tile_c51_shifted_log_loss_s3_kernel(
             turn_mass(0)
             turn_xo(3)
             exp(3, 0)
+            leave_mass((0,))
             exp(3, 1)
-            widen(7, 0, True)
             widen(7, 1, True)
             rest_pass(4, 1, 0)
             rest_pass(4, 1, 1)
@@ -549,7 +557,6 @@ def tile_c51_shifted_log_loss_s3_kernel(
             out_pass(4, 1)
             scale_x(5, 0)
             scale_x(5, 1)
-            leave_mass((0,), nc.vector.tensor_copy)
             turn_mass(1)
             turn_x(6, 0)
             turn_x(6, 1)
@@ -560,8 +567,10 @@ def tile_c51_shifted_log_loss_s3_kernel(
             leave_xo(3)
             quantise_mass((0,))
             quantise_x(5)
+            widen(7, 0)
             quantise_mass((1,))
             weigh(3, True)
+            weigh(4, True)
             scale_x(6, 0)
             scale_x(6, 1)
             project_pass(0, 0, 0)
@@ -573,25 +582,29 @@ def tile_c51_shifted_log_loss_s3_kernel(
             rest_pass(5, 0, 2)
             rest_pass(5, 0, 3)
             out_pass(5, 0)
-            store_half(0, 0)
-            leave_mass((2,))
+            project_pass(1, 0, 0)
+            project_pass(1, 0, 1)
+            project_pass(1, 1, 0)
+            project_pass(1, 1, 1)
+            store_half(0, 0, False)
             store_half(0, 1, False)
+            leave_mass((2,))
+            exp(5, 0)
+            store_half(1, 0, False)
+            store_half(1, 1, False)
+            reduce_half(0, 0, "psum_last")
+            reduce_half(0, 1, "psum_last")
+            reduce_half(1, 0, "psum_last")
+            reduce_half(1, 1, "psum_last")
             rest_pass(5, 1, 0)
             rest_pass(5, 1, 1)
             rest_pass(5, 1, 2)
             rest_pass(5, 1, 3)
             out_pass(5, 1)
-            project_pass(1, 0, 0)
-            project_pass(1, 0, 1)
-            project_pass(1, 1, 0)
-            project_pass(1, 1, 1)
-            reduce_half(0, 1, "psum_last")
-            weigh(4)
+            exp(5, 1)
             quantise_x(6)
             quantise_mass((2,))
             quantise_xo(3)
-            exp(5, 0)
-            exp(5, 1)
             weigh(5, True)
             turn_mass(3)
             turn_x(7, 0)
@@ -601,9 +614,6 @@ def tile_c51_shifted_log_loss_s3_kernel(
             scale_x(7, 1)
             leave_mass((3,))
             leave_mass((4,))
-            store_half(1, 0)
-            store_half(1, 1, False)
-            reduce_half(1, 1, "psum_last")
             rest_pass(6, 0, 0)
             rest_pass(6, 0, 1)
             rest_pass(6, 0, 2)
@@ -620,8 +630,6 @@ def tile_c51_shifted_log_loss_s3_kernel(
             out_pass(6, 1)
             quantise_mass((3,))
             quantise_x(7)
-            reduce_half(0, 0, "sbuf")
-            reduce_half(1, 0, "sbuf")
             quantise_mass((4,))
             exp(6, 0)
             store_half(2, 0, False)
@@ -658,16 +666,16 @@ def tile_c51_shifted_log_loss_s3_kernel(
             rest_pass(7, 1, 3)
             out_pass(7, 1)
             store_half(4, 0, False)
+            reduce_half(4, 1, "psum")
+            reduce_half(4, 0, "psum_last")
             leave_mass((5,))
             leave_mass((6,))
             leave_mass_pass(7, 0)
-            store_half(4, 1, False)
+            store_half(4, 1)
             quantise_mass((5,))
-            reduce_half(4, 0, "psum_last")
             quantise_mass((6,))
             quantise_mass_pass(7, 0)
             exp(7, 1)
-            reduce_half(4, 1, "psum_last")
             weigh_pass(7, 1)
             project_pass(5, 0, 0)
             project_pass(5, 0, 1)

@@ -24,8 +24,7 @@ BANK = 512
 REST_PASSES = KR // PASS
 MASS_PASSES = F // PASS
 QUAD = 2
-FIRST_LOG = 128
-SLOTS = 12
+SLOTS = 16
 WIDE_BUFS = 4
 MASS_CODE_BUFS = 4
 TARGET_BUFS = 6
@@ -45,7 +44,6 @@ def tile_c51_shifted_log_loss_s3_kernel(
 
         x_bytes = [kept([P, KR], U8, "x_bytes%d" % i) for i in range(TILES)]
         k_scale = kept([P, REST_PASSES, 8], F32, "k_scale")
-        one = kept([P, 1], F32, "one")
         base = [kept([P, 2, 2 * F], U8, "base%d" % b) for b in range(2)]
         base_sc = kept([P, REST_PASSES, F], U8, "base_sc")
         proj = kept([P, MASS_PASSES, 2 * J], U8, "proj")
@@ -54,8 +52,7 @@ def tile_c51_shifted_log_loss_s3_kernel(
         w_codes = kept([P, F], U32, "w_codes")
         w_sc = kept([P, F], U8, "w_sc")
         xo = [kept([P, QUAD, KO], BF16, "xo%d" % a) for a in range(TILES // QUAD)]
-        onl_pairs = [kept([P, 2, J], BF16, "onl%d" % a) for a in range(TILES // 2)]
-        onl = [t[:, c] for t in onl_pairs for c in range(2)]
+        onl = [kept([P, J], BF16, "onl%d" % i) for i in range(TILES)]
         logs = [kept([P, J], F32, "logs%d" % i) for i in range(TILES)]
         spacing_rows = kept([P, F], BF16, "spacing_rows")
         spacing_sorted = kept([P, F], BF16, "spacing_sorted")
@@ -114,17 +111,8 @@ def tile_c51_shifted_log_loss_s3_kernel(
         def load_proj():
             nc.sync.dma_start(out=proj[:], in_=proj_words.rearrange("g p n -> p g n"))
 
-        def load_online_pair(a):
-            nc.sync.dma_start(out=onl_pairs[a][:], in_=online_hbm[:, 2 * a : 2 * a + 2, :])
-
         def load_online(i, cols=slice(0, J)):
             nc.sync.dma_start(out=onl[i][:, cols], in_=online_hbm[:, i, cols])
-
-        def load_online_rest():
-            nc.sync.dma_start(
-                out=onl_pairs[0][:].rearrange("r i j -> r (i j)")[:, FIRST_LOG:],
-                in_=online.rearrange("(r i) j -> r (i j)", i=TILES)[:, FIRST_LOG : 2 * J],
-            )
 
         def load_xo(a):
             nc.sync.dma_start(out=xo[a][:], in_=xo_hbm[:, QUAD * a : QUAD * (a + 1), :])
@@ -145,25 +133,24 @@ def tile_c51_shifted_log_loss_s3_kernel(
         def log(i, cols=slice(0, J)):
             nc.scalar.activation(out=logs[i][:, cols], in_=onl[i][:, cols], func=ACT.Ln)
 
-        def widen(i, b, on_scalar=False):
-            if i not in wide:
-                wide[i] = work.tile([P, KR], BF16, name="wide", tag="wide", bufs=WIDE_BUFS)
-            is_sorted[i, b] = not on_scalar
-            cols = slice(2 * PASS * b, 2 * PASS * (b + 1))
-            if on_scalar:
-                nc.scalar.copy(out=wide[i][:, cols], in_=x_bytes[i][:, cols].bitcast(FP8))
-            else:
-                nc.vector.tensor_scalar(
-                    out=wide[i][:, cols].rearrange("r (u gp e) -> r gp u e", u=2, e=2),
-                    in0=x_bytes[i][:, cols].bitcast(FP8).rearrange("r (gp u e) -> r gp u e", u=2, e=2),
-                    scalar1=one[:],
-                    scalar2=None,
-                    op0=ALU.mult,
+        def widen(i, b, engine):
+            half = take_slot(("wide", i, b), 2 * PASS, newest=engine == "gpsimd")
+            codes = x_bytes[i][:, 2 * PASS * b : 2 * PASS * (b + 1)].bitcast(FP8)
+            is_sorted[i, b] = engine != "gpsimd"
+            if engine == "vector":
+                nc.vector.tensor_copy(
+                    out=half[:].rearrange("r (u gp e) -> r gp u e", u=2, e=2), in_=codes.rearrange("r (gp u e) -> r gp u e", u=2, e=2)
                 )
+            elif engine == "scalar":
+                nc.scalar.copy(
+                    out=half[:].rearrange("r (u gp e) -> r u gp e", u=2, e=2), in_=codes.rearrange("r (gp u e) -> r u gp e", u=2, e=2)
+                )
+            else:
+                nc.gpsimd.tensor_copy(out=half[:], in_=codes)
 
         def turn_x(i, b):
             bank = take_bank(("x", i, b), [P, 2, 2, P])
-            pairs = wide[i][:, 2 * PASS * b : 2 * PASS * (b + 1)].bitcast(F32)
+            pairs = free_slot(("wide", i, b))[:].bitcast(F32)
             for gg in range(2):
                 for u in range(2):
                     first = P * (2 * u + gg)
@@ -269,41 +256,41 @@ def tile_c51_shifted_log_loss_s3_kernel(
 
         def exp(i, h):
             if h == 0:
-                exps[i] = take_slot(("e", i), F, dtype=F32)[:].rearrange("r (u g p e) -> r u g p e", u=2, g=MASS_PASSES, e=2)
+                take_slot(("e", i), F, dtype=F32)
             nc.scalar.activation(
-                out=exps[i][:, :, h], in_=give_back(("logits", i, h))[:].rearrange("r (p u e) -> r u p e", u=2, e=2), func=ACT.Exp
+                out=groups["e", i][:, PASS * h : PASS * (h + 1)].rearrange("r (u p e) -> r u p e", u=2, e=2),
+                in_=give_back(("logits", i, h))[:].rearrange("r (p u e) -> r u p e", u=2, e=2),
+                func=ACT.Exp,
             )
 
         def sort_spacing():
-            nc.scalar.copy(
-                out=spacing_sorted[:].bitcast(F32).rearrange("r (u gp) -> r u gp", u=2),
-                in_=spacing_rows[:].bitcast(F32).rearrange("r (gp u) -> r u gp", u=2),
+            nc.vector.tensor_copy(
+                out=spacing_sorted[:].bitcast(F32).rearrange("r (g u p) -> r g u p", g=MASS_PASSES, u=2),
+                in_=spacing_rows[:].bitcast(F32).rearrange("r (g p u) -> r g u p", g=MASS_PASSES, u=2),
             )
 
-        def weigh(i, on_gpsimd=False):
-            mass[i] = take_slot(("m", i), F, newest=on_gpsimd)
-            engine = nc.gpsimd if on_gpsimd else nc.vector
-            engine.tensor_tensor(out=mass[i][:], in0=free_slot(("e", i))[:], in1=spacing_sorted[:], op=ALU.mult)
-
-        def weigh_pass(i, g):
-            if g == 0:
-                mass[i] = take_slot(("m", i), F)
-            nc.vector.tensor_tensor(
-                out=mass[i][:].rearrange("r (u g c) -> r u g c", u=2, g=MASS_PASSES)[:, :, g],
-                in0=exps[i][:, :, g].rearrange("r u p e -> r u (p e)"),
-                in1=spacing_sorted[:].rearrange("r (u g c) -> r u g c", u=2, g=MASS_PASSES)[:, :, g],
-                op=ALU.mult,
-            )
+        def weigh(i, engine, g0=0, g1=MASS_PASSES):
+            cols = slice(PASS * g0, PASS * g1)
+            piece = take_slot(("m", i, g0), PASS * (g1 - g0), newest=engine == "gpsimd")
+            for g in range(g0, g1):
+                mass[i, g] = piece[:, PASS * (g - g0) : PASS * (g - g0 + 1)]
+            source = free_slot(("e", i)) if g1 == MASS_PASSES else groups["e", i]
+            (nc.gpsimd if engine == "gpsimd" else nc.vector).tensor_tensor(out=piece[:], in0=source[:, cols], in1=spacing_sorted[:, cols], op=ALU.mult)
 
         def mass_pairs(i, g, u):
-            return mass[i][:].bitcast(F32)[:, P * (MASS_PASSES * u + g) : P * (MASS_PASSES * u + g + 1)]
+            return mass[i, g].bitcast(F32)[:, P * u : P * (u + 1)]
+
+        def free_mass(i, g):
+            if ("m", i, g) in slot_of:
+                free_slot(("m", i, g))
 
         def turn_mass(i):
             bank = take_bank(("mass", i), [P, 2, MASS_PASSES, P])
             for g in range(MASS_PASSES):
                 for u in range(2):
                     nc.tensor.transpose(bank[:, u, g, :], mass_pairs(i, g, u), ident[:])
-            free_slot(("m", i))
+            for g in range(MASS_PASSES):
+                free_mass(i, g)
 
         def leave_mass(tiles, copy=nc.scalar.copy):
             for n, i in enumerate(tiles):
@@ -324,8 +311,7 @@ def tile_c51_shifted_log_loss_s3_kernel(
             bank = take_bank(("mass", i, g), [P, 2, P])
             for u in range(2):
                 nc.tensor.transpose(bank[:, u, :], mass_pairs(i, g, u), ident[:])
-            if g == MASS_PASSES - 1:
-                free_slot(("m", i))
+            free_mass(i, g)
 
         def leave_mass_pass(i, g):
             nc.scalar.copy(
@@ -383,326 +369,204 @@ def tile_c51_shifted_log_loss_s3_kernel(
                 accum_out=half_loss[:, h, i : i + 1],
             )
 
-        def warm_up(n):
-            take_bank(("warm", n), [P, 2, P])
-            nc.tensor.matmul(give_back(("warm", n))[:], lhsT=ident[:], rhs=ident[:].unsqueeze(1).to_broadcast([P, 2, P]), start=True, stop=True)
-
         def both(step, *args):
             for h in range(2):
                 step(args[0], h, *args[1:])
 
         with tc.manual_schedule():
             nc.vector.memset(base_sc[:].rearrange("p g n -> p (g n)").bitcast(I32), 0)
-            nc.vector.memset(one[:], 1.0)
             nc.vector.memset(proj_sc[:].rearrange("p g n -> p (g n)").bitcast(I32), 0)
             make_identity(nc, ident[:])
             load_x(0)
             load_k_scale()
-            load_online(0, slice(0, FIRST_LOG))
+            load_online(0)
             load_x(1)
             load_x(2)
+            load_xo(0)
+            load_xo(1)
             load_scale_bytes(base_sc, base_scales)
             load_base(0)
             load_x(3)
-            load_xo(0)
-            load_x(4)
-            load_xo(1)
-            load_w(slice(0, BANK))
-            load_online_rest()
             load_base(1)
+            load_x(4)
+            load_w(slice(0, 384))
+            load_online(1)
             load_online(2)
-            load_xo(2)
+            load_w(slice(384, 640))
             load_online(3)
             load_online(4)
-            load_w(slice(BANK, F))
-            load_online(5)
-            load_online(6)
-            load_online(7)
+            load_w(slice(640, F))
+            for i in range(5, TILES):
+                load_online(i)
             load_x(5)
-            load_x(6)
             load_spacing()
-            load_xo(3)
-            load_x(7)
+            load_x(6)
+            load_xo(2)
             load_proj()
             load_scale_bytes(proj_sc, proj_scales)
-            log(0, slice(0, FIRST_LOG))
-            widen(0, 0)
-            turn_x(0, 0)
-            widen(0, 1)
-            turn_x(0, 1)
-            widen(1, 1, True)
-            widen(1, 0)
-            turn_x(1, 0)
-            scale_x(0, 0)
-            turn_x(1, 1)
-            widen(2, 0, True)
-            widen(2, 1, True)
-            scale_x(0, 1)
-            turn_x(2, 0)
-            quantise_x(0, 0, 2)
-            widen(3, 0, True)
-            widen(3, 1, True)
-            scale_x(1, 0)
-            scale_x(1, 1)
-            rest_pass(0, 0, 0)
-            rest_pass(0, 0, 1)
-            rest_pass(0, 1, 0)
-            rest_pass(0, 1, 1)
-            turn_x(2, 1)
+            load_x(7)
+            load_xo(3)
+            log(0)
+            both(widen, 0, "vector")
+            widen(1, 0, "gpsimd")
+            widen(1, 1, "scalar")
+            widen(2, 0, "gpsimd")
+            widen(2, 1, "scalar")
+            both(turn_x, 0)
+            both(turn_x, 1)
             turn_xo(0)
-            turn_x(3, 0)
-            widen(4, 0, True)
-            widen(4, 1, True)
-            quantise_x(0, 2, 4)
-            quantise_x(1)
-            group_w("gpsimd", 0, 512)
-            scale_x(2, 0)
-            scale_x(2, 1)
-            leave_xo(0)
-            rest_pass(1, 0, 0)
-            rest_pass(1, 0, 1)
-            rest_pass(1, 1, 0)
-            rest_pass(1, 1, 1)
-            turn_x(3, 1)
+            both(scale_x, 0)
             turn_xo(1)
-            scale_x(3, 0)
-            scale_x(3, 1)
-            log(0, slice(FIRST_LOG, J))
-            log(1)
-            log(2)
+            both(turn_x, 2)
+            leave_xo(0)
             leave_xo(1)
-            rest_pass(0, 0, 2)
-            rest_pass(0, 0, 3)
-            rest_pass(0, 1, 2)
-            rest_pass(0, 1, 3)
-            turn_x(4, 0)
-            turn_x(4, 1)
-            turn_xo(2)
-            rest_pass(1, 0, 2)
-            rest_pass(1, 0, 3)
-            rest_pass(1, 1, 2)
-            rest_pass(1, 1, 3)
-            quantise_x(2)
-            quantise_x(3)
+            both(widen, 3, "scalar")
+            widen(4, 0, "scalar")
+            quantise_x(0)
+            for g in range(REST_PASSES):
+                both(rest_pass, 0, g)
+            both(scale_x, 1)
+            both(turn_x, 3)
             quantise_xo(0)
-            quantise_w(0, 512)
-            log(3)
-            log(4)
-            log(5)
-            rest_pass(2, 0, 0)
-            rest_pass(2, 0, 1)
-            rest_pass(2, 0, 2)
-            rest_pass(2, 0, 3)
-            group_w("gpsimd", 512, 1024)
-            leave_xo(2, nc.vector.tensor_copy)
-            scale_x(4, 0)
-            scale_x(4, 1)
-            rest_pass(2, 1, 0)
-            rest_pass(2, 1, 1)
-            rest_pass(2, 1, 2)
-            rest_pass(2, 1, 3)
+            quantise_x(1)
+            widen(4, 1, "gpsimd")
+            group_w("gpsimd", 0, 384)
+            both(rest_passes, 1)
+            both(scale_x, 2)
+            scale_x(3, 0)
+            quantise_x(2)
             quantise_xo(1)
-            quantise_w(512, 1024)
+            group_w("gpsimd", 384, 640)
+            both(rest_passes, 2)
+            scale_x(3, 1)
+            both(turn_x, 4)
+            for i in range(1, TILES):
+                log(i)
+            quantise_w(0, 384)
+            quantise_x(3)
+            quantise_w(384, 640)
+            group_w("gpsimd", 640, F)
+            both(scale_x, 4)
+            quantise_w(640, F)
+            for i in range(3):
+                out_pass(i, 0)
+            logits(3, 0)
+            rest_passes(3, 1)
+            for i in range(4):
+                out_pass(i, 1)
             quantise_x(4)
-            quantise_xo(2)
-            log(6)
-            log(7)
-            rest_pass(3, 0, 0)
-            rest_pass(3, 0, 1)
-            rest_pass(3, 0, 2)
-            rest_pass(3, 0, 3)
-            out_pass(0, 0)
-            out_pass(1, 0)
-            out_pass(2, 0)
-            out_pass(3, 0)
-            out_pass(0, 1)
-            out_pass(1, 1)
-            out_pass(2, 1)
-            rest_pass(3, 1, 0)
-            rest_pass(3, 1, 1)
-            rest_pass(3, 1, 2)
-            rest_pass(3, 1, 3)
-            out_pass(3, 1)
-            widen(5, 0)
-            widen(5, 1)
-            widen(6, 0)
-            widen(6, 1)
-            exp(0, 0)
-            exp(0, 1)
+            both(widen, 5, "vector")
             sort_spacing()
-            exp(1, 0)
-            exp(1, 1)
-            rest_pass(4, 0, 0)
-            rest_pass(4, 0, 1)
-            rest_pass(4, 0, 2)
-            rest_pass(4, 0, 3)
-            out_pass(4, 0)
-            weigh(0)
-            weigh(1)
+            both(widen, 6, "vector")
+            both(exp, 0)
+            rest_passes(4, 0)
+            both(exp, 1)
+            weigh(0, "vector")
+            weigh(1, "gpsimd")
+            turn_xo(2)
+            both(turn_x, 5)
             exp(2, 0)
-            exp(2, 1)
-            weigh(2, True)
-            turn_x(5, 0)
-            turn_x(5, 1)
             turn_mass(0)
-            turn_xo(3)
+            leave_xo(2)
+            exp(2, 1)
+            rest_passes(4, 1)
             exp(3, 0)
             leave_mass((0,))
             exp(3, 1)
-            widen(7, 1, True)
-            rest_pass(4, 1, 0)
-            rest_pass(4, 1, 1)
-            rest_pass(4, 1, 2)
-            rest_pass(4, 1, 3)
-            out_pass(4, 1)
-            scale_x(5, 0)
-            scale_x(5, 1)
+            both(scale_x, 5)
+            both(turn_x, 6)
+            widen(7, 0, "scalar")
             turn_mass(1)
-            turn_x(6, 0)
-            turn_x(6, 1)
-            turn_mass(2)
-            leave_mass((1,))
-            exp(4, 0)
-            exp(4, 1)
-            leave_xo(3)
+            quantise_xo(2)
             quantise_mass((0,))
             quantise_x(5)
-            widen(7, 0)
+            weigh(2, "gpsimd")
+            both(out_pass, 4)
+            leave_mass((1,))
+            project(0)
+            both(exp, 4)
+            widen(7, 1, "scalar")
+            both(scale_x, 6)
+            both(logits, 5)
             quantise_mass((1,))
-            weigh(3, True)
-            weigh(4, True)
-            scale_x(6, 0)
-            scale_x(6, 1)
-            project_pass(0, 0, 0)
-            project_pass(0, 0, 1)
-            project_pass(0, 1, 0)
-            project_pass(0, 1, 1)
-            rest_pass(5, 0, 0)
-            rest_pass(5, 0, 1)
-            rest_pass(5, 0, 2)
-            rest_pass(5, 0, 3)
-            out_pass(5, 0)
-            project_pass(1, 0, 0)
-            project_pass(1, 0, 1)
-            project_pass(1, 1, 0)
-            project_pass(1, 1, 1)
-            store_half(0, 0, False)
-            store_half(0, 1, False)
-            leave_mass((2,))
-            exp(5, 0)
-            store_half(1, 0, False)
-            store_half(1, 1, False)
-            reduce_half(0, 0, "psum_last")
-            reduce_half(0, 1, "psum_last")
-            reduce_half(1, 0, "psum_last")
-            reduce_half(1, 1, "psum_last")
-            rest_pass(5, 1, 0)
-            rest_pass(5, 1, 1)
-            rest_pass(5, 1, 2)
-            rest_pass(5, 1, 3)
-            out_pass(5, 1)
-            exp(5, 1)
             quantise_x(6)
-            quantise_mass((2,))
-            quantise_xo(3)
-            weigh(5, True)
-            turn_mass(3)
-            turn_x(7, 0)
-            turn_x(7, 1)
-            turn_mass(4)
+            weigh(3, "gpsimd")
+            weigh(4, "gpsimd", 0, 1)
+            both(reduce_half, 0, "psum")
+            exp(5, 0)
+            project(1)
+            store_half(0, 0)
+            exp(5, 1)
+            store_half(0, 1)
+            turn_xo(3)
+            both(turn_x, 7)
+            turn_mass(2)
+            both(reduce_half, 1, "psum")
+            leave_xo(3)
+            store_half(1, 0)
+            leave_mass((2,))
+            store_half(1, 1)
             scale_x(7, 0)
+            both(rest_passes, 6)
+            quantise_xo(3)
+            quantise_mass((2,))
+            weigh(4, "gpsimd", 1, 2)
             scale_x(7, 1)
+            both(out_pass, 6)
+            project(2)
+            both(exp, 6)
+            turn_mass(3)
+            turn_mass(4)
+            quantise_x(7)
+            weigh(5, "gpsimd", 0, 1)
+            both(reduce_half, 2, "psum")
             leave_mass((3,))
             leave_mass((4,))
-            rest_pass(6, 0, 0)
-            rest_pass(6, 0, 1)
-            rest_pass(6, 0, 2)
-            rest_pass(6, 0, 3)
-            out_pass(6, 0)
-            project_pass(2, 0, 0)
-            project_pass(2, 0, 1)
-            project_pass(2, 1, 0)
-            project_pass(2, 1, 1)
-            rest_pass(6, 1, 0)
-            rest_pass(6, 1, 1)
-            rest_pass(6, 1, 2)
-            rest_pass(6, 1, 3)
-            out_pass(6, 1)
+            logits(7, 0)
+            store_target(2)
             quantise_mass((3,))
-            quantise_x(7)
+            weigh(5, "vector", 1, 2)
             quantise_mass((4,))
-            exp(6, 0)
-            store_half(2, 0, False)
-            store_half(2, 1, False)
-            exp(6, 1)
-            weigh(6, True)
-            reduce_half(2, 0, "psum_last")
-            reduce_half(2, 1, "psum_last")
-            project_pass(3, 0, 0)
-            project_pass(3, 0, 1)
-            project_pass(3, 1, 0)
-            project_pass(3, 1, 1)
-            rest_pass(7, 0, 0)
-            rest_pass(7, 0, 1)
-            rest_pass(7, 0, 2)
-            rest_pass(7, 0, 3)
-            out_pass(7, 0)
-            store_half(3, 0, False)
-            store_half(3, 1, False)
-            reduce_half(3, 0, "psum_last")
-            reduce_half(3, 1, "psum_last")
+            weigh(6, "gpsimd")
+            project(3)
             exp(7, 0)
-            project_pass(4, 0, 0)
-            project_pass(4, 0, 1)
-            project_pass(4, 1, 0)
-            project_pass(4, 1, 1)
-            weigh_pass(7, 0)
+            project(4)
+            both(reduce_half, 3, "psum")
             turn_mass(5)
+            store_target(3)
+            logits(7, 1)
+            leave_mass((5,))
+            both(reduce_half, 4, "psum")
+            store_half(4, 0)
+            exp(7, 1)
+            weigh(7, "vector", 0, 1)
+            quantise_mass((5,))
             turn_mass(6)
             turn_mass_pass(7, 0)
-            rest_pass(7, 1, 0)
-            rest_pass(7, 1, 1)
-            rest_pass(7, 1, 2)
-            rest_pass(7, 1, 3)
-            out_pass(7, 1)
-            store_half(4, 0, False)
-            reduce_half(4, 1, "psum")
-            reduce_half(4, 0, "psum_last")
-            leave_mass((5,))
+            weigh(7, "vector", 1, 2)
             leave_mass((6,))
             leave_mass_pass(7, 0)
-            store_half(4, 1)
-            quantise_mass((5,))
-            quantise_mass((6,))
-            quantise_mass_pass(7, 0)
-            exp(7, 1)
-            weigh_pass(7, 1)
-            project_pass(5, 0, 0)
-            project_pass(5, 0, 1)
-            project_pass(5, 1, 0)
-            project_pass(5, 1, 1)
-            project_pass(6, 0, 0)
-            project_pass(6, 0, 1)
+            project(5)
             turn_mass_pass(7, 1)
             store_half(5, 0, False)
-            store_half(5, 1, False)
             leave_mass_pass(7, 1)
+            store_half(4, 1)
+            quantise_mass((6,))
+            reduce_half(5, 1, "psum")
+            quantise_mass_pass(7, 0)
+            project(6)
             reduce_half(5, 0, "psum_last")
-            reduce_half(5, 1, "psum_last")
             quantise_mass_pass(7, 1)
-            project_pass(6, 1, 0)
-            project_pass(6, 1, 1)
-            project_pass(7, 0, 0)
-            project_pass(7, 1, 0)
-            project_pass(7, 0, 1)
-            project_pass(7, 1, 1)
+            for g in range(MASS_PASSES):
+                both(project_pass, 7, g)
             store_half(6, 0, False)
-            store_half(6, 1, False)
-            store_half(7, 0, False)
-            store_half(7, 1, False)
+            store_half(5, 1)
+            reduce_half(6, 1, "psum")
             reduce_half(6, 0, "psum_last")
-            reduce_half(6, 1, "psum_last")
+            store_half(7, 0, False)
+            store_half(6, 1)
+            reduce_half(7, 1, "psum")
             reduce_half(7, 0, "psum_last")
-            reduce_half(7, 1, "psum_last")
+            store_half(7, 1)
             nc.vector.tensor_tensor(out=row_loss[:], in0=half_loss[:, 0], in1=half_loss[:, 1], op=ALU.add)
             nc.sync.dma_start(out=loss.rearrange("(r i) -> r i", i=TILES), in_=row_loss[:])

@@ -88,8 +88,8 @@ def tile_c51_shifted_log_loss_s3_kernel(
         free_slots = list(range(SLOTS))
         slot_of = {}
 
-        def take_slot(key, width, newest=False, dtype=BF16):
-            n = free_slots[-1] if newest else free_slots[0]
+        def take_slot(key, width, back=None, dtype=BF16):
+            n = slot_of[back] if back else free_slots[0]
             free_slots.remove(n)
             slot_of[key] = n
             groups[key] = keep.tile([P, width], dtype, name="slot%d" % n, tag="slot%d" % n, align_bytes=64)
@@ -133,8 +133,8 @@ def tile_c51_shifted_log_loss_s3_kernel(
         def log(i, cols=slice(0, J)):
             nc.scalar.activation(out=logs[i][:, cols], in_=onl[i][:, cols], func=ACT.Ln)
 
-        def widen(i, b, engine):
-            half = take_slot(("wide", i, b), 2 * PASS, newest=engine == "gpsimd")
+        def widen(i, b, engine, back=None):
+            half = take_slot(("wide", i, b), 2 * PASS, back)
             codes = x_bytes[i][:, 2 * PASS * b : 2 * PASS * (b + 1)].bitcast(FP8)
             is_sorted[i, b] = engine != "gpsimd"
             if engine == "vector":
@@ -201,8 +201,8 @@ def tile_c51_shifted_log_loss_s3_kernel(
                 in_=free_slot(("xo", a))[:],
             )
 
-        def group_w(engine, c0, c1):
-            piece = take_slot(("w", c0), 4 * (c1 - c0), newest=engine == "gpsimd")
+        def group_w(engine, c0, c1, back=None):
+            piece = take_slot(("w", c0), 4 * (c1 - c0), back)
             if engine == "gpsimd":
                 nc.gpsimd.tensor_scalar(
                     out=piece[:].rearrange("p (n t) -> p n t", t=4),
@@ -269,9 +269,9 @@ def tile_c51_shifted_log_loss_s3_kernel(
                 in_=spacing_rows[:].bitcast(F32).rearrange("r (g p u) -> r g u p", g=MASS_PASSES, u=2),
             )
 
-        def weigh(i, engine, g0=0, g1=MASS_PASSES):
+        def weigh(i, engine, g0=0, g1=MASS_PASSES, back=None):
             cols = slice(PASS * g0, PASS * g1)
-            piece = take_slot(("m", i, g0), PASS * (g1 - g0), newest=engine == "gpsimd")
+            piece = take_slot(("m", i, g0), PASS * (g1 - g0), back)
             for g in range(g0, g1):
                 mass[i, g] = piece[:, PASS * (g - g0) : PASS * (g - g0 + 1)]
             source = free_slot(("e", i)) if g1 == MASS_PASSES else groups["e", i]
@@ -382,72 +382,74 @@ def tile_c51_shifted_log_loss_s3_kernel(
             load_online(0)
             load_x(1)
             load_x(2)
-            load_xo(0)
-            load_xo(1)
             load_scale_bytes(base_sc, base_scales)
             load_base(0)
             load_x(3)
             load_base(1)
-            load_x(4)
-            load_w(slice(0, 384))
             load_online(1)
             load_online(2)
-            load_w(slice(384, 640))
+            load_w(slice(0, BANK))
             load_online(3)
             load_online(4)
-            load_w(slice(640, F))
+            load_x(4)
+            load_xo(0)
+            load_xo(1)
             for i in range(5, TILES):
                 load_online(i)
+            load_w(slice(BANK, F))
             load_x(5)
             load_spacing()
-            load_x(6)
             load_xo(2)
+            load_x(6)
             load_proj()
             load_scale_bytes(proj_sc, proj_scales)
             load_x(7)
             load_xo(3)
             log(0)
             both(widen, 0, "vector")
-            widen(1, 0, "gpsimd")
+            widen(1, 0, "vector")
             widen(1, 1, "scalar")
-            widen(2, 0, "gpsimd")
-            widen(2, 1, "scalar")
+            both(widen, 2, "scalar")
             both(turn_x, 0)
             both(turn_x, 1)
-            turn_xo(0)
             both(scale_x, 0)
-            turn_xo(1)
-            both(turn_x, 2)
-            leave_xo(0)
-            leave_xo(1)
+            quantise_x(0, 0, 2)
             both(widen, 3, "scalar")
+            for i in range(1, 5):
+                log(i)
             widen(4, 0, "scalar")
-            quantise_x(0)
-            for g in range(REST_PASSES):
+            for g in range(2):
                 both(rest_pass, 0, g)
-            both(scale_x, 1)
-            both(turn_x, 3)
-            quantise_xo(0)
+            both(turn_x, 2)
+            scale_x(1, 0)
+            quantise_x(0, 2, 4)
+            for g in range(2, REST_PASSES):
+                both(rest_pass, 0, g)
+            scale_x(1, 1)
             quantise_x(1)
-            widen(4, 1, "gpsimd")
-            group_w("gpsimd", 0, 384)
+            group_w("gpsimd", 0, BANK)
+            both(turn_x, 3)
             both(rest_passes, 1)
             both(scale_x, 2)
+            turn_xo(0)
+            turn_xo(1)
             scale_x(3, 0)
+            leave_xo(0)
+            leave_xo(1)
             quantise_x(2)
-            quantise_xo(1)
-            group_w("gpsimd", 384, 640)
+            widen(4, 1, "gpsimd", ("x", 1))
             both(rest_passes, 2)
             scale_x(3, 1)
             both(turn_x, 4)
-            for i in range(1, TILES):
+            for i in range(5, TILES):
                 log(i)
-            quantise_w(0, 384)
+            quantise_w(0, BANK)
             quantise_x(3)
-            quantise_w(384, 640)
-            group_w("gpsimd", 640, F)
+            quantise_xo(0)
+            group_w("gpsimd", BANK, F, ("xo", 0))
+            quantise_xo(1)
             both(scale_x, 4)
-            quantise_w(640, F)
+            quantise_w(BANK, F)
             for i in range(3):
                 out_pass(i, 0)
             logits(3, 0)
@@ -455,92 +457,86 @@ def tile_c51_shifted_log_loss_s3_kernel(
             for i in range(4):
                 out_pass(i, 1)
             quantise_x(4)
-            both(widen, 5, "vector")
             sort_spacing()
-            both(widen, 6, "vector")
-            both(exp, 0)
-            rest_passes(4, 0)
-            both(exp, 1)
+            both(widen, 5, "vector")
+            for h in range(2):
+                exp(0, h)
+                exp(1, h)
+            turn_xo(2)
             weigh(0, "vector")
             weigh(1, "gpsimd")
-            turn_xo(2)
             both(turn_x, 5)
+            leave_xo(2)
             exp(2, 0)
             turn_mass(0)
-            leave_xo(2)
             exp(2, 1)
-            rest_passes(4, 1)
-            exp(3, 0)
-            leave_mass((0,))
-            exp(3, 1)
             both(scale_x, 5)
-            both(turn_x, 6)
-            widen(7, 0, "scalar")
-            turn_mass(1)
+            leave_mass((0,))
+            both(rest_passes, 4)
+            both(exp, 3)
+            widen(6, 0, "scalar")
             quantise_xo(2)
             quantise_mass((0,))
             quantise_x(5)
-            weigh(2, "gpsimd")
+            widen(6, 1, "vector")
+            weigh(2, "gpsimd", back=("x", 5))
+            weigh(3, "gpsimd", 0, 1)
             both(out_pass, 4)
-            leave_mass((1,))
             project(0)
             both(exp, 4)
-            widen(7, 1, "scalar")
+            turn_mass(1)
+            both(turn_x, 6)
+            both(reduce_half, 0, "psum")
+            leave_mass((1,))
+            store_target(0)
             both(scale_x, 6)
             both(logits, 5)
+            both(widen, 7, "scalar")
             quantise_mass((1,))
             quantise_x(6)
-            weigh(3, "gpsimd")
-            weigh(4, "gpsimd", 0, 1)
-            both(reduce_half, 0, "psum")
-            exp(5, 0)
+            weigh(3, "gpsimd", 1, 2, ("mass", (1,)))
+            weigh(4, "gpsimd")
             project(1)
-            store_half(0, 0)
-            exp(5, 1)
-            store_half(0, 1)
-            turn_xo(3)
+            both(exp, 5)
             both(turn_x, 7)
+            turn_xo(3)
             turn_mass(2)
             both(reduce_half, 1, "psum")
-            leave_xo(3)
             store_half(1, 0)
+            leave_xo(3)
             leave_mass((2,))
             store_half(1, 1)
-            scale_x(7, 0)
+            both(scale_x, 7)
             both(rest_passes, 6)
             quantise_xo(3)
             quantise_mass((2,))
-            weigh(4, "gpsimd", 1, 2)
-            scale_x(7, 1)
+            quantise_x(7)
+            weigh(5, "vector")
             both(out_pass, 6)
             project(2)
             both(exp, 6)
+            weigh(6, "gpsimd", 0, 1, ("x", 7))
             turn_mass(3)
             turn_mass(4)
-            quantise_x(7)
-            weigh(5, "gpsimd", 0, 1)
+            turn_mass(5)
             both(reduce_half, 2, "psum")
             leave_mass((3,))
-            leave_mass((4,))
+            leave_mass((4, 5))
             logits(7, 0)
-            store_target(2)
             quantise_mass((3,))
-            weigh(5, "vector", 1, 2)
-            quantise_mass((4,))
-            weigh(6, "gpsimd")
+            store_target(2)
+            quantise_mass((4, 5))
+            weigh(6, "gpsimd", 1, 2, ("mass", (4, 5)))
             project(3)
             exp(7, 0)
             project(4)
             both(reduce_half, 3, "psum")
-            turn_mass(5)
             store_target(3)
             logits(7, 1)
-            leave_mass((5,))
             both(reduce_half, 4, "psum")
             store_half(4, 0)
             exp(7, 1)
             weigh(7, "vector", 0, 1)
-            quantise_mass((5,))
             turn_mass(6)
             turn_mass_pass(7, 0)
             weigh(7, "vector", 1, 2)

@@ -99,8 +99,8 @@ def tile_c51_shifted_log_loss_s3_kernel(
             free_slots.append(slot_of[key])
             return groups[key]
 
-        def load_x(i):
-            nc.sync.dma_start(out=x_bytes[i][:], in_=x_hbm[:, i, :])
+        def load_x(i, cols=slice(0, KR)):
+            nc.sync.dma_start(out=x_bytes[i][:, cols], in_=x_hbm[:, i, cols])
 
         def load_k_scale():
             nc.sync.dma_start(out=k_scale[:, :, 0:4], in_=x_rest_scale.rearrange("o (g p t) -> p (o g) t", p=P, t=4))
@@ -133,14 +133,16 @@ def tile_c51_shifted_log_loss_s3_kernel(
         def log(i, cols=slice(0, J)):
             nc.scalar.activation(out=logs[i][:, cols], in_=onl[i][:, cols], func=ACT.Ln)
 
-        def widen(i, b, engine, back=None):
+        def widen(i, b, engine, back=None, plain=False):
             half = take_slot(("wide", i, b), 2 * PASS, back)
             codes = x_bytes[i][:, 2 * PASS * b : 2 * PASS * (b + 1)].bitcast(FP8)
-            is_sorted[i, b] = engine != "gpsimd"
+            is_sorted[i, b] = engine != "gpsimd" and not plain
             if engine == "vector":
                 nc.vector.tensor_copy(
                     out=half[:].rearrange("r (u gp e) -> r gp u e", u=2, e=2), in_=codes.rearrange("r (gp u e) -> r gp u e", u=2, e=2)
                 )
+            elif plain:
+                nc.scalar.copy(out=half[:], in_=codes)
             elif engine == "scalar":
                 nc.scalar.copy(
                     out=half[:].rearrange("r (u gp e) -> r u gp e", u=2, e=2), in_=codes.rearrange("r (gp u e) -> r u gp e", u=2, e=2)
@@ -380,23 +382,23 @@ def tile_c51_shifted_log_loss_s3_kernel(
             load_x(0)
             load_k_scale()
             load_online(0)
-            load_x(1)
-            load_x(2)
+            for i in range(1, 4):
+                load_x(i)
             load_scale_bytes(base_sc, base_scales)
             load_base(0)
-            load_x(3)
-            load_base(1)
             load_online(1)
-            load_online(2)
-            load_w(slice(0, BANK))
-            load_online(3)
-            load_online(4)
             load_x(4)
+            load_base(1)
+            load_w(slice(0, BANK))
+            load_online(2)
+            load_online(3)
             load_xo(0)
+            load_online(4)
             load_xo(1)
-            for i in range(5, TILES):
-                load_online(i)
+            load_online(5)
             load_w(slice(BANK, F))
+            load_online(6)
+            load_online(7)
             load_x(5)
             load_spacing()
             load_xo(2)
@@ -408,27 +410,29 @@ def tile_c51_shifted_log_loss_s3_kernel(
             log(0)
             both(widen, 0, "vector")
             widen(1, 0, "vector")
-            widen(1, 1, "scalar")
-            both(widen, 2, "scalar")
+            widen(1, 1, "scalar", plain=True)
+            widen(2, 0, "gpsimd")
+            widen(2, 1, "scalar", plain=True)
+            widen(3, 1, "scalar")
             both(turn_x, 0)
             both(turn_x, 1)
             both(scale_x, 0)
+            both(turn_x, 2)
             quantise_x(0, 0, 2)
-            both(widen, 3, "scalar")
-            for i in range(1, 5):
+            widen(3, 0, "gpsimd")
+            log(1)
+            both(widen, 4, "scalar")
+            for i in range(2, 5):
                 log(i)
-            widen(4, 0, "scalar")
             for g in range(2):
                 both(rest_pass, 0, g)
-            both(turn_x, 2)
-            scale_x(1, 0)
+            both(scale_x, 1)
+            both(turn_x, 3)
             quantise_x(0, 2, 4)
+            quantise_x(1)
             for g in range(2, REST_PASSES):
                 both(rest_pass, 0, g)
-            scale_x(1, 1)
-            quantise_x(1)
             group_w("gpsimd", 0, BANK)
-            both(turn_x, 3)
             both(rest_passes, 1)
             both(scale_x, 2)
             turn_xo(0)
@@ -437,19 +441,21 @@ def tile_c51_shifted_log_loss_s3_kernel(
             leave_xo(0)
             leave_xo(1)
             quantise_x(2)
-            widen(4, 1, "gpsimd", ("x", 1))
-            both(rest_passes, 2)
+            rest_passes(2, 0)
             scale_x(3, 1)
             both(turn_x, 4)
+            rest_passes(2, 1)
             for i in range(5, TILES):
                 log(i)
             quantise_w(0, BANK)
             quantise_x(3)
+            group_w("vector", 896, F)
             quantise_xo(0)
-            group_w("gpsimd", BANK, F, ("xo", 0))
+            group_w("gpsimd", BANK, 896, ("xo", 0))
             quantise_xo(1)
             both(scale_x, 4)
-            quantise_w(BANK, F)
+            quantise_w(896, F)
+            quantise_w(BANK, 896)
             for i in range(3):
                 out_pass(i, 0)
             logits(3, 0)
@@ -459,29 +465,32 @@ def tile_c51_shifted_log_loss_s3_kernel(
             quantise_x(4)
             sort_spacing()
             both(widen, 5, "vector")
-            for h in range(2):
-                exp(0, h)
-                exp(1, h)
+            exp(0, 0)
+            exp(1, 0)
             turn_xo(2)
+            exp(0, 1)
+            exp(2, 0)
+            both(turn_x, 5)
+            exp(1, 1)
             weigh(0, "vector")
             weigh(1, "gpsimd")
-            both(turn_x, 5)
+            rest_passes(4, 0)
             leave_xo(2)
-            exp(2, 0)
-            turn_mass(0)
             exp(2, 1)
+            turn_mass(0)
             both(scale_x, 5)
+            exp(3, 0)
             leave_mass((0,))
-            both(rest_passes, 4)
-            both(exp, 3)
+            rest_passes(4, 1)
+            exp(3, 1)
             widen(6, 0, "scalar")
             quantise_xo(2)
+            both(out_pass, 4)
             quantise_mass((0,))
             quantise_x(5)
             widen(6, 1, "vector")
             weigh(2, "gpsimd", back=("x", 5))
             weigh(3, "gpsimd", 0, 1)
-            both(out_pass, 4)
             project(0)
             both(exp, 4)
             turn_mass(1)

@@ -24,6 +24,7 @@ BANK = 512
 REST_PASSES = KR // PASS
 MASS_PASSES = F // PASS
 QUAD = 2
+FIRST_LOG = 128
 SLOTS = 16
 WIDE_BUFS = 4
 MASS_CODE_BUFS = 4
@@ -57,6 +58,7 @@ def tile_c51_shifted_log_loss_s3_kernel(
         spacing_rows = kept([P, F], BF16, "spacing_rows")
         spacing_sorted = kept([P, F], BF16, "spacing_sorted")
         ident = kept([P, P], F32, "ident")
+        zeros = kept([P, 2 * P], F32, "zeros")
         row_loss = kept([P, TILES], F32, "row_loss")
         half_loss = kept([P, 2, TILES], F32, "half_loss")
         x_codes = [kept([P, REST_PASSES, P], U32, "x_codes%d" % i) for i in range(TILES)]
@@ -160,10 +162,14 @@ def tile_c51_shifted_log_loss_s3_kernel(
                     nc.tensor.transpose(bank[:, u, gg, :], src, ident[:])
 
         def scale_x(i, b):
-            if b == 0:
-                take_slot(("x", i), 4 * PASS)
+            if i == 0:
+                half = take_slot(("x", i, b), 2 * PASS)[:]
+            else:
+                if b == 0:
+                    take_slot(("x", i), 4 * PASS)
+                half = groups["x", i][:, 2 * PASS * b : 2 * PASS * (b + 1)]
             nc.vector.tensor_tensor(
-                out=groups["x", i][:, 2 * PASS * b : 2 * PASS * (b + 1)].rearrange("p (c r u e) -> p c r u e", c=2, u=2, e=2),
+                out=half.rearrange("p (c r u e) -> p c r u e", c=2, u=2, e=2),
                 in0=give_back(("x", i, b))[:].bitcast(BF16).rearrange("p u c (r e) -> p c r u e", e=2),
                 in1=k_scale[:, 2 * b : 2 * b + 2, 0:4].rearrange("p c (u e) -> p c u e", e=2).unsqueeze(2).to_broadcast([P, 2, P, 2, 2]),
                 op=ALU.mult,
@@ -177,21 +183,33 @@ def tile_c51_shifted_log_loss_s3_kernel(
                 in_=give_back(key)[:].rearrange("p u c r -> p c r u"),
             )
 
-        def quantise_x(i, g0=0, g1=REST_PASSES):
+        def quantise_x(i, b=None):
+            passes = slice(0, REST_PASSES) if b is None else slice(2 * b, 2 * b + 2)
             nc.vector.quantize_mx(
-                out=x_codes[i][:, g0:g1].rearrange("p g r -> p (g r)").bitcast(FP8X4),
-                scales=x_sc[i][:, g0:g1].rearrange("p g r -> p (g r)"),
-                in_=groups["x", i][:, PASS * g0 : PASS * g1],
+                out=x_codes[i][:, passes].rearrange("p g r -> p (g r)").bitcast(FP8X4),
+                scales=x_sc[i][:, passes].rearrange("p g r -> p (g r)"),
+                in_=free_slot(("x", i) if b is None else ("x", i, b))[:],
             )
-            if g1 == REST_PASSES:
-                free_slot(("x", i))
+
+        def sort_xo(a):
+            nc.vector.tensor_copy(
+                out=take_slot(("xo_sorted", a), 2 * PASS)[:].bitcast(F32).rearrange("r (u cp) -> r u cp", u=2),
+                in_=xo[a][:].rearrange("r c k -> r (c k)").bitcast(F32).rearrange("r (cp u) -> r u cp", u=2),
+            )
 
         def turn_xo(a):
             bank = take_bank(("xo", a), [P, 2, 2, P])
             for c in range(2):
                 pairs = xo[a][:, c, :].bitcast(F32)
                 for u in range(2):
-                    nc.tensor.transpose(bank[:, u, c, :], pairs[:, u::2], ident[:])
+                    if ("xo_sorted", a) in groups:
+                        first = P * (2 * u + c)
+                        src = groups["xo_sorted", a][:].bitcast(F32)[:, first : first + P]
+                    else:
+                        src = pairs[:, u::2]
+                    nc.tensor.transpose(bank[:, u, c, :], src, ident[:])
+            if ("xo_sorted", a) in groups:
+                free_slot(("xo_sorted", a))
 
         def leave_xo(a, copy=nc.scalar.copy):
             leave_bank(("xo", a), ("xo", a), 0, 1, copy)
@@ -371,11 +389,16 @@ def tile_c51_shifted_log_loss_s3_kernel(
                 accum_out=half_loss[:, h, i : i + 1],
             )
 
+        def warm_up(n):
+            take_bank(("warm", n), [P, 2 * P])
+            nc.tensor.matmul(give_back(("warm", n))[:], lhsT=zeros[:, 0:P], rhs=zeros[:], start=True, stop=True)
+
         def both(step, *args):
             for h in range(2):
                 step(args[0], h, *args[1:])
 
         with tc.manual_schedule():
+            nc.vector.memset(zeros[:], 0.0)
             nc.vector.memset(base_sc[:].rearrange("p g n -> p (g n)").bitcast(I32), 0)
             nc.vector.memset(proj_sc[:].rearrange("p g n -> p (g n)").bitcast(I32), 0)
             make_identity(nc, ident[:])
@@ -393,8 +416,8 @@ def tile_c51_shifted_log_loss_s3_kernel(
             load_online(2)
             load_online(3)
             load_xo(0)
-            load_online(4)
             load_xo(1)
+            load_online(4)
             load_online(5)
             load_w(slice(BANK, F))
             load_online(6)
@@ -409,30 +432,35 @@ def tile_c51_shifted_log_loss_s3_kernel(
             load_xo(3)
             log(0)
             both(widen, 0, "vector")
-            widen(1, 0, "vector")
-            widen(1, 1, "scalar", plain=True)
+            widen(1, 0, "gpsimd")
+            widen(1, 1, "scalar")
             widen(2, 0, "gpsimd")
-            widen(2, 1, "scalar", plain=True)
+            widen(2, 1, "scalar")
             widen(3, 1, "scalar")
+            warm_up(0)
+            warm_up(1)
             both(turn_x, 0)
-            both(turn_x, 1)
+            warm_up(2)
+            turn_x(1, 0)
+            warm_up(3)
+            turn_x(1, 1)
             both(scale_x, 0)
             both(turn_x, 2)
-            quantise_x(0, 0, 2)
-            widen(3, 0, "gpsimd")
+            quantise_x(0, 0)
+            widen(3, 0, "gpsimd", ("x", 0, 0))
             log(1)
             both(widen, 4, "scalar")
-            for i in range(2, 5):
-                log(i)
+            log(2)
+            log(3)
             for g in range(2):
                 both(rest_pass, 0, g)
             both(scale_x, 1)
             both(turn_x, 3)
-            quantise_x(0, 2, 4)
+            quantise_x(0, 1)
             quantise_x(1)
             for g in range(2, REST_PASSES):
                 both(rest_pass, 0, g)
-            group_w("gpsimd", 0, BANK)
+            group_w("gpsimd", 0, 384)
             both(rest_passes, 1)
             both(scale_x, 2)
             turn_xo(0)
@@ -441,14 +469,16 @@ def tile_c51_shifted_log_loss_s3_kernel(
             leave_xo(0)
             leave_xo(1)
             quantise_x(2)
+            group_w("gpsimd", 384, BANK, ("x", 2))
             rest_passes(2, 0)
             scale_x(3, 1)
             both(turn_x, 4)
             rest_passes(2, 1)
-            for i in range(5, TILES):
+            for i in range(4, TILES):
                 log(i)
-            quantise_w(0, BANK)
+            quantise_w(0, 384)
             quantise_x(3)
+            quantise_w(384, BANK)
             group_w("vector", 896, F)
             quantise_xo(0)
             group_w("gpsimd", BANK, 896, ("xo", 0))
@@ -465,13 +495,11 @@ def tile_c51_shifted_log_loss_s3_kernel(
             quantise_x(4)
             sort_spacing()
             both(widen, 5, "vector")
-            exp(0, 0)
-            exp(1, 0)
+            both(exp, 0)
             turn_xo(2)
-            exp(0, 1)
-            exp(2, 0)
+            both(exp, 1)
             both(turn_x, 5)
-            exp(1, 1)
+            exp(2, 0)
             weigh(0, "vector")
             weigh(1, "gpsimd")
             rest_passes(4, 0)
@@ -503,7 +531,8 @@ def tile_c51_shifted_log_loss_s3_kernel(
             both(widen, 7, "scalar")
             quantise_mass((1,))
             quantise_x(6)
-            weigh(3, "gpsimd", 1, 2, ("mass", (1,)))
+            sort_xo(3)
+            weigh(3, "gpsimd", 1, 2, ("x", 6))
             weigh(4, "gpsimd")
             project(1)
             both(exp, 5)

@@ -40,18 +40,18 @@ def tile_c51_shifted_log_loss_s3_kernel(
         work = ctx.enter_context(tc.tile_pool(name="work", bufs=WIDE_BUFS))
         psum = ctx.enter_context(tc.psum_pool(name="psum", bufs=1))
 
-        def kept(shape, dtype, name):
-            return keep.tile(shape, dtype, name=name, tag=name, align_bytes=64)
+        def kept(shape, dtype, name, align=64):
+            return keep.tile(shape, dtype, name=name, tag=name, align_bytes=align)
 
         x_bytes = [kept([P, KR], U8, "x_bytes%d" % i) for i in range(TILES)]
         k_scale = kept([P, REST_PASSES, 8], F32, "k_scale")
-        base = [kept([P, 2, 2 * F], U8, "base%d" % b) for b in range(2)]
-        base_sc = kept([P, REST_PASSES, F], U8, "base_sc")
-        proj = kept([P, MASS_PASSES, 2 * J], U8, "proj")
-        proj_sc = kept([P, MASS_PASSES, J], U8, "proj_sc")
+        base = [kept([P, 2, 2 * F], U8, "base%d" % b, 256) for b in range(2)]
+        base_sc = kept([P, REST_PASSES, F], U8, "base_sc", 256)
+        proj = kept([P, MASS_PASSES, 2 * J], U8, "proj", 256)
+        proj_sc = kept([P, MASS_PASSES, J], U8, "proj_sc", 256)
         w_rows = kept([P, 4, F], BF16, "w_rows")
-        w_codes = kept([P, F], U32, "w_codes")
-        w_sc = kept([P, F], U8, "w_sc")
+        w_codes = kept([P, F], U32, "w_codes", 256)
+        w_sc = kept([P, F], U8, "w_sc", 256)
         xo = [kept([P, QUAD, KO], BF16, "xo%d" % a) for a in range(TILES // QUAD)]
         onl = [kept([P, J], BF16, "onl%d" % i) for i in range(TILES)]
         logs = [kept([P, J], F32, "logs%d" % i) for i in range(TILES)]
@@ -61,10 +61,14 @@ def tile_c51_shifted_log_loss_s3_kernel(
         zeros = kept([P, 2 * P], F32, "zeros")
         row_loss = kept([P, TILES], F32, "row_loss")
         half_loss = kept([P, 2, TILES], F32, "half_loss")
-        x_codes = [kept([P, REST_PASSES, P], U32, "x_codes%d" % i) for i in range(TILES)]
-        x_sc = [kept([P, REST_PASSES, P], U8, "x_sc%d" % i) for i in range(TILES)]
-        xo_codes = [kept([P, QUAD, P], U32, "xo_codes%d" % a) for a in range(TILES // QUAD)]
-        xo_sc = [kept([P, QUAD, P], U8, "xo_sc%d" % a) for a in range(TILES // QUAD)]
+        all_x_codes = kept([P, TILES, REST_PASSES, P], U32, "x_codes", 256)
+        all_x_sc = kept([P, TILES, REST_PASSES, P], U8, "x_sc", 256)
+        all_xo_codes = kept([P, TILES // QUAD, QUAD, P], U32, "xo_codes", 256)
+        all_xo_sc = kept([P, TILES // QUAD, QUAD, P], U8, "xo_sc", 256)
+        x_codes = [all_x_codes[:, i] for i in range(TILES)]
+        x_sc = [all_x_sc[:, i] for i in range(TILES)]
+        xo_codes = [all_xo_codes[:, a] for a in range(TILES // QUAD)]
+        xo_sc = [all_xo_sc[:, a] for a in range(TILES // QUAD)]
 
         x_hbm = x_rest_bytes.rearrange("(r i) k -> r i k", i=TILES)
         xo_hbm = x_out.rearrange("(r i) k -> r i k", i=TILES)
@@ -317,8 +321,8 @@ def tile_c51_shifted_log_loss_s3_kernel(
                 leave_bank(("mass", i), ("mass", tiles), n, len(tiles), copy)
 
         def quantise_mass(tiles):
-            codes = work.tile([P, len(tiles), MASS_PASSES, P], U32, name="mass_codes", tag="mass_codes", bufs=MASS_CODE_BUFS, align_bytes=64)
-            scales = work.tile([P, len(tiles), MASS_PASSES, P], U8, name="mass_sc", tag="mass_sc", bufs=MASS_CODE_BUFS, align_bytes=64)
+            codes = work.tile([P, len(tiles), MASS_PASSES, P], U32, name="mass_codes", tag="mass_codes", bufs=MASS_CODE_BUFS, align_bytes=256)
+            scales = work.tile([P, len(tiles), MASS_PASSES, P], U8, name="mass_sc", tag="mass_sc", bufs=MASS_CODE_BUFS, align_bytes=256)
             for n, i in enumerate(tiles):
                 mass_codes[i], mass_sc[i] = codes[:, n], scales[:, n]
             nc.vector.quantize_mx(
@@ -341,8 +345,8 @@ def tile_c51_shifted_log_loss_s3_kernel(
 
         def quantise_mass_pass(i, g):
             if g == 0:
-                codes = work.tile([P, MASS_PASSES, P], U32, name="mass_codes", tag="mass_codes", bufs=MASS_CODE_BUFS, align_bytes=64)
-                scales = work.tile([P, MASS_PASSES, P], U8, name="mass_sc", tag="mass_sc", bufs=MASS_CODE_BUFS, align_bytes=64)
+                codes = work.tile([P, MASS_PASSES, P], U32, name="mass_codes", tag="mass_codes", bufs=MASS_CODE_BUFS, align_bytes=256)
+                scales = work.tile([P, MASS_PASSES, P], U8, name="mass_sc", tag="mass_sc", bufs=MASS_CODE_BUFS, align_bytes=256)
                 mass_codes[i], mass_sc[i] = codes[:], scales[:]
             nc.vector.quantize_mx(out=mass_codes[i][:, g].bitcast(FP8X4), scales=mass_sc[i][:, g], in_=free_slot(("mass", i, g))[:])
 

@@ -28,7 +28,8 @@ FIRST_LOG = 128
 SLOTS = 16
 WIDE_BUFS = 4
 MASS_CODE_BUFS = 4
-TARGET_BUFS = 6
+TARGET_BUFS = 5
+ALIGN = 256
 
 
 def tile_c51_shifted_log_loss_s3_kernel(
@@ -40,35 +41,35 @@ def tile_c51_shifted_log_loss_s3_kernel(
         work = ctx.enter_context(tc.tile_pool(name="work", bufs=WIDE_BUFS))
         psum = ctx.enter_context(tc.psum_pool(name="psum", bufs=1))
 
-        def kept(shape, dtype, name, align=64):
-            return keep.tile(shape, dtype, name=name, tag=name, align_bytes=align)
+        def kept(shape, dtype, name):
+            return keep.tile(shape, dtype, name=name, tag=name, align_bytes=ALIGN)
 
-        x_bytes = [kept([P, KR], U8, "x_bytes%d" % i) for i in range(TILES)]
+        def kept_each(n, shape, dtype, name):
+            tile = kept([shape[0], n] + shape[1:], dtype, name)
+            return [tile[:, i] for i in range(n)]
+
+        x_bytes = kept_each(TILES, [P, KR], U8, "x_bytes")
         k_scale = kept([P, REST_PASSES, 8], F32, "k_scale")
-        base = [kept([P, 2, 2 * F], U8, "base%d" % b, 256) for b in range(2)]
-        base_sc = kept([P, REST_PASSES, F], U8, "base_sc", 256)
-        proj = kept([P, MASS_PASSES, 2 * J], U8, "proj", 256)
-        proj_sc = kept([P, MASS_PASSES, J], U8, "proj_sc", 256)
+        base = kept_each(2, [P, 2, 2 * F], U8, "base")
+        base_sc = kept([P, REST_PASSES, F], U8, "base_sc")
+        proj = kept([P, MASS_PASSES, 2 * J], U8, "proj")
+        proj_sc = kept([P, MASS_PASSES, J], U8, "proj_sc")
         w_rows = kept([P, 4, F], BF16, "w_rows")
-        w_codes = kept([P, F], U32, "w_codes", 256)
-        w_sc = kept([P, F], U8, "w_sc", 256)
-        xo = [kept([P, QUAD, KO], BF16, "xo%d" % a) for a in range(TILES // QUAD)]
-        onl = [kept([P, J], BF16, "onl%d" % i) for i in range(TILES)]
-        logs = [kept([P, J], F32, "logs%d" % i) for i in range(TILES)]
+        w_codes = kept([P, F], U32, "w_codes")
+        w_sc = kept([P, F], U8, "w_sc")
+        xo = kept_each(TILES // QUAD, [P, QUAD, KO], BF16, "xo")
+        onl = kept_each(TILES, [P, J], BF16, "onl")
+        logs = kept_each(TILES, [P, J], F32, "logs")
         spacing_rows = kept([P, F], BF16, "spacing_rows")
         spacing_sorted = kept([P, F], BF16, "spacing_sorted")
         ident = kept([P, P], F32, "ident")
         zeros = kept([P, 2 * P], F32, "zeros")
         row_loss = kept([P, TILES], F32, "row_loss")
         half_loss = kept([P, 2, TILES], F32, "half_loss")
-        all_x_codes = kept([P, TILES, REST_PASSES, P], U32, "x_codes", 256)
-        all_x_sc = kept([P, TILES, REST_PASSES, P], U8, "x_sc", 256)
-        all_xo_codes = kept([P, TILES // QUAD, QUAD, P], U32, "xo_codes", 256)
-        all_xo_sc = kept([P, TILES // QUAD, QUAD, P], U8, "xo_sc", 256)
-        x_codes = [all_x_codes[:, i] for i in range(TILES)]
-        x_sc = [all_x_sc[:, i] for i in range(TILES)]
-        xo_codes = [all_xo_codes[:, a] for a in range(TILES // QUAD)]
-        xo_sc = [all_xo_sc[:, a] for a in range(TILES // QUAD)]
+        x_codes = kept_each(TILES, [P, REST_PASSES, P], U32, "x_codes")
+        x_sc = kept_each(TILES, [P, REST_PASSES, P], U8, "x_sc")
+        xo_codes = kept_each(TILES // QUAD, [P, QUAD, P], U32, "xo_codes")
+        xo_sc = kept_each(TILES // QUAD, [P, QUAD, P], U8, "xo_sc")
 
         x_hbm = x_rest_bytes.rearrange("(r i) k -> r i k", i=TILES)
         xo_hbm = x_out.rearrange("(r i) k -> r i k", i=TILES)
@@ -98,7 +99,7 @@ def tile_c51_shifted_log_loss_s3_kernel(
             n = slot_of[back] if back else free_slots[0]
             free_slots.remove(n)
             slot_of[key] = n
-            groups[key] = keep.tile([P, width], dtype, name="slot%d" % n, tag="slot%d" % n, align_bytes=64)
+            groups[key] = keep.tile([P, width], dtype, name="slot%d" % n, tag="slot%d" % n, align_bytes=ALIGN)
             return groups[key]
 
         def free_slot(key):
@@ -321,8 +322,8 @@ def tile_c51_shifted_log_loss_s3_kernel(
                 leave_bank(("mass", i), ("mass", tiles), n, len(tiles), copy)
 
         def quantise_mass(tiles):
-            codes = work.tile([P, len(tiles), MASS_PASSES, P], U32, name="mass_codes", tag="mass_codes", bufs=MASS_CODE_BUFS, align_bytes=256)
-            scales = work.tile([P, len(tiles), MASS_PASSES, P], U8, name="mass_sc", tag="mass_sc", bufs=MASS_CODE_BUFS, align_bytes=256)
+            codes = work.tile([P, len(tiles), MASS_PASSES, P], U32, name="mass_codes", tag="mass_codes", bufs=MASS_CODE_BUFS, align_bytes=ALIGN)
+            scales = work.tile([P, len(tiles), MASS_PASSES, P], U8, name="mass_sc", tag="mass_sc", bufs=MASS_CODE_BUFS, align_bytes=ALIGN)
             for n, i in enumerate(tiles):
                 mass_codes[i], mass_sc[i] = codes[:, n], scales[:, n]
             nc.vector.quantize_mx(
@@ -345,8 +346,8 @@ def tile_c51_shifted_log_loss_s3_kernel(
 
         def quantise_mass_pass(i, g):
             if g == 0:
-                codes = work.tile([P, MASS_PASSES, P], U32, name="mass_codes", tag="mass_codes", bufs=MASS_CODE_BUFS, align_bytes=256)
-                scales = work.tile([P, MASS_PASSES, P], U8, name="mass_sc", tag="mass_sc", bufs=MASS_CODE_BUFS, align_bytes=256)
+                codes = work.tile([P, MASS_PASSES, P], U32, name="mass_codes", tag="mass_codes", bufs=MASS_CODE_BUFS, align_bytes=ALIGN)
+                scales = work.tile([P, MASS_PASSES, P], U8, name="mass_sc", tag="mass_sc", bufs=MASS_CODE_BUFS, align_bytes=ALIGN)
                 mass_codes[i], mass_sc[i] = codes[:], scales[:]
             nc.vector.quantize_mx(out=mass_codes[i][:, g].bitcast(FP8X4), scales=mass_sc[i][:, g], in_=free_slot(("mass", i, g))[:])
 
@@ -370,7 +371,7 @@ def tile_c51_shifted_log_loss_s3_kernel(
 
         def store_half(i, h, last_reader=True):
             if i not in target_sb:
-                target_sb[i] = work.tile([P, J], F32, name="target_sb", tag="target_sb", bufs=TARGET_BUFS)
+                target_sb[i] = work.tile([P, J], F32, name="target_sb", tag="target_sb", bufs=TARGET_BUFS, align_bytes=ALIGN)
             cols = slice(BANK * h, BANK * (h + 1))
             bank = give_back(("target", i, h)) if last_reader else banks["target", i, h]
             nc.scalar.copy(out=target_sb[i][:, cols], in_=bank[:])
@@ -382,7 +383,7 @@ def tile_c51_shifted_log_loss_s3_kernel(
 
         def reduce_half(i, h, source):
             cols = slice(BANK * h, BANK * (h + 1))
-            products = work.tile([P, BANK], F32, name="products", tag="products", bufs=2)
+            products = work.tile([P, BANK], F32, name="products", tag="products", bufs=2, align_bytes=ALIGN)
             nc.vector.scalar_tensor_tensor(
                 out=products[:],
                 in0=target_sb[i][:, cols] if source == "sbuf" else (give_back(("target", i, h)) if source == "psum_last" else banks["target", i, h])[:],

from contextlib import ExitStack

import concourse.mybir as mybir
from concourse.masks import make_identity

B, KO, KR, F, J = 1024, 512, 2048, 1024, 1024
FLOPS = 2 * B * F * (KO + KR) + 2 * B * J * F

F32 = mybir.dt.float32
BF16 = mybir.dt.bfloat16
I32 = mybir.dt.int32
U32 = mybir.dt.uint32
U8 = mybir.dt.uint8
FP8 = mybir.dt.float8_e4m3fn
FP8X4 = mybir.dt.float8_e4m3fn_x4
FP4X4 = mybir.dt.float4_e2m1fn_x4
ACT = mybir.ActivationFunctionType
ALU = mybir.AluOpType

P = 128
TILES = B // P
PASS = 512
BANK = 512
REST_PASSES = KR // PASS
MASS_PASSES = F // PASS
QUAD = 2
FIRST_LOG = 128
SLOTS = 16
WIDE_BUFS = 4
MASS_CODE_BUFS = 4
TARGET_BUFS = 5
ALIGN = 256


def tile_c51_shifted_log_loss_s3_kernel(
    tc, x_out, w_out, x_rest_bytes, x_rest_scale, base_words, base_scales, spacing, proj_words, proj_scales, online, target, loss
):
    nc = tc.nc
    with ExitStack() as ctx:
        keep = ctx.enter_context(tc.tile_pool(name="keep", bufs=1))
        work = ctx.enter_context(tc.tile_pool(name="work", bufs=WIDE_BUFS))
        psum = ctx.enter_context(tc.psum_pool(name="psum", bufs=1))

        def kept(shape, dtype, name):
            return keep.tile(shape, dtype, name=name, tag=name, align_bytes=ALIGN)

        def kept_each(n, shape, dtype, name):
            tile = kept([shape[0], n] + shape[1:], dtype, name)
            return [tile[:, i] for i in range(n)]

        x_bytes = kept_each(TILES, [P, KR], U8, "x_bytes")
        k_scale = kept([P, REST_PASSES, 8], F32, "k_scale")
        base = kept_each(2, [P, 2, 2 * F], U8, "base")
        base_sc = kept([P, REST_PASSES, F], U8, "base_sc")
        proj = kept([P, MASS_PASSES, 2 * J], U8, "proj")
        proj_sc = kept([P, MASS_PASSES, J], U8, "proj_sc")
        w_rows = kept([P, 4, F], BF16, "w_rows")
        w_codes = kept([P, F], U32, "w_codes")
        w_sc = kept([P, F], U8, "w_sc")
        xo = kept_each(TILES // QUAD, [P, QUAD, KO], BF16, "xo")
        onl = kept_each(TILES, [P, J], BF16, "onl")
        logs = kept_each(TILES, [P, J], F32, "logs")
        spacing_rows = kept([P, F], BF16, "spacing_rows")
        spacing_sorted = kept([P, F], BF16, "spacing_sorted")
        ident = kept([P, P], F32, "ident")
        zeros = kept([P, 2 * P], F32, "zeros")
        row_loss = kept([P, TILES], F32, "row_loss")
        half_loss = kept([P, 2, TILES], F32, "half_loss")
        x_codes = kept_each(TILES, [P, REST_PASSES, P], U32, "x_codes")
        x_sc = kept_each(TILES, [P, REST_PASSES, P], U8, "x_sc")
        xo_codes = kept_each(TILES // QUAD, [P, QUAD, P], U32, "xo_codes")
        xo_sc = kept_each(TILES // QUAD, [P, QUAD, P], U8, "xo_sc")

        x_hbm = x_rest_bytes.rearrange("(r i) k -> r i k", i=TILES)
        xo_hbm = x_out.rearrange("(r i) k -> r i k", i=TILES)
        online_hbm = online.rearrange("(r i) j -> r i j", i=TILES)
        target_hbm = target.rearrange("(r i) j -> r i j", i=TILES)

        wide, is_sorted, groups, exps, mass, mass_codes, mass_sc, target_sb = {}, {}, {}, {}, {}, {}, {}, {}

        free_banks = list(range(8))
        bank_of, banks = {}, {}

        def take_bank(key, shape):
            n = free_banks[0]
            free_banks.remove(n)
            bank_of[key] = n
            banks[key] = psum.tile(shape, F32, name="bank%d" % n, tag="bank%d" % n, bufs=1)
            return banks[key]

        def give_back(key):
            free_banks.append(bank_of[key])
            return banks[key]

        free_slots = list(range(SLOTS))
        slot_of = {}

        def take_slot(key, width, back=None, dtype=BF16):
            n = slot_of[back] if back else free_slots[0]
            free_slots.remove(n)
            slot_of[key] = n
            groups[key] = keep.tile([P, width], dtype, name="slot%d" % n, tag="slot%d" % n, align_bytes=ALIGN)
            return groups[key]

        def free_slot(key):
            free_slots.append(slot_of[key])
            return groups[key]

        def load_x(i, cols=slice(0, KR)):
            nc.sync.dma_start(out=x_bytes[i][:, cols], in_=x_hbm[:, i, cols])

        def load_k_scale():
            nc.sync.dma_start(out=k_scale[:, :, 0:4], in_=x_rest_scale.rearrange("o (g p t) -> p (o g) t", p=P, t=4))

        def load_spacing():
            nc.sync.dma_start(out=spacing_rows[:], in_=spacing.partition_broadcast(P))

        def load_proj():
            nc.sync.dma_start(out=proj[:], in_=proj_words.rearrange("g p n -> p g n"))

        def load_online(i, cols=slice(0, J)):
            nc.sync.dma_start(out=onl[i][:, cols], in_=online_hbm[:, i, cols])

        def load_xo(a):
            nc.sync.dma_start(out=xo[a][:], in_=xo_hbm[:, QUAD * a : QUAD * (a + 1), :])

        def load_base(b):
            nc.sync.dma_start(out=base[b][:], in_=base_words.rearrange("g p n -> p g n")[:, 2 * b : 2 * b + 2, :])

        def load_w(cols=slice(0, F)):
            nc.sync.dma_start(out=w_rows[:, :, cols], in_=w_out.rearrange("(p t) n -> p t n", t=4)[:, :, cols])

        def load_scale_bytes(tile, rows):
            for j in range(4):
                nc.sync.dma_start(
                    out=tile[j:P:32].bitcast(I32),
                    in_=rows[:, j:16:4, :].rearrange("g q n -> q g n").bitcast(I32),
                )

        def log(i, cols=slice(0, J)):
            nc.scalar.activation(out=logs[i][:, cols], in_=onl[i][:, cols], func=ACT.Ln)

        def widen(i, b, engine, back=None, plain=False):
            half = take_slot(("wide", i, b), 2 * PASS, back)
            codes = x_bytes[i][:, 2 * PASS * b : 2 * PASS * (b + 1)].bitcast(FP8)
            is_sorted[i, b] = engine != "gpsimd" and not plain
            if engine == "vector":
                nc.vector.tensor_copy(
                    out=half[:].rearrange("r (u gp e) -> r gp u e", u=2, e=2), in_=codes.rearrange("r (gp u e) -> r gp u e", u=2, e=2)
                )
            elif plain:
                nc.scalar.copy(out=half[:], in_=codes)
            elif engine == "scalar":
                nc.scalar.copy(
                    out=half[:].rearrange("r (u gp e) -> r u gp e", u=2, e=2), in_=codes.rearrange("r (gp u e) -> r u gp e", u=2, e=2)
                )
            else:
                nc.gpsimd.tensor_copy(out=half[:], in_=codes)

        def turn_x(i, b):
            bank = take_bank(("x", i, b), [P, 2, 2, P])
            pairs = free_slot(("wide", i, b))[:].bitcast(F32)
            for gg in range(2):
                for u in range(2):
                    first = P * (2 * u + gg)
                    src = pairs[:, first : first + P] if is_sorted[i, b] else pairs[:, 2 * P * gg + u : 2 * P * (gg + 1) : 2]
                    nc.tensor.transpose(bank[:, u, gg, :], src, ident[:])

        def scale_x(i, b):
            if i == 0:
                half = take_slot(("x", i, b), 2 * PASS)[:]
            else:
                if b == 0:
                    take_slot(("x", i), 4 * PASS)
                half = groups["x", i][:, 2 * PASS * b : 2 * PASS * (b + 1)]
            nc.vector.tensor_tensor(
                out=half.rearrange("p (c r u e) -> p c r u e", c=2, u=2, e=2),
                in0=give_back(("x", i, b))[:].bitcast(BF16).rearrange("p u c (r e) -> p c r u e", e=2),
                in1=k_scale[:, 2 * b : 2 * b + 2, 0:4].rearrange("p c (u e) -> p c u e", e=2).unsqueeze(2).to_broadcast([P, 2, P, 2, 2]),
                op=ALU.mult,
            )

        def leave_bank(key, into, n, parts, copy=nc.scalar.copy):
            if n == 0:
                take_slot(into, parts * 2 * PASS)
            copy(
                out=groups[into][:, 2 * PASS * n : 2 * PASS * (n + 1)].bitcast(F32).rearrange("p (c r u) -> p c r u", c=2, u=2),
                in_=give_back(key)[:].rearrange("p u c r -> p c r u"),
            )

        def quantise_x(i, b=None):
            passes = slice(0, REST_PASSES) if b is None else slice(2 * b, 2 * b + 2)
            nc.vector.quantize_mx(
                out=x_codes[i][:, passes].rearrange("p g r -> p (g r)").bitcast(FP8X4),
                scales=x_sc[i][:, passes].rearrange("p g r -> p (g r)"),
                in_=free_slot(("x", i) if b is None else ("x", i, b))[:],
            )

        def sort_xo(a):
            nc.vector.tensor_copy(
                out=take_slot(("xo_sorted", a), 2 * PASS)[:].bitcast(F32).rearrange("r (u cp) -> r u cp", u=2),
                in_=xo[a][:].rearrange("r c k -> r (c k)").bitcast(F32).rearrange("r (cp u) -> r u cp", u=2),
            )

        def turn_xo(a):
            bank = take_bank(("xo", a), [P, 2, 2, P])
            for c in range(2):
                pairs = xo[a][:, c, :].bitcast(F32)
                for u in range(2):
                    if ("xo_sorted", a) in groups:
                        first = P * (2 * u + c)
                        src = groups["xo_sorted", a][:].bitcast(F32)[:, first : first + P]
                    else:
                        src = pairs[:, u::2]
                    nc.tensor.transpose(bank[:, u, c, :], src, ident[:])
            if ("xo_sorted", a) in groups:
                free_slot(("xo_sorted", a))

        def leave_xo(a, copy=nc.scalar.copy):
            leave_bank(("xo", a), ("xo", a), 0, 1, copy)

        def quantise_xo(a):
            nc.vector.quantize_mx(
                out=xo_codes[a][:].rearrange("p i r -> p (i r)").bitcast(FP8X4),
                scales=xo_sc[a][:].rearrange("p i r -> p (i r)"),
                in_=free_slot(("xo", a))[:],
            )

        def group_w(engine, c0, c1, back=None):
            piece = take_slot(("w", c0), 4 * (c1 - c0), back)
            if engine == "gpsimd":
                nc.gpsimd.tensor_scalar(
                    out=piece[:].rearrange("p (n t) -> p n t", t=4),
                    in0=w_rows[:, :, c0:c1].rearrange("p t n -> p n t"),
                    scalar1=1.0,
                    scalar2=0.0,
                    op0=ALU.mult,
                    op1=ALU.add,
                )
            else:
                copy = nc.scalar.copy if engine == "scalar" else nc.vector.tensor_copy
                copy(
                    out=piece[:].rearrange("p (c i t) -> p c t i", i=4, t=4),
                    in_=w_rows[:, :, c0:c1].rearrange("p t (c i) -> p c t i", i=4),
                )

        def quantise_w(c0, c1):
            nc.vector.quantize_mx(out=w_codes[:, c0:c1].bitcast(FP8X4), scales=w_sc[:, c0:c1], in_=free_slot(("w", c0))[:])

        def rest_pass(i, h, g):
            if g == 0:
                take_bank(("logits", i, h), [P, BANK])
            nc.tensor.matmul_mx(
                out=banks["logits", i, h][:],
                lhsT=x_codes[i][:, g, :].bitcast(FP8X4),
                lhsT_scale=x_sc[i][:, g, :],
                rhs=base[g // 2][:, g % 2, 2 * BANK * h : 2 * BANK * (h + 1)].bitcast(FP4X4),
                rhs_scale=base_sc[:, g, BANK * h : BANK * (h + 1)],
                start=(g == 0),
                stop=False,
            )

        def rest_passes(i, h):
            for g in range(REST_PASSES):
                rest_pass(i, h, g)

        def out_pass(i, h):
            nc.tensor.matmul_mx(
                out=banks["logits", i, h][:],
                lhsT=xo_codes[i // QUAD][:, i % QUAD, :].bitcast(FP8X4),
                lhsT_scale=xo_sc[i // QUAD][:, i % QUAD, :],
                rhs=w_codes[:, BANK * h : BANK * (h + 1)].bitcast(FP8X4),
                rhs_scale=w_sc[:, BANK * h : BANK * (h + 1)],
                start=False,
                stop=True,
            )

        def logits(i, h):
            rest_passes(i, h)
            out_pass(i, h)

        def exp(i, h):
            if h == 0:
                take_slot(("e", i), F, dtype=F32)
            nc.scalar.activation(
                out=groups["e", i][:, PASS * h : PASS * (h + 1)].rearrange("r (u p e) -> r u p e", u=2, e=2),
                in_=give_back(("logits", i, h))[:].rearrange("r (p u e) -> r u p e", u=2, e=2),
                func=ACT.Exp,
            )

        def sort_spacing():
            nc.vector.tensor_copy(
                out=spacing_sorted[:].bitcast(F32).rearrange("r (g u p) -> r g u p", g=MASS_PASSES, u=2),
                in_=spacing_rows[:].bitcast(F32).rearrange("r (g p u) -> r g u p", g=MASS_PASSES, u=2),
            )

        def weigh(i, engine, g0=0, g1=MASS_PASSES, back=None):
            cols = slice(PASS * g0, PASS * g1)
            piece = take_slot(("m", i, g0), PASS * (g1 - g0), back)
            for g in range(g0, g1):
                mass[i, g] = piece[:, PASS * (g - g0) : PASS * (g - g0 + 1)]
            source = free_slot(("e", i)) if g1 == MASS_PASSES else groups["e", i]
            (nc.gpsimd if engine == "gpsimd" else nc.vector).tensor_tensor(out=piece[:], in0=source[:, cols], in1=spacing_sorted[:, cols], op=ALU.mult)

        def mass_pairs(i, g, u):
            return mass[i, g].bitcast(F32)[:, P * u : P * (u + 1)]

        def free_mass(i, g):
            if ("m", i, g) in slot_of:
                free_slot(("m", i, g))

        def turn_mass(i):
            bank = take_bank(("mass", i), [P, 2, MASS_PASSES, P])
            for g in range(MASS_PASSES):
                for u in range(2):
                    nc.tensor.transpose(bank[:, u, g, :], mass_pairs(i, g, u), ident[:])
            for g in range(MASS_PASSES):
                free_mass(i, g)

        def leave_mass(tiles, copy=nc.scalar.copy):
            for n, i in enumerate(tiles):
                leave_bank(("mass", i), ("mass", tiles), n, len(tiles), copy)

        def quantise_mass(tiles):
            codes = work.tile([P, len(tiles), MASS_PASSES, P], U32, name="mass_codes", tag="mass_codes", bufs=MASS_CODE_BUFS, align_bytes=ALIGN)
            scales = work.tile([P, len(tiles), MASS_PASSES, P], U8, name="mass_sc", tag="mass_sc", bufs=MASS_CODE_BUFS, align_bytes=ALIGN)
            for n, i in enumerate(tiles):
                mass_codes[i], mass_sc[i] = codes[:, n], scales[:, n]
            nc.vector.quantize_mx(
                out=codes[:].rearrange("p i g r -> p (i g r)").bitcast(FP8X4),
                scales=scales[:].rearrange("p i g r -> p (i g r)"),
                in_=free_slot(("mass", tiles))[:],
            )

        def turn_mass_pass(i, g):
            bank = take_bank(("mass", i, g), [P, 2, P])
            for u in range(2):
                nc.tensor.transpose(bank[:, u, :], mass_pairs(i, g, u), ident[:])
            free_mass(i, g)

        def leave_mass_pass(i, g):
            nc.scalar.copy(
                out=take_slot(("mass", i, g), PASS)[:].bitcast(F32).rearrange("p (r u) -> p r u", u=2),
                in_=give_back(("mass", i, g))[:].rearrange("p u r -> p r u"),
            )

        def quantise_mass_pass(i, g):
            if g == 0:
                codes = work.tile([P, MASS_PASSES, P], U32, name="mass_codes", tag="mass_codes", bufs=MASS_CODE_BUFS, align_bytes=ALIGN)
                scales = work.tile([P, MASS_PASSES, P], U8, name="mass_sc", tag="mass_sc", bufs=MASS_CODE_BUFS, align_bytes=ALIGN)
                mass_codes[i], mass_sc[i] = codes[:], scales[:]
            nc.vector.quantize_mx(out=mass_codes[i][:, g].bitcast(FP8X4), scales=mass_sc[i][:, g], in_=free_slot(("mass", i, g))[:])

        def project_pass(i, h, g):
            if g == 0:
                take_bank(("target", i, h), [P, BANK])
            nc.tensor.matmul_mx(
                out=banks["target", i, h][:],
                lhsT=mass_codes[i][:, g, :].bitcast(FP8X4),
                lhsT_scale=mass_sc[i][:, g, :],
                rhs=proj[:, g, 2 * BANK * h : 2 * BANK * (h + 1)].bitcast(FP4X4),
                rhs_scale=proj_sc[:, g, BANK * h : BANK * (h + 1)],
                start=(g == 0),
                stop=(g == MASS_PASSES - 1),
            )

        def project(i):
            for h in range(2):
                for g in range(MASS_PASSES):
                    project_pass(i, h, g)

        def store_half(i, h, last_reader=True):
            if i not in target_sb:
                target_sb[i] = work.tile([P, J], F32, name="target_sb", tag="target_sb", bufs=TARGET_BUFS, align_bytes=ALIGN)
            cols = slice(BANK * h, BANK * (h + 1))
            bank = give_back(("target", i, h)) if last_reader else banks["target", i, h]
            nc.scalar.copy(out=target_sb[i][:, cols], in_=bank[:])
            nc.sync.dma_start(out=target_hbm[:, i, cols], in_=target_sb[i][:, cols])

        def store_target(i, last_reader=True):
            for h in range(2):
                store_half(i, h, last_reader)

        def reduce_half(i, h, source):
            cols = slice(BANK * h, BANK * (h + 1))
            products = work.tile([P, BANK], F32, name="products", tag="products", bufs=2, align_bytes=ALIGN)
            nc.vector.scalar_tensor_tensor(
                out=products[:],
                in0=target_sb[i][:, cols] if source == "sbuf" else (give_back(("target", i, h)) if source == "psum_last" else banks["target", i, h])[:],
                scalar=-1.0 / J,
                in1=logs[i][:, cols],
                op0=ALU.mult,
                op1=ALU.mult,
                accum_out=half_loss[:, h, i : i + 1],
            )

        def warm_up(n):
            take_bank(("warm", n), [P, 2 * P])
            nc.tensor.matmul(give_back(("warm", n))[:], lhsT=zeros[:, 0:P], rhs=zeros[:], start=True, stop=True)

        def both(step, *args):
            for h in range(2):
                step(args[0], h, *args[1:])

        with tc.manual_schedule():
            nc.vector.memset(zeros[:], 0.0)
            nc.vector.memset(base_sc[:].rearrange("p g n -> p (g n)").bitcast(I32), 0)
            nc.vector.memset(proj_sc[:].rearrange("p g n -> p (g n)").bitcast(I32), 0)
            make_identity(nc, ident[:])
            load_x(0)
            load_k_scale()
            load_online(0)
            for i in range(1, 4):
                load_x(i)
            load_scale_bytes(base_sc, base_scales)
            load_base(0)
            load_online(1)
            load_x(4)
            load_base(1)
            load_w(slice(0, BANK))
            load_online(2)
            load_online(3)
            load_xo(0)
            load_xo(1)
            load_online(4)
            load_online(5)
            load_w(slice(BANK, F))
            load_online(6)
            load_online(7)
            load_x(5)
            load_spacing()
            load_xo(2)
            load_x(6)
            load_proj()
            load_scale_bytes(proj_sc, proj_scales)
            load_x(7)
            load_xo(3)
            log(0)
            both(widen, 0, "vector")
            widen(1, 0, "gpsimd")
            widen(1, 1, "scalar")
            widen(2, 0, "gpsimd")
            widen(2, 1, "scalar")
            widen(3, 1, "scalar")
            warm_up(0)
            warm_up(1)
            both(turn_x, 0)
            warm_up(2)
            turn_x(1, 0)
            warm_up(3)
            turn_x(1, 1)
            both(scale_x, 0)
            both(turn_x, 2)
            quantise_x(0, 0)
            widen(3, 0, "gpsimd", ("x", 0, 0))
            log(1)
            both(widen, 4, "scalar")
            log(2)
            log(3)
            for g in range(2):
                both(rest_pass, 0, g)
            both(scale_x, 1)
            both(turn_x, 3)
            quantise_x(0, 1)
            quantise_x(1)
            for g in range(2, REST_PASSES):
                both(rest_pass, 0, g)
            group_w("gpsimd", 0, 384)
            both(rest_passes, 1)
            both(scale_x, 2)
            turn_xo(0)
            turn_xo(1)
            scale_x(3, 0)
            leave_xo(0)
            leave_xo(1)
            quantise_x(2)
            group_w("gpsimd", 384, BANK, ("x", 2))
            rest_passes(2, 0)
            scale_x(3, 1)
            both(turn_x, 4)
            rest_passes(2, 1)
            for i in range(4, TILES):
                log(i)
            quantise_w(0, 384)
            quantise_x(3)
            quantise_w(384, BANK)
            group_w("vector", 896, F)
            quantise_xo(0)
            group_w("gpsimd", BANK, 896, ("xo", 0))
            quantise_xo(1)
            both(scale_x, 4)
            quantise_w(896, F)
            quantise_w(BANK, 896)
            for i in range(3):
                out_pass(i, 0)
            logits(3, 0)
            rest_passes(3, 1)
            for i in range(4):
                out_pass(i, 1)
            quantise_x(4)
            sort_spacing()
            both(widen, 5, "vector")
            both(exp, 0)
            turn_xo(2)
            both(exp, 1)
            both(turn_x, 5)
            exp(2, 0)
            weigh(0, "vector")
            weigh(1, "gpsimd")
            rest_passes(4, 0)
            leave_xo(2)
            exp(2, 1)
            turn_mass(0)
            both(scale_x, 5)
            exp(3, 0)
            leave_mass((0,))
            rest_passes(4, 1)
            exp(3, 1)
            widen(6, 0, "scalar")
            quantise_xo(2)
            both(out_pass, 4)
            quantise_mass((0,))
            quantise_x(5)
            widen(6, 1, "vector")
            weigh(2, "gpsimd", back=("x", 5))
            weigh(3, "gpsimd", 0, 1)
            project(0)
            both(exp, 4)
            turn_mass(1)
            both(turn_x, 6)
            both(reduce_half, 0, "psum")
            leave_mass((1,))
            store_target(0)
            both(scale_x, 6)
            both(logits, 5)
            both(widen, 7, "scalar")
            quantise_mass((1,))
            quantise_x(6)
            sort_xo(3)
            weigh(3, "gpsimd", 1, 2, ("x", 6))
            weigh(4, "gpsimd")
            project(1)
            both(exp, 5)
            both(turn_x, 7)
            turn_xo(3)
            turn_mass(2)
            both(reduce_half, 1, "psum")
            store_half(1, 0)
            leave_xo(3)
            leave_mass((2,))
            store_half(1, 1)
            both(scale_x, 7)
            both(rest_passes, 6)
            quantise_xo(3)
            quantise_mass((2,))
            quantise_x(7)
            weigh(5, "vector")
            both(out_pass, 6)
            project(2)
            both(exp, 6)
            weigh(6, "gpsimd", 0, 1, ("x", 7))
            turn_mass(3)
            turn_mass(4)
            turn_mass(5)
            both(reduce_half, 2, "psum")
            leave_mass((3,))
            leave_mass((4, 5))
            logits(7, 0)
            quantise_mass((3,))
            store_target(2)
            quantise_mass((4, 5))
            weigh(6, "gpsimd", 1, 2, ("mass", (4, 5)))
            project(3)
            exp(7, 0)
            project(4)
            both(reduce_half, 3, "psum")
            store_target(3)
            logits(7, 1)
            both(reduce_half, 4, "psum")
            store_half(4, 0)
            exp(7, 1)
            weigh(7, "vector", 0, 1)
            turn_mass(6)
            turn_mass_pass(7, 0)
            weigh(7, "vector", 1, 2)
            leave_mass((6,))
            leave_mass_pass(7, 0)
            project(5)
            turn_mass_pass(7, 1)
            store_half(5, 0, False)
            leave_mass_pass(7, 1)
            store_half(4, 1)
            quantise_mass((6,))
            reduce_half(5, 1, "psum")
            quantise_mass_pass(7, 0)
            project(6)
            reduce_half(5, 0, "psum_last")
            quantise_mass_pass(7, 1)
            for g in range(MASS_PASSES):
                both(project_pass, 7, g)
            store_half(6, 0, False)
            store_half(5, 1)
            reduce_half(6, 1, "psum")
            reduce_half(6, 0, "psum_last")
            store_half(7, 0, False)
            store_half(6, 1)
            reduce_half(7, 1, "psum")
            reduce_half(7, 0, "psum_last")
            store_half(7, 1)
            nc.vector.tensor_tensor(out=row_loss[:], in0=half_loss[:, 0], in1=half_loss[:, 1], op=ALU.add)
            nc.sync.dma_start(out=loss.rearrange("(r i) -> r i", i=TILES), in_=row_loss[:])
